import numpy as np
import ml_dtypes


def mxq(x, axis, fmt="e4m3"):
    dtype, down = {"e4m3": (ml_dtypes.float8_e4m3fn, 7), "e5m2": (ml_dtypes.float8_e5m2, 14)}[fmt]
    v = np.moveaxis(np.asarray(x, np.float32).astype(ml_dtypes.bfloat16).astype(np.float64), axis, -1)
    blocks = v.reshape(v.shape[:-1] + (-1, 32))
    amax = np.abs(blocks).max(-1, keepdims=True)
    byte = np.maximum(np.where(amax > 0, np.frexp(amax)[1] - 1 + 127, 0) - down, 1)
    scale = np.exp2(byte - 127.0)
    codes = (blocks / scale).astype(np.float32).astype(dtype).astype(np.float64)
    return np.moveaxis((codes * scale).reshape(v.shape), -1, axis)


WIDE = False


def mx_kscale(k):
    if not WIDE:
        return np.ones(k)
    levels = np.array([10, -10, 5, -5, 0])
    if k % 512:
        return np.exp2(np.random.permutation(np.resize(levels, k // 32))).repeat(32)
    a = np.empty((k // 512, 16))
    for p in range(k // 512):
        a[p, :8] = np.random.permutation(np.resize(levels, 8))
        for g in range(8):
            far = levels[np.abs(levels - a[p, g]) >= 10]
            a[p, g + 8] = far[np.random.randint(len(far))]
    return np.exp2(a.ravel()).repeat(32)


BF16 = ml_dtypes.bfloat16


def bf(x):
    return np.asarray(x, np.float32).astype(BF16)


def f64(x):
    return np.asarray(x).astype(np.float64)

E4M3FN = np.array([(-1.0 if i & 128 else 1.0) * ((1.0 + (i & 7) / 8.0) * 2.0 ** (((i >> 3) & 15) - 7) if i & 120 else (i & 7) * 2.0 ** -9) for i in range(256)])


def e4m3fn_bytes(y):
    return np.clip(np.asarray(y, np.float64), -448.0, 448.0).astype(np.float32).astype(ml_dtypes.float8_e4m3fn).view(np.uint8)


def e4m3fn_values(b):
    return E4M3FN[b]


T, K, N, P, B = 2048, 2048, 1024, 128, 128
TOP = 448.0


def setup_inputs():
    s = mx_kscale(K)
    mu = 0.7 * np.random.standard_normal((P, K))
    x = (np.repeat(mu, T // P, axis=0) + np.random.standard_normal((T, K))) * s
    w = np.random.standard_normal((K, N)) / np.sqrt(K) / s[:, None]
    x_scale = (np.abs(x).reshape(T, K // B, B).max(axis=2) / TOP).astype(np.float32)
    w_scale = (np.abs(w).reshape(K // B, B, N // B, B).max(axis=(1, 3)) / TOP).astype(np.float32)
    return {"x_bytes": e4m3fn_bytes(x / np.repeat(f64(x_scale), B, axis=1)),
            "x_scale": x_scale,
            "w_bytes": e4m3fn_bytes(w / np.repeat(np.repeat(f64(w_scale), B, axis=0), B, axis=1)),
            "w_scale": w_scale,
            "means": bf(mu * s),
            "gain": bf(1 + 0.1 * np.random.standard_normal(N))}


def reference(x_bytes, x_scale, w_bytes, w_scale, means, gain):
    x = e4m3fn_values(x_bytes) * np.repeat(f64(x_scale), B, axis=1)
    w = e4m3fn_values(w_bytes) * np.repeat(np.repeat(f64(w_scale), B, axis=0), B, axis=1)
    wq = mxq(w, 0, "e4m3")
    raw = mxq(x, 1, "e4m3") @ wq
    centre = mxq(f64(means), 1, "e4m3") @ wq
    scores = raw.reshape(P, T // P, N) - centre[:, None, :]
    return (scores * f64(gain)).reshape(T, N)

@@ -1,0 +1,273 @@
+from contextlib import ExitStack
+
+import concourse.mybir as mybir
+from concourse.masks import make_identity
+
+T, K, N, PLATES = 2048, 2048, 1024, 128
+FLOPS = 2 * T * K * N + 2 * PLATES * K * N
+
+F32 = mybir.dt.float32
+BF16 = mybir.dt.bfloat16
+U32 = mybir.dt.uint32
+U8 = mybir.dt.uint8
+F8 = mybir.dt.float8_e4m3fn
+X4 = mybir.dt.float8_e4m3fn_x4
+ALU = mybir.AluOpType
+COPY = mybir.ActivationFunctionType.Copy
+
+P = 128
+R = T // PLATES
+G = K // 512
+C = K // 128
+H = 2
+NH = N // H
+
+VB = [12, 10, 6, 4, 8, 8, 6, 5, 5, 3, 1, 2, 4, 4, 7, 2]
+WV = [1, 0, 0, 0, 0, 1, 0, 0]
+EX = ["S"] * 34
+GA = ["V"] * 32
+LAG = 4
+AHEAD = 2
+HEADX = 2
+
+
+def tile_plate_centred_gene_scores_d2_kernel(tc, x_bytes, x_scale, w_bytes, w_scale, means, gain, out):
+    nc = tc.nc
+    with ExitStack() as ctx:
+        keep = ctx.enter_context(tc.tile_pool(name="keep", bufs=1))
+        work = ctx.enter_context(tc.tile_pool(name="work", bufs=3))
+        outs = ctx.enter_context(tc.tile_pool(name="outs", bufs=6))
+        turn = ctx.enter_context(tc.psum_pool(name="turn", bufs=4))
+        accs = ctx.enter_context(tc.psum_pool(name="accs", bufs=4))
+
+        ident = keep.tile([P, P], F32, name="ident")
+        make_identity(nc, ident[:])
+
+        x_rows = x_bytes.rearrange("(p r) k -> p r k", r=R)
+        out_rows = out.rearrange("(p r) n -> p r n", r=R)
+
+        xs = keep.tile([P, R, C], F32, name="xs")
+        wsb = keep.tile([P, G * 4 * 8], F32, name="wsb")
+        ws = keep.tile([P, G, 8], F32, name="ws")
+        gain_b = keep.tile([P, N], BF16, name="gain_b")
+        mw = keep.tile([P, K], BF16, name="mw")
+        cen = keep.tile([P, N], F32, name="cen")
+
+        w_raw = {}
+        for h in range(H):
+            for g in range(G):
+                w_raw[h, g] = keep.tile([P, 4, NH], U8, name="wb%d%d" % (h, g))
+        x_raw = [keep.tile([P, K], U8, name="xb%d" % r) for r in range(2)]
+        x_raw2 = [keep.tile([P, 2, K], U8, name="xp%d" % i) for i in range(1, R // 2)]
+
+        def load_w(h, g):
+            nc.sync.dma_start(
+                out=w_raw[h, g][:],
+                in_=w_bytes[512 * g : 512 * g + 512, NH * h : NH * h + NH].rearrange("(p t) n -> p t n", t=4),
+            )
+
+        def xb(r):
+            if r < 2:
+                return x_raw[r][:]
+            return x_raw2[r // 2 - 1][:, r % 2, :]
+
+        nc.sync.dma_start(out=wsb[:], in_=w_scale.rearrange("c d -> (c d)").partition_broadcast(P))
+        load_w(0, 0)
+        nc.sync.dma_start(out=xs[:], in_=x_scale.rearrange("(p r) c -> p r c", r=R))
+        nc.sync.dma_start(out=x_raw[0][:], in_=x_rows[:, 0, :])
+        load_w(0, 1)
+        nc.sync.dma_start(out=mw[:], in_=means)
+        load_w(0, 2)
+        load_w(0, 3)
+        nc.sync.dma_start(out=x_raw[1][:], in_=x_rows[:, 1, :])
+        nc.sync.dma_start(out=x_raw2[0][:], in_=x_rows[:, 2:4, :])
+        load_w(1, 0)
+        load_w(1, 1)
+        nc.sync.dma_start(out=gain_b[:], in_=gain.partition_broadcast(P))
+        nc.sync.dma_start(out=x_raw2[1][:], in_=x_rows[:, 4:6, :])
+        load_w(1, 2)
+        load_w(1, 3)
+        for i in range(3, R // 2):
+            nc.sync.dma_start(out=x_raw2[i - 1][:], in_=x_rows[:, 2 * i : 2 * i + 2, :])
+
+        for q in range(4):
+            nc.vector.tensor_copy(
+                out=ws[32 * q : 32 * q + 32, :, :],
+                in_=wsb[32 * q : 32 * q + 32, :].rearrange("p (g q d) -> p g q d", q=4, d=8)[:, :, q, :],
+            )
+
+        w_codes, w_scales, w_wide, w_grp = {}, {}, {}, {}
+
+        def widen_w(h, g):
+            t = work.tile([P, 4 * NH], BF16, name="ww")
+            src = w_raw[h, g][:].rearrange("p t n -> p (t n)").bitcast(F8)
+            if WV[4 * h + g]:
+                nc.vector.tensor_copy(out=t[:], in_=src)
+            else:
+                nc.scalar.copy(out=t[:], in_=src)
+            w_wide[h, g] = t
+
+        def scale_w(h, g):
+            t = work.tile([P, NH * 4], BF16, name="wg", align_bytes=64)
+            src = w_wide[h, g][:].rearrange("p (t n) -> p n t", t=4)
+            dst = t[:].rearrange("p (n t) -> p n t", t=4)
+            for d in range(4):
+                nc.vector.tensor_scalar(
+                    out=dst[:, 128 * d : 128 * d + 128, :],
+                    in0=src[:, 128 * d : 128 * d + 128, :],
+                    scalar1=ws[:, g, 4 * h + d : 4 * h + d + 1],
+                    scalar2=None,
+                    op0=ALU.mult,
+                )
+            w_grp[h, g] = t
+
+        def quant_w(h, g):
+            codes = keep.tile([P, NH], U32, name="wc%d%d" % (h, g), align_bytes=64)
+            scales = keep.tile([P, NH], U8, name="wq%d%d" % (h, g), align_bytes=64)
+            nc.vector.quantize_mx(out=codes[:].bitcast(X4), scales=scales[:], in_=w_grp[h, g][:])
+            w_codes[h, g] = codes
+            w_scales[h, g] = scales
+
+        wide, grp, banks, codes_x, scales_x = {}, {}, {}, {}, {}
+        wide[R] = mw
+
+        def widen_x(r, vblocks):
+            t = work.tile([P, K], BF16, name="xw")
+            src = xb(r)
+            for c in range(C):
+                cols = slice(128 * c, 128 * c + 128)
+                if c < vblocks:
+                    nc.vector.tensor_scalar(
+                        out=t[:, cols], in0=src[:, cols].bitcast(F8), scalar1=xs[:, r, c : c + 1], scalar2=None, op0=ALU.mult
+                    )
+                else:
+                    nc.scalar.activation(out=t[:, cols], in_=src[:, cols].bitcast(F8), func=COPY, scale=xs[:, r, c : c + 1])
+            wide[r] = t
+
+        def turn_x(r):
+            words = wide[r][:].bitcast(F32)
+            for b in range(2):
+                pt = turn.tile([P, 2, 2, P], F32, name="pt")
+                for j in range(2):
+                    for u in range(2):
+                        g = 2 * b + j
+                        nc.tensor.transpose(pt[:, j, u, :], words[:, 256 * g + u : 256 * g + 256 : 2], ident[:])
+                banks[r, b] = pt
+
+        def exit_x(r, b, eng):
+            if b == 0:
+                grp[r] = work.tile([P, G * P * 4], BF16, name="xg", align_bytes=64)
+            dst = grp[r][:, 1024 * b : 1024 * b + 1024].bitcast(F32).rearrange("p (j s u) -> p j s u", j=2, u=2)
+            src = banks[r, b][:].rearrange("p j u s -> p j s u")
+            if eng == "S":
+                nc.scalar.copy(out=dst, in_=src)
+            else:
+                nc.vector.tensor_copy(out=dst, in_=src)
+
+        def quant_x(r):
+            codes = work.tile([P, G * P], U32, name="xc", align_bytes=64, bufs=8)
+            scales = work.tile([P, G * P], U8, name="xq", align_bytes=64, bufs=8)
+            nc.vector.quantize_mx(out=codes[:].bitcast(X4), scales=scales[:], in_=grp[r][:])
+            codes_x[r] = codes
+            scales_x[r] = scales
+
+        acc = {}
+
+        def mm(r, h):
+            t = accs.tile([P, NH], F32, name="acc")
+            for g in range(G):
+                rows = slice(P * g, P * g + P)
+                nc.tensor.matmul_mx(
+                    out=t[:],
+                    lhsT=codes_x[r][:, rows].bitcast(X4),
+                    lhsT_scale=scales_x[r][:, rows],
+                    rhs=w_codes[h, g][:].bitcast(X4),
+                    rhs_scale=w_scales[h, g][:],
+                    start=(g == 0),
+                    stop=(g == G - 1),
+                )
+            acc[r, h] = t
+
+        diffs = {}
+
+        def sub(r, h):
+            t = outs.tile([P, NH], F32, name="diff")
+            cols = slice(NH * h, NH * h + NH)
+            nc.vector.tensor_tensor(out=t[:], in0=acc[r, h][:], in1=cen[:, cols], op=ALU.subtract)
+            diffs[r, h] = t
+
+        def scale_out(r, h, eng):
+            t = outs.tile([P, NH], F32, name="res")
+            cols = slice(NH * h, NH * h + NH)
+            e = nc.vector if eng == "V" else nc.gpsimd
+            e.tensor_tensor(out=t[:], in0=diffs[r, h][:], in1=gain_b[:, cols], op=ALU.mult)
+            nc.sync.dma_start(out=out_rows[:, r, cols], in_=t[:])
+
+        def centre(h):
+            mm(R, h)
+            nc.scalar.copy(out=cen[:, NH * h : NH * h + NH], in_=acc[R, h][:])
+
+        def prep(r, part):
+            if part == 0:
+                if r < R:
+                    widen_x(r, VB[r])
+                turn_x(r)
+            elif part == 1:
+                for b in range(2):
+                    exit_x(r, b, EX[2 * r + b])
+            else:
+                quant_x(r)
+
+        def head():
+            widen_w(0, 0)
+            prep(0, 0)
+            scale_w(0, 0)
+            widen_w(0, 1)
+            prep(0, 1)
+            scale_w(0, 1)
+            quant_w(0, 0)
+            widen_w(0, 2)
+            prep(0, 2)
+            scale_w(0, 2)
+            quant_w(0, 1)
+            widen_w(0, 3)
+            prep(R, 0)
+            prep(R, 1)
+            scale_w(0, 3)
+            quant_w(0, 2)
+            prep(R, 2)
+            quant_w(0, 3)
+            for r in range(1, 1 + HEADX):
+                for part in range(3):
+                    prep(r, part)
+            centre(0)
+
+        def steady():
+            for s in range(R + LAG):
+                if s < R:
+                    mm(s, 0)
+                if s >= LAG:
+                    mm(s - LAG, 1)
+                n = s + HEADX + 1
+                if n < R:
+                    prep(n, 0)
+                    prep(n, 1)
+                if s < R:
+                    sub(s, 0)
+                if s >= LAG:
+                    sub(s - LAG, 1)
+                if n < R:
+                    prep(n, 2)
+                if s < G:
+                    widen_w(1, s)
+                    scale_w(1, s)
+                    quant_w(1, s)
+                if s == G - 1:
+                    centre(1)
+                if s < R:
+                    scale_out(s, 0, GA[2 * s])
+                if s >= LAG:
+                    scale_out(s - LAG, 1, GA[2 * (s - LAG) + 1])
+
+        head()
+        steady()

@@ -19,16 +19,25 @@ P = 128
 R = T // PLATES
 G = K // 512
 C = K // 128
-H = 2
-NH = N // H
+BANK = 512
+MEANS = R
+PARTS = [(0, 512), (512, 256), (768, 256)]
 
-VB = [12, 10, 6, 4, 8, 8, 6, 5, 5, 3, 1, 2, 4, 4, 7, 2]
-WV = [1, 0, 0, 0, 0, 1, 0, 0]
-EX = ["S"] * 34
-GA = ["V"] * 32
-LAG = 4
-AHEAD = 2
-HEADX = 2
+STEP_B = 4
+STEP_C = 8
+V_PASSES = 1
+V_FROM = 99
+V_EXIT_FROM = 99
+D_ON_S = []
+GP_FROM = 99
+GP_TO = 99
+QUOTA = 4
+SPLIT = 4
+B_PER = 2
+C_PER = 2
+B_TAKE = 2
+CEN_S = []
+C_TAKE = 3
 
 
 def tile_plate_centred_gene_scores_d2_kernel(tc, x_bytes, x_scale, w_bytes, w_scale, means, gain, out):
@@ -36,9 +45,10 @@ def tile_plate_centred_gene_scores_d2_kernel(tc, x_bytes, x_scale, w_bytes, w_sc
     with ExitStack() as ctx:
         keep = ctx.enter_context(tc.tile_pool(name="keep", bufs=1))
         work = ctx.enter_context(tc.tile_pool(name="work", bufs=3))
-        outs = ctx.enter_context(tc.tile_pool(name="outs", bufs=6))
-        turn = ctx.enter_context(tc.psum_pool(name="turn", bufs=4))
-        accs = ctx.enter_context(tc.psum_pool(name="accs", bufs=4))
+        outs = ctx.enter_context(tc.tile_pool(name="outs", bufs=4))
+        turn = ctx.enter_context(tc.psum_pool(name="turn", bufs=3))
+        accs = ctx.enter_context(tc.psum_pool(name="accs", bufs=5))
+        ctx.enter_context(tc.manual_schedule())
 
         ident = keep.tile([P, P], F32, name="ident")
         make_identity(nc, ident[:])
@@ -47,227 +57,307 @@ def tile_plate_centred_gene_scores_d2_kernel(tc, x_bytes, x_scale, w_bytes, w_sc
         out_rows = out.rearrange("(p r) n -> p r n", r=R)
 
         xs = keep.tile([P, R, C], F32, name="xs")
-        wsb = keep.tile([P, G * 4 * 8], F32, name="wsb")
+        wsb = keep.tile([P, C * 8], F32, name="wsb")
         ws = keep.tile([P, G, 8], F32, name="ws")
         gain_b = keep.tile([P, N], BF16, name="gain_b")
         mw = keep.tile([P, K], BF16, name="mw")
         cen = keep.tile([P, N], F32, name="cen")
 
-        w_raw = {}
-        for h in range(H):
-            for g in range(G):
-                w_raw[h, g] = keep.tile([P, 4, NH], U8, name="wb%d%d" % (h, g))
-        x_raw = [keep.tile([P, K], U8, name="xb%d" % r) for r in range(2)]
-        x_raw2 = [keep.tile([P, 2, K], U8, name="xp%d" % i) for i in range(1, R // 2)]
+        w_raw, x_raw = {}, {}
 
-        def load_w(h, g):
+        def load_w(part, g):
+            c0, n = PARTS[part]
+            t = keep.tile([P, 4 * n], U8, name="wb%d%d" % (part, g))
             nc.sync.dma_start(
-                out=w_raw[h, g][:],
-                in_=w_bytes[512 * g : 512 * g + 512, NH * h : NH * h + NH].rearrange("(p t) n -> p t n", t=4),
+                out=t[:].rearrange("p (t n) -> p t n", t=4),
+                in_=w_bytes[512 * g : 512 * g + 512, c0 : c0 + n].rearrange("(p t) n -> p t n", t=4),
             )
+            w_raw[part, g] = t
 
-        def xb(r):
-            if r < 2:
-                return x_raw[r][:]
-            return x_raw2[r // 2 - 1][:, r % 2, :]
+        def load_x(r, rows):
+            t = keep.tile([P, rows * K], U8, name="xb%d" % r)
+            nc.sync.dma_start(out=t[:], in_=x_rows[:, r : r + rows, :].rearrange("p r k -> p (r k)"))
+            for j in range(rows):
+                x_raw[r + j] = t[:, j * K : (j + 1) * K]
 
-        nc.sync.dma_start(out=wsb[:], in_=w_scale.rearrange("c d -> (c d)").partition_broadcast(P))
+        nc.scalar.dma_start(out=xs[:], in_=x_scale.rearrange("(p r) c -> p r c", r=R))
+        nc.scalar.dma_start(out=wsb[:], in_=w_scale.rearrange("c d -> (c d)").partition_broadcast(P))
         load_w(0, 0)
-        nc.sync.dma_start(out=xs[:], in_=x_scale.rearrange("(p r) c -> p r c", r=R))
-        nc.sync.dma_start(out=x_raw[0][:], in_=x_rows[:, 0, :])
+        load_x(0, 1)
         load_w(0, 1)
-        nc.sync.dma_start(out=mw[:], in_=means)
+        load_x(1, 1)
         load_w(0, 2)
+        nc.sync.dma_start(out=mw[:], in_=means)
         load_w(0, 3)
-        nc.sync.dma_start(out=x_raw[1][:], in_=x_rows[:, 1, :])
-        nc.sync.dma_start(out=x_raw2[0][:], in_=x_rows[:, 2:4, :])
-        load_w(1, 0)
-        load_w(1, 1)
+        for g in range(G):
+            load_w(1, g)
+        load_x(2, 2)
         nc.sync.dma_start(out=gain_b[:], in_=gain.partition_broadcast(P))
-        nc.sync.dma_start(out=x_raw2[1][:], in_=x_rows[:, 4:6, :])
-        load_w(1, 2)
-        load_w(1, 3)
-        for i in range(3, R // 2):
-            nc.sync.dma_start(out=x_raw2[i - 1][:], in_=x_rows[:, 2 * i : 2 * i + 2, :])
+        load_x(4, 2)
+        for g in range(G):
+            load_w(2, g)
+        for r in range(6, R, 2):
+            load_x(r, 2)
 
-        for q in range(4):
-            nc.vector.tensor_copy(
-                out=ws[32 * q : 32 * q + 32, :, :],
-                in_=wsb[32 * q : 32 * q + 32, :].rearrange("p (g q d) -> p g q d", q=4, d=8)[:, :, q, :],
-            )
+        def pick_w_scales():
+            for q in range(4):
+                nc.vector.tensor_copy(
+                    out=ws[32 * q : 32 * q + 32, :, :],
+                    in_=wsb[32 * q : 32 * q + 32, :].rearrange("p (g q d) -> p g q d", q=4, d=8)[:, :, q, :],
+                )
 
         w_codes, w_scales, w_wide, w_grp = {}, {}, {}, {}
 
-        def widen_w(h, g):
-            t = work.tile([P, 4 * NH], BF16, name="ww")
-            src = w_raw[h, g][:].rearrange("p t n -> p (t n)").bitcast(F8)
-            if WV[4 * h + g]:
-                nc.vector.tensor_copy(out=t[:], in_=src)
+        def widen_w(part, g):
+            n = PARTS[part][1]
+            t = work.tile([P, 4 * BANK], BF16, name="ww")
+            src = w_raw[part, g][:].bitcast(F8)
+            if (part, g) not in D_ON_S:
+                nc.vector.tensor_copy(out=t[:, : 4 * n], in_=src)
             else:
-                nc.scalar.copy(out=t[:], in_=src)
-            w_wide[h, g] = t
+                nc.scalar.copy(out=t[:, : 4 * n], in_=src)
+            w_wide[part, g] = t
 
-        def scale_w(h, g):
-            t = work.tile([P, NH * 4], BF16, name="wg", align_bytes=64)
-            src = w_wide[h, g][:].rearrange("p (t n) -> p n t", t=4)
-            dst = t[:].rearrange("p (n t) -> p n t", t=4)
-            for d in range(4):
+        def scale_w(part, g):
+            c0, n = PARTS[part]
+            t = work.tile([P, 4 * BANK], BF16, name="wg", align_bytes=64)
+            src = w_wide[part, g][:, : 4 * n].rearrange("p (t c i) -> p c t i", t=4, i=4)
+            dst = t[:, : 4 * n].rearrange("p (c i t) -> p c t i", t=4, i=4)
+            for j in range(n // 128):
+                d = c0 // 128 + j
                 nc.vector.tensor_scalar(
-                    out=dst[:, 128 * d : 128 * d + 128, :],
-                    in0=src[:, 128 * d : 128 * d + 128, :],
-                    scalar1=ws[:, g, 4 * h + d : 4 * h + d + 1],
+                    out=dst[:, 32 * j : 32 * j + 32, :, :],
+                    in0=src[:, 32 * j : 32 * j + 32, :, :],
+                    scalar1=ws[:, g, d : d + 1],
                     scalar2=None,
                     op0=ALU.mult,
                 )
-            w_grp[h, g] = t
+            w_grp[part, g] = t
 
-        def quant_w(h, g):
-            codes = keep.tile([P, NH], U32, name="wc%d%d" % (h, g), align_bytes=64)
-            scales = keep.tile([P, NH], U8, name="wq%d%d" % (h, g), align_bytes=64)
-            nc.vector.quantize_mx(out=codes[:].bitcast(X4), scales=scales[:], in_=w_grp[h, g][:])
-            w_codes[h, g] = codes
-            w_scales[h, g] = scales
+        def quant_w(part, g):
+            n = PARTS[part][1]
+            codes = keep.tile([P, n], U32, name="wc%d%d" % (part, g), align_bytes=64)
+            scales = keep.tile([P, n], U8, name="wq%d%d" % (part, g), align_bytes=64)
+            nc.vector.quantize_mx(out=codes[:].bitcast(X4), scales=scales[:], in_=w_grp[part, g][:, : 4 * n])
+            w_codes[part, g] = codes
+            w_scales[part, g] = scales
 
         wide, grp, banks, codes_x, scales_x = {}, {}, {}, {}, {}
-        wide[R] = mw
 
-        def widen_x(r, vblocks):
-            t = work.tile([P, K], BF16, name="xw")
-            src = xb(r)
-            for c in range(C):
-                cols = slice(128 * c, 128 * c + 128)
-                if c < vblocks:
-                    nc.vector.tensor_scalar(
-                        out=t[:, cols], in0=src[:, cols].bitcast(F8), scalar1=xs[:, r, c : c + 1], scalar2=None, op0=ALU.mult
-                    )
-                else:
-                    nc.scalar.activation(out=t[:, cols], in_=src[:, cols].bitcast(F8), func=COPY, scale=xs[:, r, c : c + 1])
-            wide[r] = t
+        def on_vector(r, g):
+            return V_FROM <= r < R and g >= G - V_PASSES
+
+        def widen_x(r, vector, passes=range(G)):
+            for g in passes:
+                if on_vector(r, g) != vector:
+                    continue
+                t = work.tile([P, 512], BF16, name="xv" if vector else "xw", bufs=4 * V_PASSES if vector else 12)
+                for q in range(4):
+                    c = 4 * g + q
+                    src = x_raw[r][:, 128 * c : 128 * c + 128].bitcast(F8)
+                    if vector:
+                        dst = t[:].rearrange("p (u s e) -> p s u e", u=2, e=2)[:, 32 * q : 32 * q + 32, :, :]
+                        nc.vector.tensor_scalar(
+                            out=dst,
+                            in0=src.rearrange("p (s u e) -> p s u e", u=2, e=2),
+                            scalar1=xs[:, r, c : c + 1],
+                            scalar2=None,
+                            op0=ALU.mult,
+                        )
+                    else:
+                        nc.scalar.activation(out=t[:, 128 * q : 128 * q + 128], in_=src, func=COPY, scale=xs[:, r, c : c + 1])
+                wide[r, g] = t[:]
+
+        for g in range(G):
+            wide[MEANS, g] = mw[:, 512 * g : 512 * g + 512]
 
         def turn_x(r):
-            words = wide[r][:].bitcast(F32)
             for b in range(2):
                 pt = turn.tile([P, 2, 2, P], F32, name="pt")
                 for j in range(2):
+                    g = 2 * b + j
+                    words = wide[r, g].bitcast(F32)
                     for u in range(2):
-                        g = 2 * b + j
-                        nc.tensor.transpose(pt[:, j, u, :], words[:, 256 * g + u : 256 * g + 256 : 2], ident[:])
+                        src = words[:, P * u : P * u + P] if on_vector(r, g) else words[:, u : 2 * P : 2]
+                        nc.tensor.transpose(pt[:, j, u, :], src, ident[:])
                 banks[r, b] = pt
 
-        def exit_x(r, b, eng):
+        def exit_x(r, b):
             if b == 0:
-                grp[r] = work.tile([P, G * P * 4], BF16, name="xg", align_bytes=64)
+                grp[r] = work.tile([P, G * P * 4], BF16, name="xg", tag="xg", bufs=4, align_bytes=64)
             dst = grp[r][:, 1024 * b : 1024 * b + 1024].bitcast(F32).rearrange("p (j s u) -> p j s u", j=2, u=2)
             src = banks[r, b][:].rearrange("p j u s -> p j s u")
-            if eng == "S":
-                nc.scalar.copy(out=dst, in_=src)
-            else:
+            if b == 0 and V_EXIT_FROM <= r < R:
                 nc.vector.tensor_copy(out=dst, in_=src)
+            else:
+                nc.scalar.copy(out=dst, in_=src)
 
         def quant_x(r):
-            codes = work.tile([P, G * P], U32, name="xc", align_bytes=64, bufs=8)
-            scales = work.tile([P, G * P], U8, name="xq", align_bytes=64, bufs=8)
+            codes = keep.tile([P, G * P], U32, name="xc%d" % r, align_bytes=64)
+            scales = keep.tile([P, G * P], U8, name="xq%d" % r, align_bytes=64)
             nc.vector.quantize_mx(out=codes[:].bitcast(X4), scales=scales[:], in_=grp[r][:])
             codes_x[r] = codes
             scales_x[r] = scales
 
-        acc = {}
+        def one_pass(acc, r, part, g):
+            rows = slice(P * g, P * g + P)
+            nc.tensor.matmul_mx(
+                out=acc,
+                lhsT=codes_x[r][:, rows].bitcast(X4),
+                lhsT_scale=scales_x[r][:, rows],
+                rhs=w_codes[part, g][:].bitcast(X4),
+                rhs_scale=w_scales[part, g][:],
+                start=(g == 0),
+                stop=(g == G - 1),
+            )
 
-        def mm(r, h):
-            t = accs.tile([P, NH], F32, name="acc")
-            for g in range(G):
-                rows = slice(P * g, P * g + P)
-                nc.tensor.matmul_mx(
-                    out=t[:],
-                    lhsT=codes_x[r][:, rows].bitcast(X4),
-                    lhsT_scale=scales_x[r][:, rows],
-                    rhs=w_codes[h, g][:].bitcast(X4),
-                    rhs_scale=w_scales[h, g][:],
-                    start=(g == 0),
-                    stop=(g == G - 1),
-                )
-            acc[r, h] = t
+        def multiply(units):
+            t = accs.tile([P, BANK], F32, name="acc")
+            at = 0
+            for r, part in units:
+                n = PARTS[part][1]
+                for g in range(G):
+                    one_pass(t[:, at : at + n], r, part, g)
+                at += n
+            return t
 
-        diffs = {}
+        def columns(tile, units):
+            c0, n = PARTS[units[0][1]]
+            if len(units) == 2 and units[0][1] == units[1][1]:
+                return tile[:, c0 : c0 + n].unsqueeze(1).to_broadcast([P, 2, n])
+            return tile[:, c0 : c0 + n * len(units)].rearrange("p (j n) -> p j n", n=n)
 
-        def sub(r, h):
-            t = outs.tile([P, NH], F32, name="diff")
-            cols = slice(NH * h, NH * h + NH)
-            nc.vector.tensor_tensor(out=t[:], in0=acc[r, h][:], in1=cen[:, cols], op=ALU.subtract)
-            diffs[r, h] = t
+        def shaped(tile, units):
+            n = PARTS[units[0][1]][1]
+            return tile[:, : n * len(units)].rearrange("p (j n) -> p j n", n=n)
 
-        def scale_out(r, h, eng):
-            t = outs.tile([P, NH], F32, name="res")
-            cols = slice(NH * h, NH * h + NH)
-            e = nc.vector if eng == "V" else nc.gpsimd
-            e.tensor_tensor(out=t[:], in0=diffs[r, h][:], in1=gain_b[:, cols], op=ALU.mult)
-            nc.sync.dma_start(out=out_rows[:, r, cols], in_=t[:])
+        def subtract(units, acc):
+            t = outs.tile([P, BANK], F32, name="diff", bufs=16)
+            nc.vector.tensor_tensor(out=shaped(t, units), in0=shaped(acc, units), in1=columns(cen, units), op=ALU.subtract)
+            return t
 
-        def centre(h):
-            mm(R, h)
-            nc.scalar.copy(out=cen[:, NH * h : NH * h + NH], in_=acc[R, h][:])
-
-        def prep(r, part):
-            if part == 0:
-                if r < R:
-                    widen_x(r, VB[r])
-                turn_x(r)
-            elif part == 1:
-                for b in range(2):
-                    exit_x(r, b, EX[2 * r + b])
+        def finish(units, diff, pool):
+            if pool:
+                slot = work.tile([P, G * P * 4], BF16, name="res_p", tag="xg", bufs=4, align_bytes=64)
+                t = slot[:].bitcast(F32)[:, :BANK]
+                engine = nc.gpsimd
             else:
-                quant_x(r)
+                t = diff[:]
+                engine = nc.vector
+            engine.tensor_tensor(out=shaped(t, units), in0=shaped(diff, units), in1=columns(gain_b, units), op=ALU.mult)
+            r0, part0 = units[0]
+            c0, n = PARTS[part0]
+            if len(units) == 2 and units[1] == (r0, part0 + 1):
+                nc.sync.dma_start(out=out_rows[:, r0, c0 : c0 + 2 * n], in_=t)
+            elif len(units) == 2 and units[1] == (r0 + 1, part0):
+                nc.sync.dma_start(out=out_rows[:, r0 : r0 + 2, c0 : c0 + n], in_=shaped(t, units))
+            else:
+                for j, (r, part) in enumerate(units):
+                    c0 = PARTS[part][0]
+                    nc.sync.dma_start(out=out_rows[:, r, c0 : c0 + n], in_=t[:, j * n : (j + 1) * n])
 
-        def head():
-            widen_w(0, 0)
-            prep(0, 0)
-            scale_w(0, 0)
-            widen_w(0, 1)
-            prep(0, 1)
-            scale_w(0, 1)
-            quant_w(0, 0)
-            widen_w(0, 2)
-            prep(0, 2)
-            scale_w(0, 2)
-            quant_w(0, 1)
-            widen_w(0, 3)
-            prep(R, 0)
-            prep(R, 1)
-            scale_w(0, 3)
-            quant_w(0, 2)
-            prep(R, 2)
-            quant_w(0, 3)
-            for r in range(1, 1 + HEADX):
-                for part in range(3):
-                    prep(r, part)
-            centre(0)
+        def centre(part, acc):
+            c0, n = PARTS[part]
+            if part in CEN_S:
+                nc.scalar.copy(out=cen[:, c0 : c0 + n], in_=acc[:, :n])
+            else:
+                nc.vector.tensor_copy(out=cen[:, c0 : c0 + n], in_=acc[:, :n])
 
-        def steady():
-            for s in range(R + LAG):
-                if s < R:
-                    mm(s, 0)
-                if s >= LAG:
-                    mm(s - LAG, 1)
-                n = s + HEADX + 1
-                if n < R:
-                    prep(n, 0)
-                    prep(n, 1)
-                if s < R:
-                    sub(s, 0)
-                if s >= LAG:
-                    sub(s - LAG, 1)
-                if n < R:
-                    prep(n, 2)
-                if s < G:
-                    widen_w(1, s)
-                    scale_w(1, s)
-                    quant_w(1, s)
-                if s == G - 1:
-                    centre(1)
-                if s < R:
-                    scale_out(s, 0, GA[2 * s])
-                if s >= LAG:
-                    scale_out(s - LAG, 1, GA[2 * (s - LAG) + 1])
+        done = {1: 0, 2: 0}
+        plan = []
+        for s in range(R):
+            step = [[(s, 0)]]
+            narrow = []
+            for part, first in ((1, STEP_B), (2, STEP_C)):
+                if s >= first:
+                    take = min(s + 1 - done[part], B_TAKE if part == 1 else C_TAKE)
+                    narrow += [(done[part] + j, part) for j in range(take)]
+                    done[part] += take
+            if len([u for u in narrow if u[1] == 1]) == 1 and len(narrow) > 1:
+                step.append([narrow[0], narrow[-1]])
+                narrow = narrow[1:-1]
+            step += [narrow[j : j + 2] for j in range(0, len(narrow), 2)]
+            plan.append(step)
+        assert done == {1: R, 2: R}
 
-        head()
-        steady()
+        w_jobs = {}
+        for g in range(G):
+            w_jobs.setdefault(STEP_B + 1 - (G - 1 - g) // B_PER, []).append((1, g))
+            w_jobs.setdefault(STEP_C + 1 - (G - 1 - g) // C_PER, []).append((2, g))
+
+        widen_w(0, 0)
+        pick_w_scales()
+        widen_x(0, False)
+        turn_x(0)
+        widen_w(0, 1)
+        scale_w(0, 0)
+        widen_x(1, False, range(2))
+        exit_x(0, 0)
+        exit_x(0, 1)
+        turn_x(MEANS)
+        widen_x(1, False, range(2, G))
+        exit_x(MEANS, 0)
+        exit_x(MEANS, 1)
+        turn_x(1)
+        scale_w(0, 1)
+        quant_w(0, 0)
+        widen_w(0, 2)
+        quant_w(0, 1)
+        quant_x(0)
+        scale_w(0, 2)
+        widen_w(0, 3)
+        quant_w(0, 2)
+        quant_x(MEANS)
+        scale_w(0, 3)
+        widen_x(2, False, range(2))
+        exit_x(1, 0)
+        exit_x(1, 1)
+        widen_x(2, False, range(2, G))
+        quant_x(1)
+        quant_w(0, 3)
+        early = {r: accs.tile([P, BANK], F32, name="acc") for r in (0, MEANS, 1)}
+        for r in early:
+            for g in range(G - 1):
+                one_pass(early[r][:], r, 0, g)
+        turn_x(2)
+        for r in (MEANS, 0, 1):
+            one_pass(early[r][:], r, 0, G - 1)
+        means_acc = (0, early[MEANS])
+        pending = [([(r, 0)], early[r]) for r in (0, 1)]
+        widen_x(3, False, range(SPLIT))
+        exit_x(2, 0)
+        exit_x(2, 1)
+        widen_x(3, False, range(SPLIT, G))
+        waiting = []
+        for s in range(4, R + 3):
+            jobs = w_jobs.get(s, [])
+            if s - 1 < R:
+                turn_x(s - 1)
+            if s - 2 < R:
+                quant_x(s - 2)
+            if means_acc is not None:
+                centre(*means_acc)
+            for job in jobs:
+                widen_w(*job)
+            waiting += [(units, subtract(units, acc)) for units, acc in pending]
+            if s < R:
+                widen_x(s, False, range(SPLIT))
+            if s - 1 < R:
+                exit_x(s - 1, 0)
+                exit_x(s - 1, 1)
+            if s < R:
+                widen_x(s, False, range(SPLIT, G))
+            means_acc = None
+            if s - 2 in (STEP_B, STEP_C):
+                part = 1 if s - 2 == STEP_B else 2
+                means_acc = (part, multiply([(MEANS, part)]))
+            pending = [(units, multiply(units)) for units in plan[s - 2]] if s - 2 < R else []
+            for job in jobs:
+                scale_w(*job)
+            if s + 1 < R:
+                widen_x(s + 1, True)
+            quota = len(waiting) if s >= R else min(len(waiting), max(0, QUOTA - 2 * len(jobs)))
+            for j in range(quota):
+                finish(*waiting.pop(0), False)
+            for job in jobs:
+                quant_w(*job)

@@ -23,16 +23,22 @@ BANK = 512
 MEANS = R
 PARTS = [(0, 512), (512, 256), (768, 256)]
 
-STEP_B = 4
-STEP_C = 8
+STEP_B = 3
+STEP_C = 6
 V_PASSES = 1
-V_FROM = 99
+V_FROM = 10
 V_EXIT_FROM = 99
 D_ON_S = []
-GP_FROM = 99
-GP_TO = 99
-QUOTA = 4
-SPLIT = 4
+GP_FROM = 6
+GP_TO = 16
+QUOTA = 1
+SPLIT = 2
+ACCS = 4
+XG = 4
+GP_N = 2
+C_EARLY = 3
+TAIL_GP = 1
+G_FIRST = 99
 B_PER = 2
 C_PER = 2
 B_TAKE = 2
@@ -46,12 +52,17 @@ def tile_plate_centred_gene_scores_d2_kernel(tc, x_bytes, x_scale, w_bytes, w_sc
         keep = ctx.enter_context(tc.tile_pool(name="keep", bufs=1))
         work = ctx.enter_context(tc.tile_pool(name="work", bufs=3))
         outs = ctx.enter_context(tc.tile_pool(name="outs", bufs=4))
-        turn = ctx.enter_context(tc.psum_pool(name="turn", bufs=3))
-        accs = ctx.enter_context(tc.psum_pool(name="accs", bufs=5))
+        turn = ctx.enter_context(tc.psum_pool(name="turn", bufs=7 - ACCS))
+        accs = ctx.enter_context(tc.psum_pool(name="accs", bufs=ACCS))
+        fixed = ctx.enter_context(tc.psum_pool(name="fixed", bufs=1))
         ctx.enter_context(tc.manual_schedule())
 
         ident = keep.tile([P, P], F32, name="ident")
         make_identity(nc, ident[:])
+        ident_b = keep.tile([P, P], BF16, name="ident_b")
+        make_identity(nc, ident_b[:])
+        gain_p = fixed.tile([P, N], BF16, name="gain_p")
+        grouped = [keep.tile([P, K], BF16, name="xg%d" % j, align_bytes=64) for j in range(XG)]
 
         x_rows = x_bytes.rearrange("(p r) k -> p r k", r=R)
         out_rows = out.rearrange("(p r) n -> p r n", r=R)
@@ -89,10 +100,10 @@ def tile_plate_centred_gene_scores_d2_kernel(tc, x_bytes, x_scale, w_bytes, w_sc
         load_w(0, 2)
         nc.sync.dma_start(out=mw[:], in_=means)
         load_w(0, 3)
+        nc.sync.dma_start(out=gain_b[:], in_=gain.partition_broadcast(P))
         for g in range(G):
             load_w(1, g)
         load_x(2, 2)
-        nc.sync.dma_start(out=gain_b[:], in_=gain.partition_broadcast(P))
         load_x(4, 2)
         for g in range(G):
             load_w(2, g)
@@ -184,7 +195,7 @@ def tile_plate_centred_gene_scores_d2_kernel(tc, x_bytes, x_scale, w_bytes, w_sc
 
         def exit_x(r, b):
             if b == 0:
-                grp[r] = work.tile([P, G * P * 4], BF16, name="xg", tag="xg", bufs=4, align_bytes=64)
+                grp[r] = grouped[len(grp) % XG]
             dst = grp[r][:, 1024 * b : 1024 * b + 1024].bitcast(F32).rearrange("p (j s u) -> p j s u", j=2, u=2)
             src = banks[r, b][:].rearrange("p j u s -> p j s u")
             if b == 0 and V_EXIT_FROM <= r < R:
@@ -236,15 +247,13 @@ def tile_plate_centred_gene_scores_d2_kernel(tc, x_bytes, x_scale, w_bytes, w_sc
             nc.vector.tensor_tensor(out=shaped(t, units), in0=shaped(acc, units), in1=columns(cen, units), op=ALU.subtract)
             return t
 
-        def finish(units, diff, pool):
-            if pool:
-                slot = work.tile([P, G * P * 4], BF16, name="res_p", tag="xg", bufs=4, align_bytes=64)
-                t = slot[:].bitcast(F32)[:, :BANK]
-                engine = nc.gpsimd
-            else:
+        def finish(units, diff, room=None):
+            if room is None:
                 t = diff[:]
-                engine = nc.vector
-            engine.tensor_tensor(out=shaped(t, units), in0=shaped(diff, units), in1=columns(gain_b, units), op=ALU.mult)
+                nc.vector.tensor_tensor(out=shaped(t, units), in0=shaped(diff, units), in1=columns(gain_p, units), op=ALU.mult)
+            else:
+                t = room
+                nc.gpsimd.tensor_tensor(out=shaped(t, units), in0=shaped(diff, units), in1=columns(gain_b, units), op=ALU.mult)
             r0, part0 = units[0]
             c0, n = PARTS[part0]
             if len(units) == 2 and units[1] == (r0, part0 + 1):
@@ -282,8 +291,8 @@ def tile_plate_centred_gene_scores_d2_kernel(tc, x_bytes, x_scale, w_bytes, w_sc
 
         w_jobs = {}
         for g in range(G):
-            w_jobs.setdefault(STEP_B + 1 - (G - 1 - g) // B_PER, []).append((1, g))
-            w_jobs.setdefault(STEP_C + 1 - (G - 1 - g) // C_PER, []).append((2, g))
+            w_jobs.setdefault(STEP_B - (G - 1 - g) // B_PER, []).append((1, g))
+            w_jobs.setdefault(STEP_C - (G - 1 - g) // C_PER, []).append((2, g))
 
         widen_w(0, 0)
         pick_w_scales()
@@ -315,49 +324,71 @@ def tile_plate_centred_gene_scores_d2_kernel(tc, x_bytes, x_scale, w_bytes, w_sc
         widen_x(2, False, range(2, G))
         quant_x(1)
         quant_w(0, 3)
+        for h in range(2):
+            cols = slice(BANK * h, BANK * h + BANK)
+            nc.tensor.matmul(out=gain_p[:, cols], lhsT=ident_b[:], rhs=gain_b[:, cols], start=True, stop=True)
         early = {r: accs.tile([P, BANK], F32, name="acc") for r in (0, MEANS, 1)}
-        for r in early:
+        for r in (0, MEANS):
             for g in range(G - 1):
                 one_pass(early[r][:], r, 0, g)
         turn_x(2)
+        for g in range(G - 1):
+            one_pass(early[1][:], 1, 0, g)
         for r in (MEANS, 0, 1):
             one_pass(early[r][:], r, 0, G - 1)
         means_acc = (0, early[MEANS])
-        pending = [([(r, 0)], early[r]) for r in (0, 1)]
-        widen_x(3, False, range(SPLIT))
-        exit_x(2, 0)
-        exit_x(2, 1)
-        widen_x(3, False, range(SPLIT, G))
+        pending = []
         waiting = []
-        for s in range(4, R + 3):
+        for s in range(2, R + 1):
             jobs = w_jobs.get(s, [])
-            if s - 1 < R:
-                turn_x(s - 1)
-            if s - 2 < R:
-                quant_x(s - 2)
-            if means_acc is not None:
-                centre(*means_acc)
+            if 2 < s < R:
+                turn_x(s)
             for job in jobs:
                 widen_w(*job)
+            if means_acc is not None:
+                centre(*means_acc)
             waiting += [(units, subtract(units, acc)) for units, acc in pending]
-            if s < R:
-                widen_x(s, False, range(SPLIT))
-            if s - 1 < R:
-                exit_x(s - 1, 0)
-                exit_x(s - 1, 1)
-            if s < R:
-                widen_x(s, False, range(SPLIT, G))
             means_acc = None
-            if s - 2 in (STEP_B, STEP_C):
-                part = 1 if s - 2 == STEP_B else 2
+            if s - 1 in (STEP_B, STEP_C):
+                part = 1 if s - 1 == STEP_B else 2
                 means_acc = (part, multiply([(MEANS, part)]))
-            pending = [(units, multiply(units)) for units in plan[s - 2]] if s - 2 < R else []
+            if s == 2:
+                pending = [([(r, 0)], early[r]) for r in (0, 1)]
+            else:
+                pending = [(units, multiply(units)) for units in plan[s - 1]] if s - 1 < R else []
+            if s + 1 < R:
+                widen_x(s + 1, False, range(SPLIT))
+            if s < R:
+                exit_x(s, 0)
+                exit_x(s, 1)
+            if s + 1 < R:
+                widen_x(s + 1, False, range(SPLIT, G))
+            if s < C_EARLY:
+                quant_x(s)
             for job in jobs:
                 scale_w(*job)
-            if s + 1 < R:
-                widen_x(s + 1, True)
-            quota = len(waiting) if s >= R else min(len(waiting), max(0, QUOTA - 2 * len(jobs)))
+            if s == R - 1:
+                quant_x(s)
+            quota = min(len(waiting), max(0, QUOTA - 2 * len(jobs))) if s < R else 0
             for j in range(quota):
-                finish(*waiting.pop(0), False)
+                finish(*waiting.pop(0))
             for job in jobs:
                 quant_w(*job)
+            if s + 2 < R:
+                widen_x(s + 2, True)
+            if C_EARLY <= s < R - 1:
+                quant_x(s)
+            if GP_FROM <= s < GP_TO:
+                for j in range(min(GP_N, len(waiting))):
+                    finish(*waiting.pop(0), grp[min(s, R - 1)][:].bitcast(F32)[:, BANK * j : BANK * j + BANK])
+        for j, (units, diff) in enumerate(waiting):
+            finish(units, diff, diff[:] if j < TAIL_GP else None)
+        last_units, last_acc = pending.pop()
+        diffs = [(units, subtract(units, acc)) for units, acc in pending]
+        halves = []
+        for j, unit in enumerate(last_units):
+            halves.append(([unit], subtract([unit], last_acc[:, 256 * j : 256 * j + 256])))
+            if diffs:
+                finish(*diffs.pop(0))
+        for units, diff in halves:
+            finish(units, diff)

@@ -30,20 +30,20 @@ V_FROM = 10
 V_EXIT_FROM = 99
 D_ON_S = []
 GP_FROM = 6
-GP_TO = 16
-QUOTA = 1
+QUOTA = 2
 SPLIT = 2
 ACCS = 4
 XG = 4
-GP_N = 2
-C_EARLY = 3
-TAIL_GP = 1
-G_FIRST = 99
+GP_N = 1
+PAIRS_FROM = 16
+SPLIT2 = 1
+GP_N2 = 3
+TAIL_GP = [1]
 B_PER = 2
 C_PER = 2
-B_TAKE = 2
+B_TAKE = 1
 CEN_S = []
-C_TAKE = 3
+C_TAKE = 2
 
 
 def tile_plate_centred_gene_scores_d2_kernel(tc, x_bytes, x_scale, w_bytes, w_scale, means, gain, out):
@@ -182,16 +182,15 @@ def tile_plate_centred_gene_scores_d2_kernel(tc, x_bytes, x_scale, w_bytes, w_sc
         for g in range(G):
             wide[MEANS, g] = mw[:, 512 * g : 512 * g + 512]
 
-        def turn_x(r):
-            for b in range(2):
-                pt = turn.tile([P, 2, 2, P], F32, name="pt")
-                for j in range(2):
-                    g = 2 * b + j
-                    words = wide[r, g].bitcast(F32)
-                    for u in range(2):
-                        src = words[:, P * u : P * u + P] if on_vector(r, g) else words[:, u : 2 * P : 2]
-                        nc.tensor.transpose(pt[:, j, u, :], src, ident[:])
-                banks[r, b] = pt
+        def turn_x(r, b):
+            pt = turn.tile([P, 2, 2, P], F32, name="pt")
+            for j in range(2):
+                g = 2 * b + j
+                words = wide[r, g].bitcast(F32)
+                for u in range(2):
+                    src = words[:, P * u : P * u + P] if on_vector(r, g) else words[:, u : 2 * P : 2]
+                    nc.tensor.transpose(pt[:, j, u, :], src, ident[:])
+            banks[r, b] = pt
 
         def exit_x(r, b):
             if b == 0:
@@ -223,14 +222,16 @@ def tile_plate_centred_gene_scores_d2_kernel(tc, x_bytes, x_scale, w_bytes, w_sc
             )
 
         def multiply(units):
+            if len(full) == ACCS:
+                empty_oldest()
             t = accs.tile([P, BANK], F32, name="acc")
+            full.append((units, t))
             at = 0
             for r, part in units:
                 n = PARTS[part][1]
                 for g in range(G):
                     one_pass(t[:, at : at + n], r, part, g)
                 at += n
-            return t
 
         def columns(tile, units):
             c0, n = PARTS[units[0][1]]
@@ -272,22 +273,39 @@ def tile_plate_centred_gene_scores_d2_kernel(tc, x_bytes, x_scale, w_bytes, w_sc
             else:
                 nc.vector.tensor_copy(out=cen[:, c0 : c0 + n], in_=acc[:, :n])
 
+        rounds = [[r] for r in range(2, PAIRS_FROM)] + [[r, r + 1] for r in range(PAIRS_FROM, R, 2)] + [[]]
         done = {1: 0, 2: 0}
-        plan = []
-        for s in range(R):
-            step = [[(s, 0)]]
-            narrow = []
-            for part, first in ((1, STEP_B), (2, STEP_C)):
-                if s >= first:
-                    take = min(s + 1 - done[part], B_TAKE if part == 1 else C_TAKE)
-                    narrow += [(done[part] + j, part) for j in range(take)]
+        plan = [[]]
+        for before in rounds[:-1]:
+            step = []
+            narrow = {}
+            for part, first, extra in ((1, STEP_B, B_TAKE), (2, STEP_C, C_TAKE)):
+                narrow[part] = []
+                if before[-1] >= first:
+                    if done[part] == 0:
+                        step.append([(MEANS, part)])
+                    take = min(before[-1] + 1 - done[part], len(before) + extra)
+                    narrow[part] = [(done[part] + j, part) for j in range(take)]
                     done[part] += take
-            if len([u for u in narrow if u[1] == 1]) == 1 and len(narrow) > 1:
-                step.append([narrow[0], narrow[-1]])
-                narrow = narrow[1:-1]
-            step += [narrow[j : j + 2] for j in range(0, len(narrow), 2)]
+            mixed = min(len(narrow[1]), len(narrow[2]))
+            pairs = [[narrow[1][j - mixed], narrow[2][j - mixed]] for j in range(mixed)]
+            rest = narrow[1][: len(narrow[1]) - mixed] + narrow[2][: len(narrow[2]) - mixed]
+            for r in before:
+                step.append([(r, 0)])
+                step += pairs[:1]
+                pairs = pairs[1:]
+            step += pairs + [rest[j : j + 2] for j in range(0, len(rest), 2)]
             plan.append(step)
         assert done == {1: R, 2: R}
+
+        full, waiting = [], []
+
+        def empty_oldest():
+            units, acc = full.pop(0)
+            if units[0][0] == MEANS:
+                centre(units[0][1], acc)
+            else:
+                waiting.append((units, subtract(units, acc)))
 
         w_jobs = {}
         for g in range(G):
@@ -297,19 +315,22 @@ def tile_plate_centred_gene_scores_d2_kernel(tc, x_bytes, x_scale, w_bytes, w_sc
         widen_w(0, 0)
         pick_w_scales()
         widen_x(0, False)
-        turn_x(0)
-        widen_w(0, 1)
+        turn_x(0, 0)
+        turn_x(0, 1)
         scale_w(0, 0)
+        widen_w(0, 1)
         widen_x(1, False, range(2))
         exit_x(0, 0)
         exit_x(0, 1)
-        turn_x(MEANS)
+        turn_x(MEANS, 0)
+        turn_x(MEANS, 1)
         widen_x(1, False, range(2, G))
         exit_x(MEANS, 0)
         exit_x(MEANS, 1)
-        turn_x(1)
-        scale_w(0, 1)
+        turn_x(1, 0)
+        turn_x(1, 1)
         quant_w(0, 0)
+        scale_w(0, 1)
         widen_w(0, 2)
         quant_w(0, 1)
         quant_x(0)
@@ -327,68 +348,69 @@ def tile_plate_centred_gene_scores_d2_kernel(tc, x_bytes, x_scale, w_bytes, w_sc
         for h in range(2):
             cols = slice(BANK * h, BANK * h + BANK)
             nc.tensor.matmul(out=gain_p[:, cols], lhsT=ident_b[:], rhs=gain_b[:, cols], start=True, stop=True)
-        early = {r: accs.tile([P, BANK], F32, name="acc") for r in (0, MEANS, 1)}
+        early = {r: accs.tile([P, BANK], F32, name="acc") for r in (MEANS, 0, 1)}
         for r in (0, MEANS):
             for g in range(G - 1):
                 one_pass(early[r][:], r, 0, g)
-        turn_x(2)
+        turn_x(2, 0)
+        turn_x(2, 1)
         for g in range(G - 1):
             one_pass(early[1][:], 1, 0, g)
         for r in (MEANS, 0, 1):
             one_pass(early[r][:], r, 0, G - 1)
-        means_acc = (0, early[MEANS])
-        pending = []
-        waiting = []
-        for s in range(2, R + 1):
-            jobs = w_jobs.get(s, [])
-            if 2 < s < R:
-                turn_x(s)
+        full.extend([([(r, 0)], early[r]) for r in early])
+        for i, tiles in enumerate(rounds[:-1]):
+            following = rounds[i + 1]
+            by_scalar = [(r, g) for r in following for g in range(G) if not on_vector(r, g)]
+            jobs = [job for r in tiles for job in w_jobs.get(r, [])]
+            if i > 0:
+                for r in tiles:
+                    turn_x(r, 0)
+                    if r == tiles[0]:
+                        turn_x(r, 1)
             for job in jobs:
                 widen_w(*job)
-            if means_acc is not None:
-                centre(*means_acc)
-            waiting += [(units, subtract(units, acc)) for units, acc in pending]
-            means_acc = None
-            if s - 1 in (STEP_B, STEP_C):
-                part = 1 if s - 1 == STEP_B else 2
-                means_acc = (part, multiply([(MEANS, part)]))
-            if s == 2:
-                pending = [([(r, 0)], early[r]) for r in (0, 1)]
-            else:
-                pending = [(units, multiply(units)) for units in plan[s - 1]] if s - 1 < R else []
-            if s + 1 < R:
-                widen_x(s + 1, False, range(SPLIT))
-            if s < R:
-                exit_x(s, 0)
-                exit_x(s, 1)
-            if s + 1 < R:
-                widen_x(s + 1, False, range(SPLIT, G))
-            if s < C_EARLY:
-                quant_x(s)
+            for j in range(1 if i == 0 else len(full)):
+                empty_oldest()
+            split = SPLIT if len(tiles) == 1 else SPLIT2
+            for r, g in by_scalar[:split]:
+                widen_x(r, False, [g])
+            exit_x(tiles[0], 0)
+            for r in tiles[1:]:
+                turn_x(r, 1)
+            for units in plan[i]:
+                multiply(units)
+            exit_x(tiles[0], 1)
+            for r in tiles[1:]:
+                exit_x(r, 0)
+                exit_x(r, 1)
+            for r, g in by_scalar[split:]:
+                widen_x(r, False, [g])
+            if i == 0:
+                quant_x(tiles[0])
             for job in jobs:
                 scale_w(*job)
-            if s == R - 1:
-                quant_x(s)
-            quota = min(len(waiting), max(0, QUOTA - 2 * len(jobs))) if s < R else 0
-            for j in range(quota):
+            quota = min(len(waiting), max(0, QUOTA * len(tiles) - 2 * len(jobs)))
+            for j in range(quota if following else len(waiting)):
                 finish(*waiting.pop(0))
             for job in jobs:
                 quant_w(*job)
-            if s + 2 < R:
-                widen_x(s + 2, True)
-            if C_EARLY <= s < R - 1:
-                quant_x(s)
-            if GP_FROM <= s < GP_TO:
-                for j in range(min(GP_N, len(waiting))):
-                    finish(*waiting.pop(0), grp[min(s, R - 1)][:].bitcast(F32)[:, BANK * j : BANK * j + BANK])
-        for j, (units, diff) in enumerate(waiting):
-            finish(units, diff, diff[:] if j < TAIL_GP else None)
-        last_units, last_acc = pending.pop()
-        diffs = [(units, subtract(units, acc)) for units, acc in pending]
-        halves = []
-        for j, unit in enumerate(last_units):
-            halves.append(([unit], subtract([unit], last_acc[:, 256 * j : 256 * j + 256])))
-            if diffs:
-                finish(*diffs.pop(0))
-        for units, diff in halves:
-            finish(units, diff)
+            for r in rounds[i + 2] if i + 2 < len(rounds) else []:
+                widen_x(r, True)
+            for r in tiles if i > 0 else []:
+                quant_x(r)
+            if GP_FROM <= tiles[0]:
+                for j in range(min(GP_N if len(tiles) == 1 else GP_N2, len(waiting))):
+                    room = grp[tiles[-1 - j // 2]][:].bitcast(F32)
+                    finish(*waiting.pop(0), room[:, BANK * (j % 2) : BANK * (j % 2) + BANK])
+
+        for units in plan[-1][:-1] + [[unit] for unit in plan[-1][-1]]:
+            multiply(units)
+        count = 0
+        while full:
+            empty_oldest()
+            if len(waiting) > 1:
+                units, diff = waiting.pop(0)
+                finish(units, diff, diff[:] if count in TAIL_GP else None)
+                count += 1
+        finish(*waiting.pop(0))

@@ -23,27 +23,141 @@ BANK = 512
 MEANS = R
 PARTS = [(0, 512), (512, 256), (768, 256)]
 
+ACCS = 4
+TURNS = 3
+XG = 4
+WIDE = 12
 STEP_B = 3
 STEP_C = 6
-V_PASSES = 1
-V_FROM = 10
-V_EXIT_FROM = 99
-D_ON_S = []
-GP_FROM = 6
-QUOTA = 2
-SPLIT = 2
-ACCS = 4
-XG = 4
-GP_N = 1
-PAIRS_FROM = 16
-SPLIT2 = 1
-GP_N2 = 3
-TAIL_GP = [1]
-B_PER = 2
-C_PER = 2
-B_TAKE = 1
-CEN_S = []
-C_TAKE = 2
+RUNS_FROM = 7
+RUN = 2
+TAKE = 3
+V_FROM = 8
+V_TWO = 99
+GP_FROM = 7
+LEAD = 2
+G_V = 2
+EARLY = 2
+C_AT = 2
+V_EARLY = []
+D_S = []
+D_AT = 0
+GP_TWO = 3
+CEN_S = [1,2]
+WS_FIRST = 0
+ORDER = None
+
+
+def default_order():
+    vector_w = [(r, g) for r in range(V_FROM, R) for g in ((1, 3) if r >= V_TWO else (3,))] + V_EARLY
+    halves = [(r, b) for r in range(RUNS_FROM, R) for b in range(2)]
+    runs = [[(r, 0), (r, 1)] for r in range(2, RUNS_FROM)] + [halves[j : j + RUN] for j in range(0, len(halves), RUN)]
+
+    def passes(run, on_vector):
+        return [("W", r, g) for r, b in run for g in (2 * b, 2 * b + 1) if ((r, g) in vector_w) == on_vector]
+
+    def all_jobs(s):
+        return [(part, g) for part, first in ((1, STEP_B), (2, STEP_C)) for g in range(G) if first - (G - 1 - g) // 2 == s]
+
+    scalar = passes([(0, 0), (0, 1), (1, 0)], False) + [("B", 0, 0), ("B", 0, 1)] + passes([(1, 1)], False)
+    scalar += [("B", MEANS, 0), ("B", MEANS, 1)] + passes([(2, 0)], False) + [("B", 1, 0), ("B", 1, 1)] + passes([(2, 1)], False)
+    scalar += [("D",) + job for job in all_jobs(2) if job in D_S]
+    banks = [[(MEANS, 0)], [(0, 0)], [(1, 0)]]
+    tensor = [("T", r, b) for r in (0, MEANS, 1) for b in range(2)] + [("gain",)]
+    tensor += [("Ma", 1), ("Ma", 0), ("T", 2, 0), ("T", 2, 1), ("Ma", 2), ("Mb", 0), ("Mb", 1), ("Mb", 2)]
+    vector = ([("ws",), ("D", 0, 0)] if WS_FIRST else [("D", 0, 0), ("ws",)]) + [("D", 0, 1), ("E", 0, 0), ("E", 0, 1), ("Q", 0, 0), ("D", 0, 2), ("Q", 0, 1), ("C", 0)]
+    vector += [("E", 0, 2), ("D", 0, 3), ("Q", 0, 2), ("C", MEANS), ("E", 0, 3), ("C", 1), ("Q", 0, 3)] + passes(runs[1], True)
+    pool, stores = [], []
+    done = [2, 0, 0]
+    emptied = 0
+    waiting = []
+    ready = 2
+    for i, run in enumerate(runs + [[]]):
+        s = i + 2
+        jobs = all_jobs(s)
+        if i > 0:
+            tensor += [("T",) + half for half in run]
+        following = passes(runs[i + 1], False) if i + 1 < len(runs) else []
+        ahead = [("D",) + job for job in all_jobs(s + 1) if job in D_S]
+        scalar += following[:LEAD] + [("B",) + half for half in run] + ahead[:D_AT] + following[LEAD:] + ahead[D_AT:]
+        vector += [("D",) + job for job in jobs if job not in D_S]
+        upto = 1 if i == 0 else len(banks)
+        first_of_round = len(banks)
+        step = []
+        for part, first in ((1, STEP_B), (2, STEP_C)):
+            if s - 1 == first:
+                step.append([(MEANS, part)])
+        room = len(step) + (TAKE if s - 1 >= STEP_C else 2) if run else 99
+        while len(step) < room:
+            narrow = [part for part, first in ((1, STEP_B), (2, STEP_C)) if s - 1 >= first]
+            behind = min([done[part] for part in narrow], default=R)
+            if done[0] < ready and (done[0] <= behind + 99 and (not step or step[-1][0][1] != 0 or behind >= ready)):
+                step.append([(done[0], 0)])
+                done[0] += 1
+            elif behind < ready:
+                pair = []
+                for j in range(2):
+                    part = min(narrow, key=lambda q: done[q])
+                    if done[part] < ready:
+                        pair.append((done[part], part))
+                        done[part] += 1
+                step.append(sorted(pair, key=lambda u: (u[1], u[0])))
+            else:
+                break
+        if s - 1 == STEP_B and EARLY:
+            step = [step[0], step[2], step[1]]
+        if s - 1 == STEP_C:
+            step = [step[1], step[0]] + step[2:]
+        if not run:
+            step = step[:-1] + [[unit] for unit in step[-1]]
+        tensor += [("M", len(banks) + j) for j in range(len(step))]
+        if s - 1 == STEP_B and EARLY:
+            tensor.remove(("M", 3))
+            tensor.insert(tensor.index(("T", 4, EARLY - 1)), ("M", 3))
+        banks += step
+        wide_round = len([units for units in step if units[0][0] != MEANS]) >= GP_TWO
+        upto = max(upto, len(banks) - ACCS) if run else first_of_round
+        moved = [("F", k) for k in range(emptied, upto) if banks[k][0][0] == MEANS and banks[k][0][1] in CEN_S]
+        at = len(scalar) - len(following) - len(run) - len(ahead)
+        scalar[at:at] = moved
+        late = [("F", k) for k in range(emptied, upto) if ("F", k) not in moved]
+        if not (s == STEP_B and EARLY):
+            vector += late
+            late = []
+        waiting += [k for k in range(emptied, upto) if banks[k][0][0] != MEANS]
+        emptied = upto
+        complete = [r for r, b in run if b == 1]
+        if i == 0:
+            vector.append(("C", 2))
+        vector += [("E",) + job for job in jobs[:C_AT]]
+        if jobs and s > STEP_B:
+            vector += [("C", r) for r in complete]
+        vector += [("E",) + job for job in jobs[C_AT:]]
+        quota = 0 if jobs or s <= STEP_C else G_V
+        if not run or i + 1 == len(runs):
+            quota = len(waiting) - (0 if run else 1)
+        vector += [("G", k) for k in waiting[:quota]]
+        stores += waiting[:quota]
+        waiting = waiting[quota:]
+        vector += [("Q",) + job for job in jobs]
+        vector += passes(runs[i + 2], True) if i + 2 < len(runs) else []
+        if i > 0:
+            vector += late[:1] + [("C", r) for r in complete if ("C", r) not in vector] + late[1:]
+        ready = max(complete, default=ready - 1) + 1
+        if s >= GP_FROM:
+            for r in (complete + [None])[: 2 if wide_round else 1]:
+                if waiting:
+                    pool.append(("G", waiting[0], r))
+                    stores.append(waiting.pop(0))
+    for k in range(emptied, len(banks)):
+        vector.append(("F", k))
+        if k > emptied:
+            vector.append(("G", k - 1))
+            stores.append(k - 1)
+    vector.append(("G", len(banks) - 1))
+    stores.append(len(banks) - 1)
+    assert not waiting
+    return banks, tensor, scalar, vector, pool, [("St", k) for k in stores]
 
 
 def tile_plate_centred_gene_scores_d2_kernel(tc, x_bytes, x_scale, w_bytes, w_scale, means, gain, out):
@@ -52,7 +166,7 @@ def tile_plate_centred_gene_scores_d2_kernel(tc, x_bytes, x_scale, w_bytes, w_sc
         keep = ctx.enter_context(tc.tile_pool(name="keep", bufs=1))
         work = ctx.enter_context(tc.tile_pool(name="work", bufs=3))
         outs = ctx.enter_context(tc.tile_pool(name="outs", bufs=4))
-        turn = ctx.enter_context(tc.psum_pool(name="turn", bufs=7 - ACCS))
+        turn = ctx.enter_context(tc.psum_pool(name="turn", bufs=TURNS))
         accs = ctx.enter_context(tc.psum_pool(name="accs", bufs=ACCS))
         fixed = ctx.enter_context(tc.psum_pool(name="fixed", bufs=1))
         ctx.enter_context(tc.manual_schedule())
@@ -67,7 +181,13 @@ def tile_plate_centred_gene_scores_d2_kernel(tc, x_bytes, x_scale, w_bytes, w_sc
         x_rows = x_bytes.rearrange("(p r) k -> p r k", r=R)
         out_rows = out.rearrange("(p r) n -> p r n", r=R)
 
-        xs = keep.tile([P, R, C], F32, name="xs")
+        xs_first = keep.tile([P, 2, C], F32, name="xs_first")
+        xs_rest = keep.tile([P, R - 2, C], F32, name="xs_rest")
+        x_scales = x_scale.rearrange("(p r) c -> p r c", r=R)
+
+        def scale_of(r, c):
+            return xs_first[:, r, c : c + 1] if r < 2 else xs_rest[:, r - 2, c : c + 1]
+
         wsb = keep.tile([P, C * 8], F32, name="wsb")
         ws = keep.tile([P, G, 8], F32, name="ws")
         gain_b = keep.tile([P, N], BF16, name="gain_b")
@@ -89,21 +209,29 @@ def tile_plate_centred_gene_scores_d2_kernel(tc, x_bytes, x_scale, w_bytes, w_sc
             t = keep.tile([P, rows * K], U8, name="xb%d" % r)
             nc.sync.dma_start(out=t[:], in_=x_rows[:, r : r + rows, :].rearrange("p r k -> p (r k)"))
             for j in range(rows):
-                x_raw[r + j] = t[:, j * K : (j + 1) * K]
+                for b in range(2):
+                    x_raw[r + j, b] = t[:, j * K + b * 1024 : j * K + (b + 1) * 1024]
 
-        nc.scalar.dma_start(out=xs[:], in_=x_scale.rearrange("(p r) c -> p r c", r=R))
+        def load_x_half(r, b):
+            t = keep.tile([P, 1024], U8, name="xh%d%d" % (r, b))
+            nc.sync.dma_start(out=t[:], in_=x_rows[:, r, 1024 * b : 1024 * b + 1024])
+            x_raw[r, b] = t[:]
+
         nc.scalar.dma_start(out=wsb[:], in_=w_scale.rearrange("c d -> (c d)").partition_broadcast(P))
+        nc.scalar.dma_start(out=xs_first[:], in_=x_scales[:, :2, :])
         load_w(0, 0)
-        load_x(0, 1)
+        load_x_half(0, 0)
         load_w(0, 1)
+        load_x_half(0, 1)
         load_x(1, 1)
         load_w(0, 2)
         nc.sync.dma_start(out=mw[:], in_=means)
         load_w(0, 3)
+        nc.sync.dma_start(out=xs_rest[:], in_=x_scales[:, 2:, :])
+        load_x(2, 2)
         nc.sync.dma_start(out=gain_b[:], in_=gain.partition_broadcast(P))
         for g in range(G):
             load_w(1, g)
-        load_x(2, 2)
         load_x(4, 2)
         for g in range(G):
             load_w(2, g)
@@ -119,11 +247,11 @@ def tile_plate_centred_gene_scores_d2_kernel(tc, x_bytes, x_scale, w_bytes, w_sc
 
         w_codes, w_scales, w_wide, w_grp = {}, {}, {}, {}
 
-        def widen_w(part, g):
+        def widen_w(part, g, vector):
             n = PARTS[part][1]
             t = work.tile([P, 4 * BANK], BF16, name="ww")
             src = w_raw[part, g][:].bitcast(F8)
-            if (part, g) not in D_ON_S:
+            if vector:
                 nc.vector.tensor_copy(out=t[:, : 4 * n], in_=src)
             else:
                 nc.scalar.copy(out=t[:, : 4 * n], in_=src)
@@ -155,29 +283,26 @@ def tile_plate_centred_gene_scores_d2_kernel(tc, x_bytes, x_scale, w_bytes, w_sc
 
         wide, grp, banks, codes_x, scales_x = {}, {}, {}, {}, {}
 
-        def on_vector(r, g):
-            return V_FROM <= r < R and g >= G - V_PASSES
+        side_by_side = set()
 
-        def widen_x(r, vector, passes=range(G)):
-            for g in passes:
-                if on_vector(r, g) != vector:
-                    continue
-                t = work.tile([P, 512], BF16, name="xv" if vector else "xw", bufs=4 * V_PASSES if vector else 12)
-                for q in range(4):
-                    c = 4 * g + q
-                    src = x_raw[r][:, 128 * c : 128 * c + 128].bitcast(F8)
-                    if vector:
-                        dst = t[:].rearrange("p (u s e) -> p s u e", u=2, e=2)[:, 32 * q : 32 * q + 32, :, :]
-                        nc.vector.tensor_scalar(
-                            out=dst,
-                            in0=src.rearrange("p (s u e) -> p s u e", u=2, e=2),
-                            scalar1=xs[:, r, c : c + 1],
-                            scalar2=None,
-                            op0=ALU.mult,
-                        )
-                    else:
-                        nc.scalar.activation(out=t[:, 128 * q : 128 * q + 128], in_=src, func=COPY, scale=xs[:, r, c : c + 1])
-                wide[r, g] = t[:]
+        def widen_x(r, g, vector):
+            t = work.tile([P, 512], BF16, name="xv" if vector else "xw", bufs=4 if vector else WIDE)
+            for q in range(4):
+                c = 4 * g + q
+                src = x_raw[r, c // 8][:, 128 * (c % 8) : 128 * (c % 8) + 128].bitcast(F8)
+                if vector:
+                    dst = t[:].rearrange("p (u s e) -> p s u e", u=2, e=2)[:, 32 * q : 32 * q + 32, :, :]
+                    nc.vector.tensor_scalar(
+                        out=dst,
+                        in0=src.rearrange("p (s u e) -> p s u e", u=2, e=2),
+                        scalar1=scale_of(r, c),
+                        scalar2=None,
+                        op0=ALU.mult,
+                    )
+                    side_by_side.add((r, g))
+                else:
+                    nc.scalar.activation(out=t[:, 128 * q : 128 * q + 128], in_=src, func=COPY, scale=scale_of(r, c))
+            wide[r, g] = t[:]
 
         for g in range(G):
             wide[MEANS, g] = mw[:, 512 * g : 512 * g + 512]
@@ -188,16 +313,16 @@ def tile_plate_centred_gene_scores_d2_kernel(tc, x_bytes, x_scale, w_bytes, w_sc
                 g = 2 * b + j
                 words = wide[r, g].bitcast(F32)
                 for u in range(2):
-                    src = words[:, P * u : P * u + P] if on_vector(r, g) else words[:, u : 2 * P : 2]
+                    src = words[:, P * u : P * u + P] if (r, g) in side_by_side else words[:, u : 2 * P : 2]
                     nc.tensor.transpose(pt[:, j, u, :], src, ident[:])
             banks[r, b] = pt
 
-        def exit_x(r, b):
-            if b == 0:
-                grp[r] = grouped[len(grp) % XG]
+        def exit_x(r, b, vector):
+            if r not in grp:
+                grp[r] = grouped[places[r] % XG]
             dst = grp[r][:, 1024 * b : 1024 * b + 1024].bitcast(F32).rearrange("p (j s u) -> p j s u", j=2, u=2)
             src = banks[r, b][:].rearrange("p j u s -> p j s u")
-            if b == 0 and V_EXIT_FROM <= r < R:
+            if vector:
                 nc.vector.tensor_copy(out=dst, in_=src)
             else:
                 nc.scalar.copy(out=dst, in_=src)
@@ -221,16 +346,16 @@ def tile_plate_centred_gene_scores_d2_kernel(tc, x_bytes, x_scale, w_bytes, w_sc
                 stop=(g == G - 1),
             )
 
-        def multiply(units):
-            if len(full) == ACCS:
-                empty_oldest()
-            t = accs.tile([P, BANK], F32, name="acc")
-            full.append((units, t))
+        acc, diffs, results = {}, {}, {}
+
+        def multiply(k, passes):
+            if k not in acc:
+                acc[k] = accs.tile([P, BANK], F32, name="acc")
             at = 0
-            for r, part in units:
+            for r, part in psum_banks[k]:
                 n = PARTS[part][1]
-                for g in range(G):
-                    one_pass(t[:, at : at + n], r, part, g)
+                for g in passes:
+                    one_pass(acc[k][:, at : at + n], r, part, g)
                 at += n
 
         def columns(tile, units):
@@ -243,18 +368,30 @@ def tile_plate_centred_gene_scores_d2_kernel(tc, x_bytes, x_scale, w_bytes, w_sc
             n = PARTS[units[0][1]][1]
             return tile[:, : n * len(units)].rearrange("p (j n) -> p j n", n=n)
 
-        def subtract(units, acc):
+        def empty(k, vector):
+            units = psum_banks[k]
+            if units[0][0] == MEANS:
+                c0, n = PARTS[units[0][1]]
+                if vector:
+                    nc.vector.tensor_copy(out=cen[:, c0 : c0 + n], in_=acc[k][:, :n])
+                else:
+                    nc.scalar.copy(out=cen[:, c0 : c0 + n], in_=acc[k][:, :n])
+                return
             t = outs.tile([P, BANK], F32, name="diff", bufs=16)
-            nc.vector.tensor_tensor(out=shaped(t, units), in0=shaped(acc, units), in1=columns(cen, units), op=ALU.subtract)
-            return t
+            nc.vector.tensor_tensor(out=shaped(t, units), in0=shaped(acc[k], units), in1=columns(cen, units), op=ALU.subtract)
+            diffs[k] = t
 
-        def finish(units, diff, room=None):
-            if room is None:
-                t = diff[:]
-                nc.vector.tensor_tensor(out=shaped(t, units), in0=shaped(diff, units), in1=columns(gain_p, units), op=ALU.mult)
+        def apply_gain(k, vector, room):
+            units = psum_banks[k]
+            t = diffs[k][:] if room is None else grp[room][:].bitcast(F32)[:, :BANK]
+            if vector:
+                nc.vector.tensor_tensor(out=shaped(t, units), in0=shaped(diffs[k], units), in1=columns(gain_p, units), op=ALU.mult)
             else:
-                t = room
-                nc.gpsimd.tensor_tensor(out=shaped(t, units), in0=shaped(diff, units), in1=columns(gain_b, units), op=ALU.mult)
+                nc.gpsimd.tensor_tensor(out=shaped(t, units), in0=shaped(diffs[k], units), in1=columns(gain_b, units), op=ALU.mult)
+            results[k] = t
+
+        def store(k):
+            units, t = psum_banks[k], results[k]
             r0, part0 = units[0]
             c0, n = PARTS[part0]
             if len(units) == 2 and units[1] == (r0, part0 + 1):
@@ -266,151 +403,101 @@ def tile_plate_centred_gene_scores_d2_kernel(tc, x_bytes, x_scale, w_bytes, w_sc
                     c0 = PARTS[part][0]
                     nc.sync.dma_start(out=out_rows[:, r, c0 : c0 + n], in_=t[:, j * n : (j + 1) * n])
 
-        def centre(part, acc):
-            c0, n = PARTS[part]
-            if part in CEN_S:
-                nc.scalar.copy(out=cen[:, c0 : c0 + n], in_=acc[:, :n])
+        def spread_gain():
+            for h in range(2):
+                cols = slice(BANK * h, BANK * h + BANK)
+                nc.tensor.matmul(out=gain_p[:, cols], lhsT=ident_b[:], rhs=gain_b[:, cols], start=True, stop=True)
+
+        psum_banks, tensor, scalar, vector, pool, stores = ORDER or default_order()
+        places = {r: j for j, r in enumerate([op[1] for op in tensor if op[0] == "T" and op[2] == 0])}
+        rooms = {op[2]: op[1] for op in pool if op[2] is not None}
+        means_bank = {units[0][1]: k for k, units in enumerate(psum_banks) if units[0][0] == MEANS}
+
+        def earlier(queue, op, kinds, back):
+            same = [o for o in queue if o[0] in kinds]
+            j = same.index(op) - back
+            return same[j] if j >= 0 else None
+
+        def needs(op, queue):
+            kind = op[0]
+            if kind == "W":
+                old = earlier(queue, op, ("W",), 4 if queue is vector else WIDE)
+                return [("T", old[1], old[2] // 2)] if old else []
+            if kind == "T":
+                old = earlier(queue, op, ("T",), TURNS)
+                widened = [("W", op[1], 2 * op[2] + j) for j in range(2)] if op[1] != MEANS else []
+                return widened + ([("B",) + old[1:]] if old else [])
+            if kind == "B":
+                old = [r for r in places if places[r] == places[op[1]] - XG]
+                return [("T",) + op[1:]] + [("C", r) for r in old] + [("St", rooms[r]) for r in old if r in rooms]
+            if kind == "C":
+                return [("B", op[1], 0), ("B", op[1], 1)]
+            if kind == "D":
+                j = 4 * op[1] + op[2] - 3
+                return [("E", j // 4, j % 4)] if j >= 0 else []
+            if kind == "E":
+                j = 4 * op[1] + op[2] - 3
+                return [("D",) + op[1:], ("ws",)] + ([("Q", j // 4, j % 4)] if j >= 0 else [])
+            if kind == "Q":
+                return [("E",) + op[1:]]
+            if kind in ("M", "Ma", "Mb"):
+                last = G - 1 if kind == "Ma" else G
+                old = earlier(queue, op, ("M", "Ma"), ACCS) if kind != "Mb" else None
+                ready = [("C", r) for r, part in psum_banks[op[1]]] + [("Q", part, g) for r, part in psum_banks[op[1]] for g in range(last)]
+                return ready + ([("F", old[1])] if old else []) + ([("Ma", op[1])] if kind == "Mb" else [])
+            if kind == "F":
+                split = ("Mb", op[1]) in tensor
+                centres = [("F", means_bank[part]) for r, part in psum_banks[op[1]] if r != MEANS]
+                return [("Mb" if split else "M", op[1])] + centres
+            if kind == "G":
+                return [("F", op[1]), ("gain",)] + ([("C", op[2])] if len(op) > 2 and op[2] is not None else [])
+            if kind == "St":
+                return [("G", op[1])]
+            return []
+
+        def emit(op, queue):
+            kind, on_vector = op[0], queue is vector
+            if kind == "W":
+                widen_x(op[1], op[2], on_vector)
+            elif kind == "T":
+                turn_x(op[1], op[2])
+            elif kind == "B":
+                exit_x(op[1], op[2], on_vector)
+            elif kind == "C":
+                quant_x(op[1])
+            elif kind == "D":
+                widen_w(op[1], op[2], on_vector)
+            elif kind == "E":
+                scale_w(op[1], op[2])
+            elif kind == "Q":
+                quant_w(op[1], op[2])
+            elif kind == "M":
+                multiply(op[1], range(G))
+            elif kind == "Ma":
+                multiply(op[1], range(G - 1))
+            elif kind == "Mb":
+                multiply(op[1], [G - 1])
+            elif kind == "F":
+                empty(op[1], on_vector)
+            elif kind == "G":
+                apply_gain(op[1], on_vector, None if on_vector else op[2])
+            elif kind == "St":
+                store(op[1])
+            elif kind == "ws":
+                pick_w_scales()
             else:
-                nc.vector.tensor_copy(out=cen[:, c0 : c0 + n], in_=acc[:, :n])
+                spread_gain()
 
-        rounds = [[r] for r in range(2, PAIRS_FROM)] + [[r, r + 1] for r in range(PAIRS_FROM, R, 2)] + [[]]
-        done = {1: 0, 2: 0}
-        plan = [[]]
-        for before in rounds[:-1]:
-            step = []
-            narrow = {}
-            for part, first, extra in ((1, STEP_B, B_TAKE), (2, STEP_C, C_TAKE)):
-                narrow[part] = []
-                if before[-1] >= first:
-                    if done[part] == 0:
-                        step.append([(MEANS, part)])
-                    take = min(before[-1] + 1 - done[part], len(before) + extra)
-                    narrow[part] = [(done[part] + j, part) for j in range(take)]
-                    done[part] += take
-            mixed = min(len(narrow[1]), len(narrow[2]))
-            pairs = [[narrow[1][j - mixed], narrow[2][j - mixed]] for j in range(mixed)]
-            rest = narrow[1][: len(narrow[1]) - mixed] + narrow[2][: len(narrow[2]) - mixed]
-            for r in before:
-                step.append([(r, 0)])
-                step += pairs[:1]
-                pairs = pairs[1:]
-            step += pairs + [rest[j : j + 2] for j in range(0, len(rest), 2)]
-            plan.append(step)
-        assert done == {1: R, 2: R}
-
-        full, waiting = [], []
-
-        def empty_oldest():
-            units, acc = full.pop(0)
-            if units[0][0] == MEANS:
-                centre(units[0][1], acc)
-            else:
-                waiting.append((units, subtract(units, acc)))
-
-        w_jobs = {}
-        for g in range(G):
-            w_jobs.setdefault(STEP_B - (G - 1 - g) // B_PER, []).append((1, g))
-            w_jobs.setdefault(STEP_C - (G - 1 - g) // C_PER, []).append((2, g))
-
-        widen_w(0, 0)
-        pick_w_scales()
-        widen_x(0, False)
-        turn_x(0, 0)
-        turn_x(0, 1)
-        scale_w(0, 0)
-        widen_w(0, 1)
-        widen_x(1, False, range(2))
-        exit_x(0, 0)
-        exit_x(0, 1)
-        turn_x(MEANS, 0)
-        turn_x(MEANS, 1)
-        widen_x(1, False, range(2, G))
-        exit_x(MEANS, 0)
-        exit_x(MEANS, 1)
-        turn_x(1, 0)
-        turn_x(1, 1)
-        quant_w(0, 0)
-        scale_w(0, 1)
-        widen_w(0, 2)
-        quant_w(0, 1)
-        quant_x(0)
-        scale_w(0, 2)
-        widen_w(0, 3)
-        quant_w(0, 2)
-        quant_x(MEANS)
-        scale_w(0, 3)
-        widen_x(2, False, range(2))
-        exit_x(1, 0)
-        exit_x(1, 1)
-        widen_x(2, False, range(2, G))
-        quant_x(1)
-        quant_w(0, 3)
-        for h in range(2):
-            cols = slice(BANK * h, BANK * h + BANK)
-            nc.tensor.matmul(out=gain_p[:, cols], lhsT=ident_b[:], rhs=gain_b[:, cols], start=True, stop=True)
-        early = {r: accs.tile([P, BANK], F32, name="acc") for r in (MEANS, 0, 1)}
-        for r in (0, MEANS):
-            for g in range(G - 1):
-                one_pass(early[r][:], r, 0, g)
-        turn_x(2, 0)
-        turn_x(2, 1)
-        for g in range(G - 1):
-            one_pass(early[1][:], 1, 0, g)
-        for r in (MEANS, 0, 1):
-            one_pass(early[r][:], r, 0, G - 1)
-        full.extend([([(r, 0)], early[r]) for r in early])
-        for i, tiles in enumerate(rounds[:-1]):
-            following = rounds[i + 1]
-            by_scalar = [(r, g) for r in following for g in range(G) if not on_vector(r, g)]
-            jobs = [job for r in tiles for job in w_jobs.get(r, [])]
-            if i > 0:
-                for r in tiles:
-                    turn_x(r, 0)
-                    if r == tiles[0]:
-                        turn_x(r, 1)
-            for job in jobs:
-                widen_w(*job)
-            for j in range(1 if i == 0 else len(full)):
-                empty_oldest()
-            split = SPLIT if len(tiles) == 1 else SPLIT2
-            for r, g in by_scalar[:split]:
-                widen_x(r, False, [g])
-            exit_x(tiles[0], 0)
-            for r in tiles[1:]:
-                turn_x(r, 1)
-            for units in plan[i]:
-                multiply(units)
-            exit_x(tiles[0], 1)
-            for r in tiles[1:]:
-                exit_x(r, 0)
-                exit_x(r, 1)
-            for r, g in by_scalar[split:]:
-                widen_x(r, False, [g])
-            if i == 0:
-                quant_x(tiles[0])
-            for job in jobs:
-                scale_w(*job)
-            quota = min(len(waiting), max(0, QUOTA * len(tiles) - 2 * len(jobs)))
-            for j in range(quota if following else len(waiting)):
-                finish(*waiting.pop(0))
-            for job in jobs:
-                quant_w(*job)
-            for r in rounds[i + 2] if i + 2 < len(rounds) else []:
-                widen_x(r, True)
-            for r in tiles if i > 0 else []:
-                quant_x(r)
-            if GP_FROM <= tiles[0]:
-                for j in range(min(GP_N if len(tiles) == 1 else GP_N2, len(waiting))):
-                    room = grp[tiles[-1 - j // 2]][:].bitcast(F32)
-                    finish(*waiting.pop(0), room[:, BANK * (j % 2) : BANK * (j % 2) + BANK])
-
-        for units in plan[-1][:-1] + [[unit] for unit in plan[-1][-1]]:
-            multiply(units)
-        count = 0
-        while full:
-            empty_oldest()
-            if len(waiting) > 1:
-                units, diff = waiting.pop(0)
-                finish(units, diff, diff[:] if count in TAIL_GP else None)
-                count += 1
-        finish(*waiting.pop(0))
+        queues = [stores, pool, vector, scalar, tensor]
+        at = [0] * len(queues)
+        written = set()
+        while any(at[j] < len(queue) for j, queue in enumerate(queues)):
+            moved = False
+            for j, queue in enumerate(queues):
+                if at[j] < len(queue) and all(need in written for need in needs(queue[at[j]], queue)):
+                    op = queue[at[j]]
+                    emit(op, queue)
+                    written.add(op[:2] if op[0] == "G" else op)
+                    at[j] += 1
+                    moved = True
+            assert moved

@@ -26,126 +26,116 @@ PARTS = [(0, 512), (512, 256), (768, 256)]
 ACCS = 4
 TURNS = 3
 XG = 4
-WIDE = 12
-STEP_B = 3
-STEP_C = 6
-RUNS_FROM = 7
-RUN = 2
+WIDE = 8
+CODES = 12
+STEP_C = 7
+JOBS_C = 5
 TAKE = 3
-V_FROM = 8
-V_TWO = 99
+V_FROM = 10
+V_TWO = 12
 GP_FROM = 7
+GP_TWO = 3
 LEAD = 2
 G_V = 2
-EARLY = 2
-C_AT = 2
-V_EARLY = []
+C_AT = 1
+CEN_S = [1, 2]
 D_S = []
-D_AT = 0
-GP_TWO = 3
-CEN_S = [1,2]
-WS_FIRST = 0
+A_LAST = 7
+KEEP = 1
+CEN_AT = 3
+P_FROM = 9
+LEAD_P = 2
+V_THREE = 99
+GP_TO = 16
 ORDER = None
 
 
 def default_order():
-    vector_w = [(r, g) for r in range(V_FROM, R) for g in ((1, 3) if r >= V_TWO else (3,))] + V_EARLY
-    halves = [(r, b) for r in range(RUNS_FROM, R) for b in range(2)]
-    runs = [[(r, 0), (r, 1)] for r in range(2, RUNS_FROM)] + [halves[j : j + RUN] for j in range(0, len(halves), RUN)]
+    vector_w = [(r, g) for r in range(V_FROM, R) for g in ((0, 1, 3) if r >= V_THREE else (1, 3) if r >= V_TWO else (3,))]
 
-    def passes(run, on_vector):
-        return [("W", r, g) for r, b in run for g in (2 * b, 2 * b + 1) if ((r, g) in vector_w) == on_vector]
+    def passes(r, on_vector):
+        return [("W", r, g) for g in range(G) if r < R and ((r, g) in vector_w) == on_vector]
 
-    def all_jobs(s):
-        return [(part, g) for part, first in ((1, STEP_B), (2, STEP_C)) for g in range(G) if first - (G - 1 - g) // 2 == s]
+    def both(kind, r):
+        return [(kind, r, 0), (kind, r, 1)]
 
-    scalar = passes([(0, 0), (0, 1), (1, 0)], False) + [("B", 0, 0), ("B", 0, 1)] + passes([(1, 1)], False)
-    scalar += [("B", MEANS, 0), ("B", MEANS, 1)] + passes([(2, 0)], False) + [("B", 1, 0), ("B", 1, 1)] + passes([(2, 1)], False)
-    scalar += [("D",) + job for job in all_jobs(2) if job in D_S]
-    banks = [[(MEANS, 0)], [(0, 0)], [(1, 0)]]
-    tensor = [("T", r, b) for r in (0, MEANS, 1) for b in range(2)] + [("gain",)]
-    tensor += [("Ma", 1), ("Ma", 0), ("T", 2, 0), ("T", 2, 1), ("Ma", 2), ("Mb", 0), ("Mb", 1), ("Mb", 2)]
-    vector = ([("ws",), ("D", 0, 0)] if WS_FIRST else [("D", 0, 0), ("ws",)]) + [("D", 0, 1), ("E", 0, 0), ("E", 0, 1), ("Q", 0, 0), ("D", 0, 2), ("Q", 0, 1), ("C", 0)]
-    vector += [("E", 0, 2), ("D", 0, 3), ("Q", 0, 2), ("C", MEANS), ("E", 0, 3), ("C", 1), ("Q", 0, 3)] + passes(runs[1], True)
+    def steps(text, part):
+        return [(word[0], part, int(word[1])) for word in text.split()]
+
+    scalar = passes(0, False)
+    for r in range(R):
+        following = passes(r + 1, False)
+        if r + 1 >= P_FROM:
+            copies = [("P",) + op[1:] for op in following]
+            following = following[:1] + [op for pair in zip(following[1:], copies) for op in pair] + copies[-1:]
+        lead = LEAD if r + 1 < P_FROM else LEAD_P
+        scalar += following[:lead] + both("B", r) + following[lead:] + (both("B", MEANS) if r == 0 else [])
+    banks = [[(0, 0)], [(MEANS, 0)], [(1, 0)], [(2, 0)], [(3, 0)]]
+    tensor = both("T", 0) + both("T", MEANS) + both("T", 1) + [("gain",)] + both("T", 2)
+    tensor += [("M", 0)] + both("T", 3) + [("M", 1), ("M", 2)] + both("T", 4) + [("M", 3), ("M", 4)]
+    vector = [("D", 0, 0), ("ws",)] + steps("D1 E0 D2 Q0 E1 D3 Q1 E2", 0) + [("C", 0)] + steps("Q2 E3", 0)
+    vector += [("D", 1, 0), ("Q", 0, 3), ("C", MEANS), ("D", 1, 1), ("E", 1, 0), ("C", 1)] + steps("E1 Q0 D2 Q1 D3", 1)
+    vector += [("C", 2), ("F", 1), ("E", 1, 2), ("F", 0), ("C", 3)] + steps("E3 Q2 Q3", 1) + [("F", 2), ("C", 4)]
     pool, stores = [], []
-    done = [2, 0, 0]
-    emptied = 0
-    waiting = []
-    ready = 2
-    for i, run in enumerate(runs + [[]]):
-        s = i + 2
-        jobs = all_jobs(s)
-        if i > 0:
-            tensor += [("T",) + half for half in run]
-        following = passes(runs[i + 1], False) if i + 1 < len(runs) else []
-        ahead = [("D",) + job for job in all_jobs(s + 1) if job in D_S]
-        scalar += following[:LEAD] + [("B",) + half for half in run] + ahead[:D_AT] + following[LEAD:] + ahead[D_AT:]
+    done = [4, 0, 0]
+    emptied = 3
+    waiting = [0, 2]
+    for s in range(5, R + 1):
+        jobs = [(2, g) for g in range(G) if JOBS_C + g // 2 == s]
+        if s < R:
+            tensor += both("T", s)
         vector += [("D",) + job for job in jobs if job not in D_S]
-        upto = 1 if i == 0 else len(banks)
-        first_of_round = len(banks)
-        step = []
-        for part, first in ((1, STEP_B), (2, STEP_C)):
-            if s - 1 == first:
-                step.append([(MEANS, part)])
-        room = len(step) + (TAKE if s - 1 >= STEP_C else 2) if run else 99
-        while len(step) < room:
-            narrow = [part for part, first in ((1, STEP_B), (2, STEP_C)) if s - 1 >= first]
-            behind = min([done[part] for part in narrow], default=R)
-            if done[0] < ready and (done[0] <= behind + 99 and (not step or step[-1][0][1] != 0 or behind >= ready)):
-                step.append([(done[0], 0)])
-                done[0] += 1
-            elif behind < ready:
-                pair = []
-                for j in range(2):
-                    part = min(narrow, key=lambda q: done[q])
-                    if done[part] < ready:
-                        pair.append((done[part], part))
-                        done[part] += 1
+        before = len(banks)
+        narrow = [1, 2] if s >= STEP_C else [1]
+        step = [[(MEANS, 1)]] if s == 5 else []
+        wide = [[(s - 1, 0)]]
+        if s > A_LAST:
+            step += wide
+        if s == STEP_C:
+            step += [[(done[1], 1), (done[1] + 1, 1)]] + wide + [[(MEANS, 2)]]
+            done[1] += 2
+            wide = []
+        for j in range((TAKE if s >= STEP_C else 2) - 1 - (s == STEP_C)):
+            pair = []
+            for i in range(2):
+                part = min(narrow, key=lambda q: done[q])
+                if done[part] < s:
+                    pair.append((done[part], part))
+                    done[part] += 1
+            if pair:
                 step.append(sorted(pair, key=lambda u: (u[1], u[0])))
-            else:
-                break
-        if s - 1 == STEP_B and EARLY:
-            step = [step[0], step[2], step[1]]
-        if s - 1 == STEP_C:
-            step = [step[1], step[0]] + step[2:]
-        if not run:
+        if s <= A_LAST:
+            step += wide
+        if s == R:
             step = step[:-1] + [[unit] for unit in step[-1]]
-        tensor += [("M", len(banks) + j) for j in range(len(step))]
-        if s - 1 == STEP_B and EARLY:
-            tensor.remove(("M", 3))
-            tensor.insert(tensor.index(("T", 4, EARLY - 1)), ("M", 3))
+        tensor += [("M", before + j) for j in range(len(step))]
         banks += step
-        wide_round = len([units for units in step if units[0][0] != MEANS]) >= GP_TWO
-        upto = max(upto, len(banks) - ACCS) if run else first_of_round
-        moved = [("F", k) for k in range(emptied, upto) if banks[k][0][0] == MEANS and banks[k][0][1] in CEN_S]
-        at = len(scalar) - len(following) - len(run) - len(ahead)
-        scalar[at:at] = moved
-        late = [("F", k) for k in range(emptied, upto) if ("F", k) not in moved]
-        if not (s == STEP_B and EARLY):
-            vector += late
-            late = []
-        waiting += [k for k in range(emptied, upto) if banks[k][0][0] != MEANS]
+        upto = max(before, len(banks) - ACCS) if s < R else before
+        for k in range(emptied, upto):
+            if banks[k][0][0] != MEANS:
+                vector.append(("F", k))
+                waiting.append(k)
+            elif banks[k][0][1] in CEN_S:
+                scalar.insert(scalar.index(("B", s - 1, 1)) + CEN_AT, ("F", k))
+            else:
+                vector.append(("F", k))
         emptied = upto
-        complete = [r for r, b in run if b == 1]
-        if i == 0:
-            vector.append(("C", 2))
-        vector += [("E",) + job for job in jobs[:C_AT]]
-        if jobs and s > STEP_B:
-            vector += [("C", r) for r in complete]
-        vector += [("E",) + job for job in jobs[C_AT:]]
-        quota = 0 if jobs or s <= STEP_C else G_V
-        if not run or i + 1 == len(runs):
-            quota = len(waiting) - (0 if run else 1)
+        for job in [(2, g) for g in range(G) if JOBS_C + g // 2 == s + 1 or (s == 5 and JOBS_C + g // 2 == s)]:
+            if job in D_S:
+                scalar.insert(scalar.index(("B", s - (JOBS_C + job[1] // 2 == s), 1)) + 1, ("D",) + job)
+        vector += [("E",) + job for job in jobs[:C_AT]] + ([("C", s)] if jobs else []) + [("E",) + job for job in jobs[C_AT:]]
+        quota = 0 if jobs else min(G_V, len(waiting) - KEEP)
+        if s >= R - 1:
+            quota = len(waiting) - (s == R or s < GP_TO)
         vector += [("G", k) for k in waiting[:quota]]
         stores += waiting[:quota]
         waiting = waiting[quota:]
-        vector += [("Q",) + job for job in jobs]
-        vector += passes(runs[i + 2], True) if i + 2 < len(runs) else []
-        if i > 0:
-            vector += late[:1] + [("C", r) for r in complete if ("C", r) not in vector] + late[1:]
-        ready = max(complete, default=ready - 1) + 1
+        vector += [("Q",) + job for job in jobs] + passes(s + 2, True)
+        if not jobs and s < R:
+            vector.append(("C", s))
         if s >= GP_FROM:
-            for r in (complete + [None])[: 2 if wide_round else 1]:
+            wide_round = len([units for units in step if units[0][0] != MEANS]) >= GP_TWO
+            for r in [s if s < R else None, None][: 2 if wide_round and s < R else 1]:
                 if waiting:
                     pool.append(("G", waiting[0], r))
                     stores.append(waiting.pop(0))
@@ -156,7 +146,7 @@ def default_order():
             stores.append(k - 1)
     vector.append(("G", len(banks) - 1))
     stores.append(len(banks) - 1)
-    assert not waiting
+    assert not waiting and done == [4, R, R]
     return banks, tensor, scalar, vector, pool, [("St", k) for k in stores]
 
 
@@ -249,7 +239,7 @@ def tile_plate_centred_gene_scores_d2_kernel(tc, x_bytes, x_scale, w_bytes, w_sc
 
         def widen_w(part, g, vector):
             n = PARTS[part][1]
-            t = work.tile([P, 4 * BANK], BF16, name="ww")
+            t = work.tile([P, 4 * BANK], BF16, name="ww", bufs=2)
             src = w_raw[part, g][:].bitcast(F8)
             if vector:
                 nc.vector.tensor_copy(out=t[:, : 4 * n], in_=src)
@@ -259,7 +249,7 @@ def tile_plate_centred_gene_scores_d2_kernel(tc, x_bytes, x_scale, w_bytes, w_sc
 
         def scale_w(part, g):
             c0, n = PARTS[part]
-            t = work.tile([P, 4 * BANK], BF16, name="wg", align_bytes=64)
+            t = work.tile([P, 4 * BANK], BF16, name="wg", bufs=2, align_bytes=64)
             src = w_wide[part, g][:, : 4 * n].rearrange("p (t c i) -> p c t i", t=4, i=4)
             dst = t[:, : 4 * n].rearrange("p (c i t) -> p c t i", t=4, i=4)
             for j in range(n // 128):
@@ -304,6 +294,12 @@ def tile_plate_centred_gene_scores_d2_kernel(tc, x_bytes, x_scale, w_bytes, w_sc
                     nc.scalar.activation(out=t[:, 128 * q : 128 * q + 128], in_=src, func=COPY, scale=scale_of(r, c))
             wide[r, g] = t[:]
 
+        def reorder_x(r, g):
+            t = work.tile([P, 2, P], F32, name="xp", bufs=6)
+            nc.scalar.copy(out=t[:], in_=wide[r, g].bitcast(F32).rearrange("p (s u) -> p u s", u=2))
+            wide[r, g] = t[:].rearrange("p u s -> p (u s)").bitcast(BF16)
+            side_by_side.add((r, g))
+
         for g in range(G):
             wide[MEANS, g] = mw[:, 512 * g : 512 * g + 512]
 
@@ -328,8 +324,8 @@ def tile_plate_centred_gene_scores_d2_kernel(tc, x_bytes, x_scale, w_bytes, w_sc
                 nc.scalar.copy(out=dst, in_=src)
 
         def quant_x(r):
-            codes = keep.tile([P, G * P], U32, name="xc%d" % r, align_bytes=64)
-            scales = keep.tile([P, G * P], U8, name="xq%d" % r, align_bytes=64)
+            codes = work.tile([P, G * P], U32, name="xc", bufs=CODES, align_bytes=64)
+            scales = work.tile([P, G * P], U8, name="xq", bufs=CODES, align_bytes=64)
             nc.vector.quantize_mx(out=codes[:].bitcast(X4), scales=scales[:], in_=grp[r][:])
             codes_x[r] = codes
             scales_x[r] = scales
@@ -377,7 +373,7 @@ def tile_plate_centred_gene_scores_d2_kernel(tc, x_bytes, x_scale, w_bytes, w_sc
                 else:
                     nc.scalar.copy(out=cen[:, c0 : c0 + n], in_=acc[k][:, :n])
                 return
-            t = outs.tile([P, BANK], F32, name="diff", bufs=16)
+            t = outs.tile([P, BANK], F32, name="diff", bufs=33)
             nc.vector.tensor_tensor(out=shaped(t, units), in0=shaped(acc[k], units), in1=columns(cen, units), op=ALU.subtract)
             diffs[k] = t
 
@@ -422,21 +418,27 @@ def tile_plate_centred_gene_scores_d2_kernel(tc, x_bytes, x_scale, w_bytes, w_sc
             kind = op[0]
             if kind == "W":
                 old = earlier(queue, op, ("W",), 4 if queue is vector else WIDE)
-                return [("T", old[1], old[2] // 2)] if old else []
+                return [("P",) + old[1:] if ("P",) + old[1:] in scalar else ("T", old[1], old[2] // 2)] if old else []
+            if kind == "P":
+                old = earlier(queue, op, ("P",), 6)
+                return [("W",) + op[1:]] + ([("T", old[1], old[2] // 2)] if old else [])
             if kind == "T":
                 old = earlier(queue, op, ("T",), TURNS)
                 widened = [("W", op[1], 2 * op[2] + j) for j in range(2)] if op[1] != MEANS else []
+                widened = [("P",) + need[1:] if ("P",) + need[1:] in scalar else need for need in widened]
                 return widened + ([("B",) + old[1:]] if old else [])
             if kind == "B":
                 old = [r for r in places if places[r] == places[op[1]] - XG]
                 return [("T",) + op[1:]] + [("C", r) for r in old] + [("St", rooms[r]) for r in old if r in rooms]
             if kind == "C":
-                return [("B", op[1], 0), ("B", op[1], 1)]
+                old = earlier(queue, op, ("C",), CODES)
+                users = [("M", k) for k, units in enumerate(psum_banks) if old and old[1] in [r for r, part in units]]
+                return [("B", op[1], 0), ("B", op[1], 1)] + users
             if kind == "D":
-                j = 4 * op[1] + op[2] - 3
+                j = 4 * op[1] + op[2] - 2
                 return [("E", j // 4, j % 4)] if j >= 0 else []
             if kind == "E":
-                j = 4 * op[1] + op[2] - 3
+                j = 4 * op[1] + op[2] - 2
                 return [("D",) + op[1:], ("ws",)] + ([("Q", j // 4, j % 4)] if j >= 0 else [])
             if kind == "Q":
                 return [("E",) + op[1:]]
@@ -459,6 +461,8 @@ def tile_plate_centred_gene_scores_d2_kernel(tc, x_bytes, x_scale, w_bytes, w_sc
             kind, on_vector = op[0], queue is vector
             if kind == "W":
                 widen_x(op[1], op[2], on_vector)
+            elif kind == "P":
+                reorder_x(op[1], op[2])
             elif kind == "T":
                 turn_x(op[1], op[2])
             elif kind == "B":

@@ -21,132 +21,174 @@ G = K // 512
 C = K // 128
 BANK = 512
 MEANS = R
-PARTS = [(0, 512), (512, 256), (768, 256)]
 
+PART = 512
+PARTS = [(0, 512), (512, 256), (768, 256)]
+J1 = 2
+J1N = 3
+J2 = 4
+J2S = 3
+XA = 9
+X0 = 2
+X1 = 1
+X2 = 1
+X3 = 1
+XB = 9
+XC = 15
+R1 = 13
+RN = 2
+C1 = 0
+CA = 3
+CB = 3
+H1 = 10
+HN = 3
+G1 = 9
+GN = 2
+LD = 6
+MD = 1
+LD0 = 3
+MD0 = 0
+FL = 0
+DLEAD = 0
+D0 = 1
+AH = 1
+KEEP = 1
+GAIN_AT = 2
 ACCS = 4
 TURNS = 3
 XG = 4
-WIDE = 8
-CODES = 12
-STEP_C = 7
-JOBS_C = 5
-TAKE = 3
-V_FROM = 10
-V_TWO = 12
-GP_FROM = 7
-GP_TWO = 3
-LEAD = 2
-G_V = 2
-C_AT = 1
-CEN_S = [1, 2]
-D_S = []
-A_LAST = 7
-KEEP = 1
-CEN_AT = 3
-P_FROM = 9
-LEAD_P = 2
-V_THREE = 99
-GP_TO = 16
-ORDER = None
+CV1 = 0
 
 
-def default_order():
-    vector_w = [(r, g) for r in range(V_FROM, R) for g in ((0, 1, 3) if r >= V_THREE else (1, 3) if r >= V_TWO else (3,))]
+def orders():
+    tiles = [MEANS] + list(range(R))
+    JOBS = [0] * 20
+    JOBS[0] = JOBS[1] = 2
+    for j in range(4):
+        JOBS[J1 + j // J1N] += 1
+        JOBS[J2 + j * J2S // 2] += 1
+    assert J2 >= J1 + 3 // J1N and J1 >= 1
+    XV = [X0 if r < XA else X1 if r < XB else X2 if r < XC else X3 for r in range(R)]
+    RP = [RN if r >= R1 else 0 for r in range(R)]
+    CAP = [CA if s < C1 else CB for s in range(20)]
+    HV = [HN if s >= H1 else 0 for s in range(20)]
+    HG = [GN if s >= G1 else 0 for s in range(20)]
+    LEAD = [LD0] + [LD] * 16
+    MID = [MD0] + [MD] * 16
+    DV = [D0] + [0] * 11
+    AHEAD = [AH] * R
+    CPOS = [99] * 17
+    FLAG = [FL] * 20
+    MB = [0] * 17
+    CENV = [0, 0, CV1, CV1]
+    jobs = [(j // G, j % G) for j in range(len(PARTS) * G)]
+    assert sum(JOBS) == len(jobs) and max(XV) <= 4 and max(DV) <= 1 and max(AHEAD) <= 2 and min(AHEAD) >= 1
+
+    def at(values, s):
+        return values[min(s, len(values) - 1)]
+
+    def first(s):
+        return sum(JOBS[:s])
 
     def passes(r, on_vector):
-        return [("W", r, g) for g in range(G) if r < R and ((r, g) in vector_w) == on_vector]
+        return [g for g in range(G) if (g in (3, 1, 2, 0)[: XV[r]]) == on_vector]
 
-    def both(kind, r):
-        return [(kind, r, 0), (kind, r, 1)]
-
-    def steps(text, part):
-        return [(word[0], part, int(word[1])) for word in text.split()]
-
-    scalar = passes(0, False)
-    for r in range(R):
-        following = passes(r + 1, False)
-        if r + 1 >= P_FROM:
-            copies = [("P",) + op[1:] for op in following]
-            following = following[:1] + [op for pair in zip(following[1:], copies) for op in pair] + copies[-1:]
-        lead = LEAD if r + 1 < P_FROM else LEAD_P
-        scalar += following[:lead] + both("B", r) + following[lead:] + (both("B", MEANS) if r == 0 else [])
-    banks = [[(0, 0)], [(MEANS, 0)], [(1, 0)], [(2, 0)], [(3, 0)]]
-    tensor = both("T", 0) + both("T", MEANS) + both("T", 1) + [("gain",)] + both("T", 2)
-    tensor += [("M", 0)] + both("T", 3) + [("M", 1), ("M", 2)] + both("T", 4) + [("M", 3), ("M", 4)]
-    vector = [("D", 0, 0), ("ws",)] + steps("D1 E0 D2 Q0 E1 D3 Q1 E2", 0) + [("C", 0)] + steps("Q2 E3", 0)
-    vector += [("D", 1, 0), ("Q", 0, 3), ("C", MEANS), ("D", 1, 1), ("E", 1, 0), ("C", 1)] + steps("E1 Q0 D2 Q1 D3", 1)
-    vector += [("C", 2), ("F", 1), ("E", 1, 2), ("F", 0), ("C", 3)] + steps("E3 Q2 Q3", 1) + [("F", 2), ("C", 4)]
-    pool, stores = [], []
-    done = [4, 0, 0]
-    emptied = 3
-    waiting = [0, 2]
-    for s in range(5, R + 1):
-        jobs = [(2, g) for g in range(G) if JOBS_C + g // 2 == s]
-        if s < R:
-            tensor += both("T", s)
-        vector += [("D",) + job for job in jobs if job not in D_S]
+    scalar, vector, tensor, pool, stores, banks = [], [], [], [], [], []
+    done = {r: 0 for r in tiles}
+    widened = emptied = 0
+    waiting, quantised = [], []
+    s = 0
+    while emptied < len(banks) or min(done.values()) < N:
+        assert s < 40
+        tile = tiles[s] if s < len(tiles) else None
+        upto = min(len(jobs), first(s + 1) + DLEAD)
+        ds = [("D",) + jobs[j] for j in range(widened, upto) if not DV[j]]
+        dv = [("D",) + jobs[j] for j in range(widened, upto) if DV[j]]
+        widened = upto
+        follow = [("W", s, g) for g in passes(s, False)] if s < R else []
+        copies = [("P",) + op[1:] for op in follow][len(follow) - min(len(follow), at(RP, s)) :]
+        for op in copies:
+            follow.insert(min(len(follow), follow.index(("W",) + op[1:]) + 2), op)
+        mixed = []
+        for j in range(max(len(ds), len(follow))):
+            mixed += (ds[j : j + 1] + follow[j : j + 1]) if s else []
+        if s == 0:
+            mixed = ds + follow
+        ready = sum(n for part, (c0, n) in enumerate(PARTS) if first(s) >= G * (part + 1))
         before = len(banks)
-        narrow = [1, 2] if s >= STEP_C else [1]
-        step = [[(MEANS, 1)]] if s == 5 else []
-        wide = [[(s - 1, 0)]]
-        if s > A_LAST:
-            step += wide
-        if s == STEP_C:
-            step += [[(done[1], 1), (done[1] + 1, 1)]] + wide + [[(MEANS, 2)]]
-            done[1] += 2
-            wide = []
-        for j in range((TAKE if s >= STEP_C else 2) - 1 - (s == STEP_C)):
-            pair = []
-            for i in range(2):
-                part = min(narrow, key=lambda q: done[q])
-                if done[part] < s:
-                    pair.append((done[part], part))
-                    done[part] += 1
-            if pair:
-                step.append(sorted(pair, key=lambda u: (u[1], u[0])))
-        if s <= A_LAST:
-            step += wide
-        if s == R:
-            step = step[:-1] + [[unit] for unit in step[-1]]
-        tensor += [("M", before + j) for j in range(len(step))]
-        banks += step
-        upto = max(before, len(banks) - ACCS) if s < R else before
-        for k in range(emptied, upto):
-            if banks[k][0][0] != MEANS:
-                vector.append(("F", k))
-                waiting.append(k)
-            elif banks[k][0][1] in CEN_S:
-                scalar.insert(scalar.index(("B", s - 1, 1)) + CEN_AT, ("F", k))
+        while len(banks) - before < at(CAP, s):
+            cand = [r for r in quantised if done[r] < ready]
+            if not cand:
+                break
+            r = min(cand, key=lambda q: (q != MEANS, done[q], q))
+            c0 = done[r]
+            n = [m for c, m in PARTS if c == c0][0]
+            if c0 % BANK == 0 and c0 + BANK <= ready:
+                units = [(r, c0, BANK)]
+            else:
+                units = [(r, c0, n)]
+                if r + 1 in cand and done[r + 1] == c0 and r + 1 != MEANS and n < BANK:
+                    units.append((r + 1, c0, n))
+            for q, c, m in units:
+                done[q] = c + m
+            banks.append(units)
+        products = [("M", k) for k in range(before, len(banks))]
+        turns = [("T", tile, 0), ("T", tile, 1)] if tile is not None else []
+        tensor += products[: at(MB, s)] + turns + products[at(MB, s) :]
+        if s == GAIN_AT:
+            tensor.append(("gain",))
+        last = min(done.values()) >= N and tile is None
+        upto = min(len(banks), max(before + at(FLAG, s), len(banks) - ACCS + 1))
+        centres = []
+        vector += dv[:1] if s == 0 else []
+        if s == 0:
+            vector.append(("ws",))
+        for k in range(emptied, max(emptied, upto)):
+            if banks[k][0][0] == MEANS and not CENV[banks[k][0][1] // 256]:
+                centres.append(("F", k))
             else:
                 vector.append(("F", k))
-        emptied = upto
-        for job in [(2, g) for g in range(G) if JOBS_C + g // 2 == s + 1 or (s == 5 and JOBS_C + g // 2 == s)]:
-            if job in D_S:
-                scalar.insert(scalar.index(("B", s - (JOBS_C + job[1] // 2 == s), 1)) + 1, ("D",) + job)
-        vector += [("E",) + job for job in jobs[:C_AT]] + ([("C", s)] if jobs else []) + [("E",) + job for job in jobs[C_AT:]]
-        quota = 0 if jobs else min(G_V, len(waiting) - KEEP)
-        if s >= R - 1:
-            quota = len(waiting) - (s == R or s < GP_TO)
-        vector += [("G", k) for k in waiting[:quota]]
-        stores += waiting[:quota]
-        waiting = waiting[quota:]
-        vector += [("Q",) + job for job in jobs] + passes(s + 2, True)
-        if not jobs and s < R:
-            vector.append(("C", s))
-        if s >= GP_FROM:
-            wide_round = len([units for units in step if units[0][0] != MEANS]) >= GP_TWO
-            for r in [s if s < R else None, None][: 2 if wide_round and s < R else 1]:
-                if waiting:
-                    pool.append(("G", waiting[0], r))
+            if banks[k][0][0] != MEANS:
+                waiting.append(k)
+        emptied = max(emptied, upto)
+        a, b = at(LEAD, s), at(LEAD, s) + at(MID, s)
+        exits = [[("B", tile, 0)], [("B", tile, 1)]] if tile is not None else [[], []]
+        scalar += centres + mixed[:a] + exits[0] + mixed[a:b] + exits[1] + mixed[b:]
+        take = sorted(waiting, key=lambda k: -len(banks[k]))[: min(at(HV, s), max(0, len(waiting) - KEEP))] if s > GAIN_AT else []
+        vector += [("H", k) for k in take]
+        stores += take
+        waiting = [k for k in waiting if k not in take]
+        mine = jobs[first(s) : first(s + 1)]
+        seq = dv[1:] if s == 0 else dv
+        for j, job in enumerate(mine):
+            seq.append(("E",) + job)
+            if j > 0:
+                seq.append(("Q",) + mine[j - 1])
+        wide = [("W", r, g) for r in range(R) if max(0, r + 1 - AHEAD[r]) == s for g in passes(r, True)]
+        seq += wide + ([("Q",) + mine[-1]] if mine else [])
+        if tile is not None:
+            seq.insert(at(CPOS, s), ("C", tile))
+            quantised.append(tile)
+        vector += seq
+        for j in range(at(HG, s) if s > GAIN_AT else 0):
+            plain = [k for k in waiting if len(banks[k]) == 1]
+            if plain and not last:
+                pool.append(("H", plain[0], ("C", tile) if j == 0 and tile is not None else None))
+                stores.append(plain[0])
+                waiting.remove(plain[0])
+        if last:
+            for k in range(emptied, len(banks)):
+                vector.append(("F", k))
+                waiting.append(k)
+                if len(waiting) > 1:
+                    vector.append(("H", waiting[0]))
                     stores.append(waiting.pop(0))
-    for k in range(emptied, len(banks)):
-        vector.append(("F", k))
-        if k > emptied:
-            vector.append(("G", k - 1))
-            stores.append(k - 1)
-    vector.append(("G", len(banks) - 1))
-    stores.append(len(banks) - 1)
-    assert not waiting and done == [4, R, R]
+            emptied = len(banks)
+            for k in waiting:
+                vector.append(("H", k))
+                stores.append(k)
+            waiting = []
+        s += 1
     return banks, tensor, scalar, vector, pool, [("St", k) for k in stores]
 
 
@@ -154,23 +196,36 @@ def tile_plate_centred_gene_scores_d2_kernel(tc, x_bytes, x_scale, w_bytes, w_sc
     nc = tc.nc
     with ExitStack() as ctx:
         keep = ctx.enter_context(tc.tile_pool(name="keep", bufs=1))
-        work = ctx.enter_context(tc.tile_pool(name="work", bufs=3))
-        outs = ctx.enter_context(tc.tile_pool(name="outs", bufs=4))
-        turn = ctx.enter_context(tc.psum_pool(name="turn", bufs=TURNS))
-        accs = ctx.enter_context(tc.psum_pool(name="accs", bufs=ACCS))
-        fixed = ctx.enter_context(tc.psum_pool(name="fixed", bufs=1))
+        psum = ctx.enter_context(tc.psum_pool(name="psum", bufs=1))
         ctx.enter_context(tc.manual_schedule())
+
+        def ring(pool, name, count, shape, dtype, align):
+            return [pool.tile(shape, dtype, name="%s%d" % (name, j), align_bytes=align) for j in range(count)]
 
         ident = keep.tile([P, P], F32, name="ident")
         make_identity(nc, ident[:])
         ident_b = keep.tile([P, P], BF16, name="ident_b")
         make_identity(nc, ident_b[:])
-        gain_p = fixed.tile([P, N], BF16, name="gain_p")
-        grouped = [keep.tile([P, K], BF16, name="xg%d" % j, align_bytes=64) for j in range(XG)]
+        gain_p = psum.tile([P, N], BF16, name="gain_p")
+        psum_banks, tensor, scalar, vector, pool, stores = orders()
+        rings = {
+            "xs": ring(keep, "xw", 6, [P, 512], BF16, 64),
+            "xv": ring(keep, "xv", 4, [P, 512], BF16, 64),
+            "xp": ring(keep, "xp", 4, [P, 512], BF16, 64),
+            "xg": ring(keep, "xg", XG, [P, K], BF16, 64),
+            "ww": ring(keep, "ww", 3, [P, 4 * PART], BF16, 64),
+            "wg": ring(keep, "wg", 2, [P, 4 * PART], BF16, 64),
+            "turn": [psum.tile([P, BANK], F32, name="turn%d" % j) for j in range(TURNS)],
+            "acc": [psum.tile([P, BANK], F32, name="acc%d" % j) for j in range(ACCS)],
+        }
+        x_codes = ring(keep, "xc", R + 1, [P, G * P], U32, 64)
+        x_exps = ring(keep, "xq", R + 1, [P, G * P], U8, 64)
+        w_codes = ring(keep, "wc", G, [P, N], U32, 64)
+        w_exps = ring(keep, "wq", G, [P, N], U8, 64)
+        diffs = {k: keep.tile([P, sum(n for r, c0, n in units)], F32, name="diff%d" % k) for k, units in enumerate(psum_banks) if units[0][0] != MEANS}
 
         x_rows = x_bytes.rearrange("(p r) k -> p r k", r=R)
         out_rows = out.rearrange("(p r) n -> p r n", r=R)
-
         xs_first = keep.tile([P, 2, C], F32, name="xs_first")
         xs_rest = keep.tile([P, R - 2, C], F32, name="xs_rest")
         x_scales = x_scale.rearrange("(p r) c -> p r c", r=R)
@@ -199,309 +254,249 @@ def tile_plate_centred_gene_scores_d2_kernel(tc, x_bytes, x_scale, w_bytes, w_sc
             t = keep.tile([P, rows * K], U8, name="xb%d" % r)
             nc.sync.dma_start(out=t[:], in_=x_rows[:, r : r + rows, :].rearrange("p r k -> p (r k)"))
             for j in range(rows):
-                for b in range(2):
-                    x_raw[r + j, b] = t[:, j * K + b * 1024 : j * K + (b + 1) * 1024]
-
-        def load_x_half(r, b):
-            t = keep.tile([P, 1024], U8, name="xh%d%d" % (r, b))
-            nc.sync.dma_start(out=t[:], in_=x_rows[:, r, 1024 * b : 1024 * b + 1024])
-            x_raw[r, b] = t[:]
+                x_raw[r + j] = t[:, j * K : (j + 1) * K]
 
         nc.scalar.dma_start(out=wsb[:], in_=w_scale.rearrange("c d -> (c d)").partition_broadcast(P))
         nc.scalar.dma_start(out=xs_first[:], in_=x_scales[:, :2, :])
         load_w(0, 0)
-        load_x_half(0, 0)
+        load_x(0, 1)
         load_w(0, 1)
-        load_x_half(0, 1)
-        load_x(1, 1)
-        load_w(0, 2)
         nc.sync.dma_start(out=mw[:], in_=means)
+        load_w(0, 2)
         load_w(0, 3)
+        load_x(1, 1)
         nc.sync.dma_start(out=xs_rest[:], in_=x_scales[:, 2:, :])
-        load_x(2, 2)
-        nc.sync.dma_start(out=gain_b[:], in_=gain.partition_broadcast(P))
         for g in range(G):
             load_w(1, g)
-        load_x(4, 2)
-        for g in range(G):
-            load_w(2, g)
-        for r in range(6, R, 2):
+        load_x(2, 2)
+        nc.sync.dma_start(out=gain_b[:], in_=gain.partition_broadcast(P))
+        for part in range(2, len(PARTS)):
+            for g in range(G):
+                load_w(part, g)
+            load_x(2 * part, 2)
+        for r in range(2 * len(PARTS), R, 2):
             load_x(r, 2)
 
-        def pick_w_scales():
-            for q in range(4):
-                nc.vector.tensor_copy(
-                    out=ws[32 * q : 32 * q + 32, :, :],
-                    in_=wsb[32 * q : 32 * q + 32, :].rearrange("p (g q d) -> p g q d", q=4, d=8)[:, :, q, :],
-                )
-
-        w_codes, w_scales, w_wide, w_grp = {}, {}, {}, {}
-
-        def widen_w(part, g, vector):
-            n = PARTS[part][1]
-            t = work.tile([P, 4 * BANK], BF16, name="ww", bufs=2)
-            src = w_raw[part, g][:].bitcast(F8)
-            if vector:
-                nc.vector.tensor_copy(out=t[:, : 4 * n], in_=src)
-            else:
-                nc.scalar.copy(out=t[:, : 4 * n], in_=src)
-            w_wide[part, g] = t
-
-        def scale_w(part, g):
-            c0, n = PARTS[part]
-            t = work.tile([P, 4 * BANK], BF16, name="wg", bufs=2, align_bytes=64)
-            src = w_wide[part, g][:, : 4 * n].rearrange("p (t c i) -> p c t i", t=4, i=4)
-            dst = t[:, : 4 * n].rearrange("p (c i t) -> p c t i", t=4, i=4)
-            for j in range(n // 128):
-                d = c0 // 128 + j
-                nc.vector.tensor_scalar(
-                    out=dst[:, 32 * j : 32 * j + 32, :, :],
-                    in0=src[:, 32 * j : 32 * j + 32, :, :],
-                    scalar1=ws[:, g, d : d + 1],
-                    scalar2=None,
-                    op0=ALU.mult,
-                )
-            w_grp[part, g] = t
-
-        def quant_w(part, g):
-            n = PARTS[part][1]
-            codes = keep.tile([P, n], U32, name="wc%d%d" % (part, g), align_bytes=64)
-            scales = keep.tile([P, n], U8, name="wq%d%d" % (part, g), align_bytes=64)
-            nc.vector.quantize_mx(out=codes[:].bitcast(X4), scales=scales[:], in_=w_grp[part, g][:, : 4 * n])
-            w_codes[part, g] = codes
-            w_scales[part, g] = scales
-
-        wide, grp, banks, codes_x, scales_x = {}, {}, {}, {}, {}
-
-        side_by_side = set()
-
-        def widen_x(r, g, vector):
-            t = work.tile([P, 512], BF16, name="xv" if vector else "xw", bufs=4 if vector else WIDE)
-            for q in range(4):
-                c = 4 * g + q
-                src = x_raw[r, c // 8][:, 128 * (c % 8) : 128 * (c % 8) + 128].bitcast(F8)
-                if vector:
-                    dst = t[:].rearrange("p (u s e) -> p s u e", u=2, e=2)[:, 32 * q : 32 * q + 32, :, :]
-                    nc.vector.tensor_scalar(
-                        out=dst,
-                        in0=src.rearrange("p (s u e) -> p s u e", u=2, e=2),
-                        scalar1=scale_of(r, c),
-                        scalar2=None,
-                        op0=ALU.mult,
-                    )
-                    side_by_side.add((r, g))
-                else:
-                    nc.scalar.activation(out=t[:, 128 * q : 128 * q + 128], in_=src, func=COPY, scale=scale_of(r, c))
-            wide[r, g] = t[:]
-
-        def reorder_x(r, g):
-            t = work.tile([P, 2, P], F32, name="xp", bufs=6)
-            nc.scalar.copy(out=t[:], in_=wide[r, g].bitcast(F32).rearrange("p (s u) -> p u s", u=2))
-            wide[r, g] = t[:].rearrange("p u s -> p (u s)").bitcast(BF16)
-            side_by_side.add((r, g))
-
-        for g in range(G):
-            wide[MEANS, g] = mw[:, 512 * g : 512 * g + 512]
-
-        def turn_x(r, b):
-            pt = turn.tile([P, 2, 2, P], F32, name="pt")
-            for j in range(2):
-                g = 2 * b + j
-                words = wide[r, g].bitcast(F32)
-                for u in range(2):
-                    src = words[:, P * u : P * u + P] if (r, g) in side_by_side else words[:, u : 2 * P : 2]
-                    nc.tensor.transpose(pt[:, j, u, :], src, ident[:])
-            banks[r, b] = pt
-
-        def exit_x(r, b, vector):
-            if r not in grp:
-                grp[r] = grouped[places[r] % XG]
-            dst = grp[r][:, 1024 * b : 1024 * b + 1024].bitcast(F32).rearrange("p (j s u) -> p j s u", j=2, u=2)
-            src = banks[r, b][:].rearrange("p j u s -> p j s u")
-            if vector:
-                nc.vector.tensor_copy(out=dst, in_=src)
-            else:
-                nc.scalar.copy(out=dst, in_=src)
-
-        def quant_x(r):
-            codes = work.tile([P, G * P], U32, name="xc", bufs=CODES, align_bytes=64)
-            scales = work.tile([P, G * P], U8, name="xq", bufs=CODES, align_bytes=64)
-            nc.vector.quantize_mx(out=codes[:].bitcast(X4), scales=scales[:], in_=grp[r][:])
-            codes_x[r] = codes
-            scales_x[r] = scales
-
-        def one_pass(acc, r, part, g):
-            rows = slice(P * g, P * g + P)
-            nc.tensor.matmul_mx(
-                out=acc,
-                lhsT=codes_x[r][:, rows].bitcast(X4),
-                lhsT_scale=scales_x[r][:, rows],
-                rhs=w_codes[part, g][:].bitcast(X4),
-                rhs_scale=w_scales[part, g][:],
-                start=(g == 0),
-                stop=(g == G - 1),
-            )
-
-        acc, diffs, results = {}, {}, {}
-
-        def multiply(k, passes):
-            if k not in acc:
-                acc[k] = accs.tile([P, BANK], F32, name="acc")
-            at = 0
-            for r, part in psum_banks[k]:
-                n = PARTS[part][1]
-                for g in passes:
-                    one_pass(acc[k][:, at : at + n], r, part, g)
-                at += n
-
-        def columns(tile, units):
-            c0, n = PARTS[units[0][1]]
-            if len(units) == 2 and units[0][1] == units[1][1]:
-                return tile[:, c0 : c0 + n].unsqueeze(1).to_broadcast([P, 2, n])
-            return tile[:, c0 : c0 + n * len(units)].rearrange("p (j n) -> p j n", n=n)
-
-        def shaped(tile, units):
-            n = PARTS[units[0][1]][1]
-            return tile[:, : n * len(units)].rearrange("p (j n) -> p j n", n=n)
-
-        def empty(k, vector):
-            units = psum_banks[k]
-            if units[0][0] == MEANS:
-                c0, n = PARTS[units[0][1]]
-                if vector:
-                    nc.vector.tensor_copy(out=cen[:, c0 : c0 + n], in_=acc[k][:, :n])
-                else:
-                    nc.scalar.copy(out=cen[:, c0 : c0 + n], in_=acc[k][:, :n])
-                return
-            t = outs.tile([P, BANK], F32, name="diff", bufs=33)
-            nc.vector.tensor_tensor(out=shaped(t, units), in0=shaped(acc[k], units), in1=columns(cen, units), op=ALU.subtract)
-            diffs[k] = t
-
-        def apply_gain(k, vector, room):
-            units = psum_banks[k]
-            t = diffs[k][:] if room is None else grp[room][:].bitcast(F32)[:, :BANK]
-            if vector:
-                nc.vector.tensor_tensor(out=shaped(t, units), in0=shaped(diffs[k], units), in1=columns(gain_p, units), op=ALU.mult)
-            else:
-                nc.gpsimd.tensor_tensor(out=shaped(t, units), in0=shaped(diffs[k], units), in1=columns(gain_b, units), op=ALU.mult)
-            results[k] = t
-
-        def store(k):
-            units, t = psum_banks[k], results[k]
-            r0, part0 = units[0]
-            c0, n = PARTS[part0]
-            if len(units) == 2 and units[1] == (r0, part0 + 1):
-                nc.sync.dma_start(out=out_rows[:, r0, c0 : c0 + 2 * n], in_=t)
-            elif len(units) == 2 and units[1] == (r0 + 1, part0):
-                nc.sync.dma_start(out=out_rows[:, r0 : r0 + 2, c0 : c0 + n], in_=shaped(t, units))
-            else:
-                for j, (r, part) in enumerate(units):
-                    c0 = PARTS[part][0]
-                    nc.sync.dma_start(out=out_rows[:, r, c0 : c0 + n], in_=t[:, j * n : (j + 1) * n])
-
-        def spread_gain():
-            for h in range(2):
-                cols = slice(BANK * h, BANK * h + BANK)
-                nc.tensor.matmul(out=gain_p[:, cols], lhsT=ident_b[:], rhs=gain_b[:, cols], start=True, stop=True)
-
-        psum_banks, tensor, scalar, vector, pool, stores = ORDER or default_order()
-        places = {r: j for j, r in enumerate([op[1] for op in tensor if op[0] == "T" and op[2] == 0])}
-        rooms = {op[2]: op[1] for op in pool if op[2] is not None}
-        means_bank = {units[0][1]: k for k, units in enumerate(psum_banks) if units[0][0] == MEANS}
-
-        def earlier(queue, op, kinds, back):
-            same = [o for o in queue if o[0] in kinds]
-            j = same.index(op) - back
-            return same[j] if j >= 0 else None
-
-        def needs(op, queue):
-            kind = op[0]
-            if kind == "W":
-                old = earlier(queue, op, ("W",), 4 if queue is vector else WIDE)
-                return [("P",) + old[1:] if ("P",) + old[1:] in scalar else ("T", old[1], old[2] // 2)] if old else []
-            if kind == "P":
-                old = earlier(queue, op, ("P",), 6)
-                return [("W",) + op[1:]] + ([("T", old[1], old[2] // 2)] if old else [])
-            if kind == "T":
-                old = earlier(queue, op, ("T",), TURNS)
-                widened = [("W", op[1], 2 * op[2] + j) for j in range(2)] if op[1] != MEANS else []
-                widened = [("P",) + need[1:] if ("P",) + need[1:] in scalar else need for need in widened]
-                return widened + ([("B",) + old[1:]] if old else [])
-            if kind == "B":
-                old = [r for r in places if places[r] == places[op[1]] - XG]
-                return [("T",) + op[1:]] + [("C", r) for r in old] + [("St", rooms[r]) for r in old if r in rooms]
-            if kind == "C":
-                old = earlier(queue, op, ("C",), CODES)
-                users = [("M", k) for k, units in enumerate(psum_banks) if old and old[1] in [r for r, part in units]]
-                return [("B", op[1], 0), ("B", op[1], 1)] + users
-            if kind == "D":
-                j = 4 * op[1] + op[2] - 2
-                return [("E", j // 4, j % 4)] if j >= 0 else []
-            if kind == "E":
-                j = 4 * op[1] + op[2] - 2
-                return [("D",) + op[1:], ("ws",)] + ([("Q", j // 4, j % 4)] if j >= 0 else [])
-            if kind == "Q":
-                return [("E",) + op[1:]]
-            if kind in ("M", "Ma", "Mb"):
-                last = G - 1 if kind == "Ma" else G
-                old = earlier(queue, op, ("M", "Ma"), ACCS) if kind != "Mb" else None
-                ready = [("C", r) for r, part in psum_banks[op[1]]] + [("Q", part, g) for r, part in psum_banks[op[1]] for g in range(last)]
-                return ready + ([("F", old[1])] if old else []) + ([("Ma", op[1])] if kind == "Mb" else [])
-            if kind == "F":
-                split = ("Mb", op[1]) in tensor
-                centres = [("F", means_bank[part]) for r, part in psum_banks[op[1]] if r != MEANS]
-                return [("Mb" if split else "M", op[1])] + centres
-            if kind == "G":
-                return [("F", op[1]), ("gain",)] + ([("C", op[2])] if len(op) > 2 and op[2] is not None else [])
-            if kind == "St":
-                return [("G", op[1])]
-            return []
-
-        def emit(op, queue):
-            kind, on_vector = op[0], queue is vector
-            if kind == "W":
-                widen_x(op[1], op[2], on_vector)
-            elif kind == "P":
-                reorder_x(op[1], op[2])
-            elif kind == "T":
-                turn_x(op[1], op[2])
-            elif kind == "B":
-                exit_x(op[1], op[2], on_vector)
-            elif kind == "C":
-                quant_x(op[1])
-            elif kind == "D":
-                widen_w(op[1], op[2], on_vector)
-            elif kind == "E":
-                scale_w(op[1], op[2])
-            elif kind == "Q":
-                quant_w(op[1], op[2])
-            elif kind == "M":
-                multiply(op[1], range(G))
-            elif kind == "Ma":
-                multiply(op[1], range(G - 1))
-            elif kind == "Mb":
-                multiply(op[1], [G - 1])
-            elif kind == "F":
-                empty(op[1], on_vector)
-            elif kind == "G":
-                apply_gain(op[1], on_vector, None if on_vector else op[2])
-            elif kind == "St":
-                store(op[1])
-            elif kind == "ws":
-                pick_w_scales()
-            else:
-                spread_gain()
+        def parts_of(c0, n):
+            return [part for part, (c, m) in enumerate(PARTS) if c < c0 + n and c0 < c + m]
 
         queues = [stores, pool, vector, scalar, tensor]
+        reordered = set(op[1:] for op in scalar if op[0] == "P")
+        on_vector = set(op[1:] for op in vector if op[0] == "W")
+        centre_bank = {}
+        for k, units in enumerate(psum_banks):
+            if units[0][0] == MEANS:
+                for part in parts_of(units[0][1], units[0][2]):
+                    centre_bank[part] = k
+
+        def turned(r, g):
+            return ("P" if (r, g) in reordered else "W", r, g)
+
+        def reads(op):
+            kind = op[0]
+            if kind == "P":
+                return [("W",) + op[1:]]
+            if kind == "T":
+                return [turned(op[1], 2 * op[2] + j) for j in range(2)] if op[1] != MEANS else []
+            if kind == "B":
+                return [("T",) + op[1:]]
+            if kind == "C":
+                return [("B", op[1], 0), ("B", op[1], 1)]
+            if kind == "E":
+                return [("D",) + op[1:], ("ws",)]
+            if kind == "Q":
+                return [("E",) + op[1:]]
+            if kind == "M":
+                units = psum_banks[op[1]]
+                return [("C", r) for r, c0, n in units] + [("Q", part, g) for r, c0, n in units for part in parts_of(c0, n) for g in range(G)]
+            if kind == "F":
+                units = psum_banks[op[1]]
+                return [("M", op[1])] + [("F", centre_bank[part]) for r, c0, n in units if r != MEANS for part in parts_of(c0, n)]
+            if kind == "H":
+                return [("F", op[1]), ("gain",)] + ([op[2]] if len(op) > 2 and op[2] is not None else [])
+            if kind == "St":
+                return [("H", op[1])]
+            return []
+
+        def name_of(op):
+            return op[:2] if op[0] == "H" else op
+
+        ring_of = {"P": "xp", "T": "turn", "D": "ww", "E": "wg", "M": "acc"}
+        place, previous = {}, {}
+        counts = {}
+        for queue in (scalar, vector, tensor):
+            for op in queue:
+                name = ring_of.get(op[0])
+                if op[0] == "W":
+                    name = "xv" if queue is vector else "xs"
+                if op[0] == "B" and op[2] == 0:
+                    name = "xg"
+                if op[0] == "D":
+                    continue
+                if name:
+                    counts.setdefault(name, []).append(op)
+        counts["ww"] = sorted([op for op in scalar + vector if op[0] == "D"])
+        for name, ops in counts.items():
+            size = len(rings[name])
+            for j, op in enumerate(ops):
+                place[op] = rings[name][j % size]
+                if j >= size:
+                    previous[op] = ops[j - size]
+        readers = {}
+        for queue in queues:
+            for op in queue:
+                for value in reads(op):
+                    readers.setdefault(value, []).append(name_of(op))
+        rooms = {op[2][1]: op[1] for op in pool if op[2] is not None}
+
+        def needs(op):
+            wanted = list(reads(op))
+            if op in previous:
+                old = previous[op]
+                wanted += readers.get(old, [])
+                if op[0] == "B" and old[1] in rooms:
+                    wanted.append(("St", rooms[old[1]]))
+            return wanted
+
+        def words_of(r, g):
+            if r == MEANS:
+                return mw[:, 512 * g : 512 * g + 512].bitcast(F32)
+            return place[turned(r, g)][:].bitcast(F32)
+
+        def columns(tile, units):
+            r, c0, n = units[0]
+            if len(units) == 2:
+                return tile[:, c0 : c0 + n].unsqueeze(1).to_broadcast([P, 2, n])
+            return tile[:, c0 : c0 + n]
+
+        def shaped(tile, units):
+            n = units[0][2]
+            if len(units) == 2:
+                return tile[:, : 2 * n].rearrange("p (j n) -> p j n", n=n)
+            return tile[:, :n]
+
+        results = {}
+
+        def emit(op, queue):
+            kind, vec = op[0], queue is vector
+            if kind == "W":
+                r, g = op[1:]
+                t = place[op]
+                for q in range(4):
+                    c = 4 * g + q
+                    src = x_raw[r][:, 128 * c : 128 * c + 128].bitcast(F8)
+                    if vec:
+                        dst = t[:].rearrange("p (u s e) -> p s u e", u=2, e=2)[:, 32 * q : 32 * q + 32, :, :]
+                        nc.vector.tensor_scalar(out=dst, in0=src.rearrange("p (s u e) -> p s u e", u=2, e=2), scalar1=scale_of(r, c), scalar2=None, op0=ALU.mult)
+                    else:
+                        nc.scalar.activation(out=t[:, 128 * q : 128 * q + 128], in_=src, func=COPY, scale=scale_of(r, c))
+            elif kind == "P":
+                nc.scalar.copy(
+                    out=place[op][:].bitcast(F32).rearrange("p (u s) -> p u s", u=2),
+                    in_=place[("W",) + op[1:]][:].bitcast(F32).rearrange("p (s u) -> p u s", u=2),
+                )
+            elif kind == "T":
+                r, b = op[1:]
+                for j in range(2):
+                    g = 2 * b + j
+                    words = words_of(r, g)
+                    for u in range(2):
+                        side = (r, g) in reordered or (r, g) in on_vector
+                        src = words[:, P * u : P * u + P] if side else words[:, u : 2 * P : 2]
+                        nc.tensor.transpose(place[op][:, P * (2 * j + u) : P * (2 * j + u + 1)], src, ident[:])
+            elif kind == "B":
+                r, b = op[1:]
+                dst = place[("B", r, 0)][:, 1024 * b : 1024 * b + 1024].bitcast(F32).rearrange("p (j s u) -> p j s u", j=2, u=2)
+                src = place[("T", r, b)][:].rearrange("p (j u s) -> p j s u", j=2, u=2)
+                if vec:
+                    nc.vector.tensor_copy(out=dst, in_=src)
+                else:
+                    nc.scalar.copy(out=dst, in_=src)
+            elif kind == "C":
+                r = op[1]
+                nc.vector.quantize_mx(out=x_codes[r][:].bitcast(X4), scales=x_exps[r][:], in_=place[("B", r, 0)][:])
+            elif kind == "D":
+                src = w_raw[op[1:]][:].bitcast(F8)
+                dst = place[op][:, : 4 * PARTS[op[1]][1]]
+                if vec:
+                    nc.vector.tensor_copy(out=dst, in_=src)
+                else:
+                    nc.scalar.copy(out=dst, in_=src)
+            elif kind == "E":
+                part, g = op[1:]
+                c0, n = PARTS[part]
+                src = place[("D", part, g)][:, : 4 * n].rearrange("p (t c i) -> p c t i", t=4, i=4)
+                dst = place[op][:, : 4 * n].rearrange("p (c i t) -> p c t i", t=4, i=4)
+                for j in range(n // 128):
+                    d = c0 // 128 + j
+                    nc.vector.tensor_scalar(out=dst[:, 32 * j : 32 * j + 32, :, :], in0=src[:, 32 * j : 32 * j + 32, :, :], scalar1=ws[:, g, d : d + 1], scalar2=None, op0=ALU.mult)
+            elif kind == "Q":
+                part, g = op[1:]
+                c0, n = PARTS[part]
+                cols = slice(c0, c0 + n)
+                nc.vector.quantize_mx(out=w_codes[g][:, cols].bitcast(X4), scales=w_exps[g][:, cols], in_=place[("E", part, g)][:, : 4 * n])
+            elif kind == "M":
+                at = 0
+                for r, c0, n in psum_banks[op[1]]:
+                    for g in range(G):
+                        rows = slice(P * g, P * g + P)
+                        nc.tensor.matmul_mx(
+                            out=place[op][:, at : at + n],
+                            lhsT=x_codes[r][:, rows].bitcast(X4),
+                            lhsT_scale=x_exps[r][:, rows],
+                            rhs=w_codes[g][:, c0 : c0 + n].bitcast(X4),
+                            rhs_scale=w_exps[g][:, c0 : c0 + n],
+                            start=(g == 0),
+                            stop=(g == G - 1),
+                        )
+                    at += n
+            elif kind == "F":
+                units = psum_banks[op[1]]
+                acc = place[("M", op[1])]
+                r, c0, n = units[0]
+                if r != MEANS:
+                    nc.vector.tensor_tensor(out=shaped(diffs[op[1]], units), in0=shaped(acc, units), in1=columns(cen, units), op=ALU.subtract)
+                elif vec:
+                    nc.vector.tensor_copy(out=cen[:, c0 : c0 + n], in_=acc[:, :n])
+                else:
+                    nc.scalar.copy(out=cen[:, c0 : c0 + n], in_=acc[:, :n])
+            elif kind == "H":
+                units = psum_banks[op[1]]
+                diff = diffs[op[1]]
+                if vec:
+                    results[op[1]] = diff[:]
+                    nc.vector.tensor_tensor(out=shaped(diff, units), in0=shaped(diff, units), in1=columns(gain_p, units), op=ALU.mult)
+                else:
+                    t = diff[:] if op[2] is None else place[("B", op[2][1], 0)][:].bitcast(F32)[:, :BANK]
+                    results[op[1]] = t
+                    nc.gpsimd.tensor_tensor(out=shaped(t, units), in0=shaped(diff, units), in1=columns(gain_b, units), op=ALU.mult)
+            elif kind == "St":
+                units = psum_banks[op[1]]
+                r, c0, n = units[0]
+                if len(units) == 2:
+                    nc.sync.dma_start(out=out_rows[:, r : r + 2, c0 : c0 + n], in_=shaped(results[op[1]], units))
+                else:
+                    nc.sync.dma_start(out=out_rows[:, r, c0 : c0 + n], in_=shaped(results[op[1]], units))
+            elif kind == "ws":
+                for q in range(4):
+                    nc.vector.tensor_copy(
+                        out=ws[32 * q : 32 * q + 32, :, :],
+                        in_=wsb[32 * q : 32 * q + 32, :].rearrange("p (g q d) -> p g q d", q=4, d=8)[:, :, q, :],
+                    )
+            else:
+                for h in range(2):
+                    cols = slice(BANK * h, BANK * h + BANK)
+                    nc.tensor.matmul(out=gain_p[:, cols], lhsT=ident_b[:], rhs=gain_b[:, cols], start=True, stop=True)
+
         at = [0] * len(queues)
         written = set()
         while any(at[j] < len(queue) for j, queue in enumerate(queues)):
             moved = False
             for j, queue in enumerate(queues):
-                if at[j] < len(queue) and all(need in written for need in needs(queue[at[j]], queue)):
+                if at[j] < len(queue) and all(need in written for need in needs(queue[at[j]])):
                     op = queue[at[j]]
                     emit(op, queue)
-                    written.add(op[:2] if op[0] == "G" else op)
+                    written.add(name_of(op))
                     at[j] += 1
                     moved = True
-            assert moved
+            assert moved, [queue[at[j]] for j, queue in enumerate(queues) if at[j] < len(queue)]

@@ -21,175 +21,20 @@ G = K // 512
 C = K // 128
 BANK = 512
 MEANS = R
-
-PART = 512
 PARTS = [(0, 512), (512, 256), (768, 256)]
-J1 = 2
-J1N = 3
-J2 = 4
-J2S = 3
-XA = 9
-X0 = 2
-X1 = 1
-X2 = 1
-X3 = 1
-XB = 9
-XC = 15
-R1 = 13
-RN = 2
-C1 = 0
-CA = 3
-CB = 3
-H1 = 10
-HN = 3
-G1 = 9
-GN = 2
-LD = 6
-MD = 1
-LD0 = 3
-MD0 = 0
-FL = 0
-DLEAD = 0
-D0 = 1
-AH = 1
-KEEP = 1
-GAIN_AT = 2
+
+THIRD_FROM = 2
+FOURTH_FROM = 6
+RATE3 = 1
+RATE4 = 2
+ONE_FROM = 9
+REORDER_FROM = 8
+HOLD = 1
+TG = 2
+GAIN_AT = 4
+TURNABLE = 10
 ACCS = 4
 TURNS = 3
-XG = 4
-CV1 = 0
-
-
-def orders():
-    tiles = [MEANS] + list(range(R))
-    JOBS = [0] * 20
-    JOBS[0] = JOBS[1] = 2
-    for j in range(4):
-        JOBS[J1 + j // J1N] += 1
-        JOBS[J2 + j * J2S // 2] += 1
-    assert J2 >= J1 + 3 // J1N and J1 >= 1
-    XV = [X0 if r < XA else X1 if r < XB else X2 if r < XC else X3 for r in range(R)]
-    RP = [RN if r >= R1 else 0 for r in range(R)]
-    CAP = [CA if s < C1 else CB for s in range(20)]
-    HV = [HN if s >= H1 else 0 for s in range(20)]
-    HG = [GN if s >= G1 else 0 for s in range(20)]
-    LEAD = [LD0] + [LD] * 16
-    MID = [MD0] + [MD] * 16
-    DV = [D0] + [0] * 11
-    AHEAD = [AH] * R
-    CPOS = [99] * 17
-    FLAG = [FL] * 20
-    MB = [0] * 17
-    CENV = [0, 0, CV1, CV1]
-    jobs = [(j // G, j % G) for j in range(len(PARTS) * G)]
-    assert sum(JOBS) == len(jobs) and max(XV) <= 4 and max(DV) <= 1 and max(AHEAD) <= 2 and min(AHEAD) >= 1
-
-    def at(values, s):
-        return values[min(s, len(values) - 1)]
-
-    def first(s):
-        return sum(JOBS[:s])
-
-    def passes(r, on_vector):
-        return [g for g in range(G) if (g in (3, 1, 2, 0)[: XV[r]]) == on_vector]
-
-    scalar, vector, tensor, pool, stores, banks = [], [], [], [], [], []
-    done = {r: 0 for r in tiles}
-    widened = emptied = 0
-    waiting, quantised = [], []
-    s = 0
-    while emptied < len(banks) or min(done.values()) < N:
-        assert s < 40
-        tile = tiles[s] if s < len(tiles) else None
-        upto = min(len(jobs), first(s + 1) + DLEAD)
-        ds = [("D",) + jobs[j] for j in range(widened, upto) if not DV[j]]
-        dv = [("D",) + jobs[j] for j in range(widened, upto) if DV[j]]
-        widened = upto
-        follow = [("W", s, g) for g in passes(s, False)] if s < R else []
-        copies = [("P",) + op[1:] for op in follow][len(follow) - min(len(follow), at(RP, s)) :]
-        for op in copies:
-            follow.insert(min(len(follow), follow.index(("W",) + op[1:]) + 2), op)
-        mixed = []
-        for j in range(max(len(ds), len(follow))):
-            mixed += (ds[j : j + 1] + follow[j : j + 1]) if s else []
-        if s == 0:
-            mixed = ds + follow
-        ready = sum(n for part, (c0, n) in enumerate(PARTS) if first(s) >= G * (part + 1))
-        before = len(banks)
-        while len(banks) - before < at(CAP, s):
-            cand = [r for r in quantised if done[r] < ready]
-            if not cand:
-                break
-            r = min(cand, key=lambda q: (q != MEANS, done[q], q))
-            c0 = done[r]
-            n = [m for c, m in PARTS if c == c0][0]
-            if c0 % BANK == 0 and c0 + BANK <= ready:
-                units = [(r, c0, BANK)]
-            else:
-                units = [(r, c0, n)]
-                if r + 1 in cand and done[r + 1] == c0 and r + 1 != MEANS and n < BANK:
-                    units.append((r + 1, c0, n))
-            for q, c, m in units:
-                done[q] = c + m
-            banks.append(units)
-        products = [("M", k) for k in range(before, len(banks))]
-        turns = [("T", tile, 0), ("T", tile, 1)] if tile is not None else []
-        tensor += products[: at(MB, s)] + turns + products[at(MB, s) :]
-        if s == GAIN_AT:
-            tensor.append(("gain",))
-        last = min(done.values()) >= N and tile is None
-        upto = min(len(banks), max(before + at(FLAG, s), len(banks) - ACCS + 1))
-        centres = []
-        vector += dv[:1] if s == 0 else []
-        if s == 0:
-            vector.append(("ws",))
-        for k in range(emptied, max(emptied, upto)):
-            if banks[k][0][0] == MEANS and not CENV[banks[k][0][1] // 256]:
-                centres.append(("F", k))
-            else:
-                vector.append(("F", k))
-            if banks[k][0][0] != MEANS:
-                waiting.append(k)
-        emptied = max(emptied, upto)
-        a, b = at(LEAD, s), at(LEAD, s) + at(MID, s)
-        exits = [[("B", tile, 0)], [("B", tile, 1)]] if tile is not None else [[], []]
-        scalar += centres + mixed[:a] + exits[0] + mixed[a:b] + exits[1] + mixed[b:]
-        take = sorted(waiting, key=lambda k: -len(banks[k]))[: min(at(HV, s), max(0, len(waiting) - KEEP))] if s > GAIN_AT else []
-        vector += [("H", k) for k in take]
-        stores += take
-        waiting = [k for k in waiting if k not in take]
-        mine = jobs[first(s) : first(s + 1)]
-        seq = dv[1:] if s == 0 else dv
-        for j, job in enumerate(mine):
-            seq.append(("E",) + job)
-            if j > 0:
-                seq.append(("Q",) + mine[j - 1])
-        wide = [("W", r, g) for r in range(R) if max(0, r + 1 - AHEAD[r]) == s for g in passes(r, True)]
-        seq += wide + ([("Q",) + mine[-1]] if mine else [])
-        if tile is not None:
-            seq.insert(at(CPOS, s), ("C", tile))
-            quantised.append(tile)
-        vector += seq
-        for j in range(at(HG, s) if s > GAIN_AT else 0):
-            plain = [k for k in waiting if len(banks[k]) == 1]
-            if plain and not last:
-                pool.append(("H", plain[0], ("C", tile) if j == 0 and tile is not None else None))
-                stores.append(plain[0])
-                waiting.remove(plain[0])
-        if last:
-            for k in range(emptied, len(banks)):
-                vector.append(("F", k))
-                waiting.append(k)
-                if len(waiting) > 1:
-                    vector.append(("H", waiting[0]))
-                    stores.append(waiting.pop(0))
-            emptied = len(banks)
-            for k in waiting:
-                vector.append(("H", k))
-                stores.append(k)
-            waiting = []
-        s += 1
-    return banks, tensor, scalar, vector, pool, [("St", k) for k in stores]
 
 
 def tile_plate_centred_gene_scores_d2_kernel(tc, x_bytes, x_scale, w_bytes, w_scale, means, gain, out):
@@ -199,46 +44,35 @@ def tile_plate_centred_gene_scores_d2_kernel(tc, x_bytes, x_scale, w_bytes, w_sc
         psum = ctx.enter_context(tc.psum_pool(name="psum", bufs=1))
         ctx.enter_context(tc.manual_schedule())
 
-        def ring(pool, name, count, shape, dtype, align):
-            return [pool.tile(shape, dtype, name="%s%d" % (name, j), align_bytes=align) for j in range(count)]
+        def tiles(pool, name, count, shape, dtype):
+            return [pool.tile(shape, dtype, name="%s%d" % (name, j), align_bytes=64) for j in range(count)]
 
         ident = keep.tile([P, P], F32, name="ident")
         make_identity(nc, ident[:])
         ident_b = keep.tile([P, P], BF16, name="ident_b")
         make_identity(nc, ident_b[:])
         gain_p = psum.tile([P, N], BF16, name="gain_p")
-        psum_banks, tensor, scalar, vector, pool, stores = orders()
-        rings = {
-            "xs": ring(keep, "xw", 6, [P, 512], BF16, 64),
-            "xv": ring(keep, "xv", 4, [P, 512], BF16, 64),
-            "xp": ring(keep, "xp", 4, [P, 512], BF16, 64),
-            "xg": ring(keep, "xg", XG, [P, K], BF16, 64),
-            "ww": ring(keep, "ww", 3, [P, 4 * PART], BF16, 64),
-            "wg": ring(keep, "wg", 2, [P, 4 * PART], BF16, 64),
-            "turn": [psum.tile([P, BANK], F32, name="turn%d" % j) for j in range(TURNS)],
-            "acc": [psum.tile([P, BANK], F32, name="acc%d" % j) for j in range(ACCS)],
-        }
-        x_codes = ring(keep, "xc", R + 1, [P, G * P], U32, 64)
-        x_exps = ring(keep, "xq", R + 1, [P, G * P], U8, 64)
-        w_codes = ring(keep, "wc", G, [P, N], U32, 64)
-        w_exps = ring(keep, "wq", G, [P, N], U8, 64)
-        diffs = {k: keep.tile([P, sum(n for r, c0, n in units)], F32, name="diff%d" % k) for k, units in enumerate(psum_banks) if units[0][0] != MEANS}
-
-        x_rows = x_bytes.rearrange("(p r) k -> p r k", r=R)
-        out_rows = out.rearrange("(p r) n -> p r n", r=R)
-        xs_first = keep.tile([P, 2, C], F32, name="xs_first")
-        xs_rest = keep.tile([P, R - 2, C], F32, name="xs_rest")
-        x_scales = x_scale.rearrange("(p r) c -> p r c", r=R)
-
-        def scale_of(r, c):
-            return xs_first[:, r, c : c + 1] if r < 2 else xs_rest[:, r - 2, c : c + 1]
-
+        turns = [psum.tile([P, BANK], F32, name="turn%d" % j) for j in range(TURNS)]
+        free_banks = [psum.tile([P, BANK], F32, name="acc%d" % j) for j in range(ACCS)]
+        turnable = tiles(keep, "xt", TURNABLE, [P, 512], BF16)
+        plain = tiles(keep, "xs", 4, [P, 512], BF16)
+        grouped = tiles(keep, "xg", R + 1, [P, K], BF16)
+        w_wide = tiles(keep, "ww", 3, [P, K], BF16)
+        w_grouped = tiles(keep, "wg", 2, [P, K], BF16)
+        x_codes = tiles(keep, "xc", R + 1, [P, G * P], U32)
+        x_exps = tiles(keep, "xq", R + 1, [P, G * P], U8)
+        w_codes = tiles(keep, "wc", G, [P, N], U32)
+        w_exps = tiles(keep, "wq", G, [P, N], U8)
+        xs_first = keep.tile([P, 2 * C], F32, name="xs_first")
+        xs_rest = keep.tile([P, (R - 2) * C], F32, name="xs_rest")
         wsb = keep.tile([P, C * 8], F32, name="wsb")
         ws = keep.tile([P, G, 8], F32, name="ws")
         gain_b = keep.tile([P, N], BF16, name="gain_b")
         mw = keep.tile([P, K], BF16, name="mw")
         cen = keep.tile([P, N], F32, name="cen")
 
+        x_rows = x_bytes.rearrange("(p r) k -> p r k", r=R)
+        out_rows = out.rearrange("(p r) n -> p r n", r=R)
         w_raw, x_raw = {}, {}
 
         def load_w(part, g):
@@ -256,247 +90,264 @@ def tile_plate_centred_gene_scores_d2_kernel(tc, x_bytes, x_scale, w_bytes, w_sc
             for j in range(rows):
                 x_raw[r + j] = t[:, j * K : (j + 1) * K]
 
+        x_scales = x_scale.rearrange("(p r) c -> p (r c)", r=R)
+
+        def scale_of(r, c):
+            return xs_first[:, C * r + c : C * r + c + 1] if r < 2 else xs_rest[:, C * (r - 2) + c : C * (r - 2) + c + 1]
+
+        nc.scalar.dma_start(out=xs_first[:], in_=x_scales[:, : 2 * C])
         nc.scalar.dma_start(out=wsb[:], in_=w_scale.rearrange("c d -> (c d)").partition_broadcast(P))
-        nc.scalar.dma_start(out=xs_first[:], in_=x_scales[:, :2, :])
-        load_w(0, 0)
         load_x(0, 1)
-        load_w(0, 1)
-        nc.sync.dma_start(out=mw[:], in_=means)
-        load_w(0, 2)
-        load_w(0, 3)
+        for g in range(G):
+            load_w(0, g)
         load_x(1, 1)
-        nc.sync.dma_start(out=xs_rest[:], in_=x_scales[:, 2:, :])
+        nc.sync.dma_start(out=mw[:], in_=means)
+        nc.sync.dma_start(out=xs_rest[:], in_=x_scales[:, 2 * C :])
+        load_x(2, 2)
         for g in range(G):
             load_w(1, g)
-        load_x(2, 2)
+        load_x(4, 2)
+        for g in range(G):
+            load_w(2, g)
         nc.sync.dma_start(out=gain_b[:], in_=gain.partition_broadcast(P))
-        for part in range(2, len(PARTS)):
-            for g in range(G):
-                load_w(part, g)
-            load_x(2 * part, 2)
-        for r in range(2 * len(PARTS), R, 2):
+        for r in range(6, R, 2):
             load_x(r, 2)
 
-        def parts_of(c0, n):
-            return [part for part, (c, m) in enumerate(PARTS) if c < c0 + n and c0 < c + m]
+        order = [0, MEANS] + list(range(1, R))
+        count = {"turnable": 0, "plain": 0, "turn": 0, "diff": 0, "wide": 0, "grouped": 0}
+        words, turned, widened, interleaved = {}, {}, {}, {}
 
-        queues = [stores, pool, vector, scalar, tensor]
-        reordered = set(op[1:] for op in scalar if op[0] == "P")
-        on_vector = set(op[1:] for op in vector if op[0] == "W")
-        centre_bank = {}
-        for k, units in enumerate(psum_banks):
-            if units[0][0] == MEANS:
-                for part in parts_of(units[0][1], units[0][2]):
-                    centre_bank[part] = k
+        def take(name, ring):
+            count[name] += 1
+            return ring[(count[name] - 1) % len(ring)]
 
-        def turned(r, g):
-            return ("P" if (r, g) in reordered else "W", r, g)
+        def vector_share(r):
+            return G if r == 0 else 0 if r == 1 else 1 if r >= ONE_FROM and r % 2 else 2
 
-        def reads(op):
-            kind = op[0]
-            if kind == "P":
-                return [("W",) + op[1:]]
-            if kind == "T":
-                return [turned(op[1], 2 * op[2] + j) for j in range(2)] if op[1] != MEANS else []
-            if kind == "B":
-                return [("T",) + op[1:]]
-            if kind == "C":
-                return [("B", op[1], 0), ("B", op[1], 1)]
-            if kind == "E":
-                return [("D",) + op[1:], ("ws",)]
-            if kind == "Q":
-                return [("E",) + op[1:]]
-            if kind == "M":
-                units = psum_banks[op[1]]
-                return [("C", r) for r, c0, n in units] + [("Q", part, g) for r, c0, n in units for part in parts_of(c0, n) for g in range(G)]
-            if kind == "F":
-                units = psum_banks[op[1]]
-                return [("M", op[1])] + [("F", centre_bank[part]) for r, c0, n in units if r != MEANS for part in parts_of(c0, n)]
-            if kind == "H":
-                return [("F", op[1]), ("gain",)] + ([op[2]] if len(op) > 2 and op[2] is not None else [])
-            if kind == "St":
-                return [("H", op[1])]
-            return []
-
-        def name_of(op):
-            return op[:2] if op[0] == "H" else op
-
-        ring_of = {"P": "xp", "T": "turn", "D": "ww", "E": "wg", "M": "acc"}
-        place, previous = {}, {}
-        counts = {}
-        for queue in (scalar, vector, tensor):
-            for op in queue:
-                name = ring_of.get(op[0])
-                if op[0] == "W":
-                    name = "xv" if queue is vector else "xs"
-                if op[0] == "B" and op[2] == 0:
-                    name = "xg"
-                if op[0] == "D":
-                    continue
-                if name:
-                    counts.setdefault(name, []).append(op)
-        counts["ww"] = sorted([op for op in scalar + vector if op[0] == "D"])
-        for name, ops in counts.items():
-            size = len(rings[name])
-            for j, op in enumerate(ops):
-                place[op] = rings[name][j % size]
-                if j >= size:
-                    previous[op] = ops[j - size]
-        readers = {}
-        for queue in queues:
-            for op in queue:
-                for value in reads(op):
-                    readers.setdefault(value, []).append(name_of(op))
-        rooms = {op[2][1]: op[1] for op in pool if op[2] is not None}
-
-        def needs(op):
-            wanted = list(reads(op))
-            if op in previous:
-                old = previous[op]
-                wanted += readers.get(old, [])
-                if op[0] == "B" and old[1] in rooms:
-                    wanted.append(("St", rooms[old[1]]))
-            return wanted
-
-        def words_of(r, g):
-            if r == MEANS:
-                return mw[:, 512 * g : 512 * g + 512].bitcast(F32)
-            return place[turned(r, g)][:].bitcast(F32)
-
-        def columns(tile, units):
-            r, c0, n = units[0]
-            if len(units) == 2:
-                return tile[:, c0 : c0 + n].unsqueeze(1).to_broadcast([P, 2, n])
-            return tile[:, c0 : c0 + n]
-
-        def shaped(tile, units):
-            n = units[0][2]
-            if len(units) == 2:
-                return tile[:, : 2 * n].rearrange("p (j n) -> p j n", n=n)
-            return tile[:, :n]
-
-        results = {}
-
-        def emit(op, queue):
-            kind, vec = op[0], queue is vector
-            if kind == "W":
-                r, g = op[1:]
-                t = place[op]
+        def widen_x_vector(r):
+            for g in range(G - vector_share(r), G):
+                t = take("turnable", turnable)
+                dst = t[:].rearrange("p (u s e) -> p s u e", u=2, e=2)
                 for q in range(4):
                     c = 4 * g + q
-                    src = x_raw[r][:, 128 * c : 128 * c + 128].bitcast(F8)
-                    if vec:
-                        dst = t[:].rearrange("p (u s e) -> p s u e", u=2, e=2)[:, 32 * q : 32 * q + 32, :, :]
-                        nc.vector.tensor_scalar(out=dst, in0=src.rearrange("p (s u e) -> p s u e", u=2, e=2), scalar1=scale_of(r, c), scalar2=None, op0=ALU.mult)
-                    else:
-                        nc.scalar.activation(out=t[:, 128 * q : 128 * q + 128], in_=src, func=COPY, scale=scale_of(r, c))
-            elif kind == "P":
-                nc.scalar.copy(
-                    out=place[op][:].bitcast(F32).rearrange("p (u s) -> p u s", u=2),
-                    in_=place[("W",) + op[1:]][:].bitcast(F32).rearrange("p (s u) -> p u s", u=2),
-                )
-            elif kind == "T":
-                r, b = op[1:]
-                for j in range(2):
-                    g = 2 * b + j
-                    words = words_of(r, g)
-                    for u in range(2):
-                        side = (r, g) in reordered or (r, g) in on_vector
-                        src = words[:, P * u : P * u + P] if side else words[:, u : 2 * P : 2]
-                        nc.tensor.transpose(place[op][:, P * (2 * j + u) : P * (2 * j + u + 1)], src, ident[:])
-            elif kind == "B":
-                r, b = op[1:]
-                dst = place[("B", r, 0)][:, 1024 * b : 1024 * b + 1024].bitcast(F32).rearrange("p (j s u) -> p j s u", j=2, u=2)
-                src = place[("T", r, b)][:].rearrange("p (j u s) -> p j s u", j=2, u=2)
-                if vec:
-                    nc.vector.tensor_copy(out=dst, in_=src)
-                else:
-                    nc.scalar.copy(out=dst, in_=src)
-            elif kind == "C":
-                r = op[1]
-                nc.vector.quantize_mx(out=x_codes[r][:].bitcast(X4), scales=x_exps[r][:], in_=place[("B", r, 0)][:])
-            elif kind == "D":
-                src = w_raw[op[1:]][:].bitcast(F8)
-                dst = place[op][:, : 4 * PARTS[op[1]][1]]
-                if vec:
-                    nc.vector.tensor_copy(out=dst, in_=src)
-                else:
-                    nc.scalar.copy(out=dst, in_=src)
-            elif kind == "E":
-                part, g = op[1:]
-                c0, n = PARTS[part]
-                src = place[("D", part, g)][:, : 4 * n].rearrange("p (t c i) -> p c t i", t=4, i=4)
-                dst = place[op][:, : 4 * n].rearrange("p (c i t) -> p c t i", t=4, i=4)
-                for j in range(n // 128):
-                    d = c0 // 128 + j
-                    nc.vector.tensor_scalar(out=dst[:, 32 * j : 32 * j + 32, :, :], in0=src[:, 32 * j : 32 * j + 32, :, :], scalar1=ws[:, g, d : d + 1], scalar2=None, op0=ALU.mult)
-            elif kind == "Q":
-                part, g = op[1:]
-                c0, n = PARTS[part]
-                cols = slice(c0, c0 + n)
-                nc.vector.quantize_mx(out=w_codes[g][:, cols].bitcast(X4), scales=w_exps[g][:, cols], in_=place[("E", part, g)][:, : 4 * n])
-            elif kind == "M":
-                at = 0
-                for r, c0, n in psum_banks[op[1]]:
-                    for g in range(G):
-                        rows = slice(P * g, P * g + P)
-                        nc.tensor.matmul_mx(
-                            out=place[op][:, at : at + n],
-                            lhsT=x_codes[r][:, rows].bitcast(X4),
-                            lhsT_scale=x_exps[r][:, rows],
-                            rhs=w_codes[g][:, c0 : c0 + n].bitcast(X4),
-                            rhs_scale=w_exps[g][:, c0 : c0 + n],
-                            start=(g == 0),
-                            stop=(g == G - 1),
-                        )
-                    at += n
-            elif kind == "F":
-                units = psum_banks[op[1]]
-                acc = place[("M", op[1])]
-                r, c0, n = units[0]
-                if r != MEANS:
-                    nc.vector.tensor_tensor(out=shaped(diffs[op[1]], units), in0=shaped(acc, units), in1=columns(cen, units), op=ALU.subtract)
-                elif vec:
-                    nc.vector.tensor_copy(out=cen[:, c0 : c0 + n], in_=acc[:, :n])
-                else:
-                    nc.scalar.copy(out=cen[:, c0 : c0 + n], in_=acc[:, :n])
-            elif kind == "H":
-                units = psum_banks[op[1]]
-                diff = diffs[op[1]]
-                if vec:
-                    results[op[1]] = diff[:]
-                    nc.vector.tensor_tensor(out=shaped(diff, units), in0=shaped(diff, units), in1=columns(gain_p, units), op=ALU.mult)
-                else:
-                    t = diff[:] if op[2] is None else place[("B", op[2][1], 0)][:].bitcast(F32)[:, :BANK]
-                    results[op[1]] = t
-                    nc.gpsimd.tensor_tensor(out=shaped(t, units), in0=shaped(diff, units), in1=columns(gain_b, units), op=ALU.mult)
-            elif kind == "St":
-                units = psum_banks[op[1]]
-                r, c0, n = units[0]
-                if len(units) == 2:
-                    nc.sync.dma_start(out=out_rows[:, r : r + 2, c0 : c0 + n], in_=shaped(results[op[1]], units))
-                else:
-                    nc.sync.dma_start(out=out_rows[:, r, c0 : c0 + n], in_=shaped(results[op[1]], units))
-            elif kind == "ws":
+                    src = x_raw[r][:, 128 * c : 128 * c + 128].bitcast(F8).rearrange("p (s u e) -> p s u e", u=2, e=2)
+                    nc.vector.tensor_scalar(out=dst[:, 32 * q : 32 * q + 32, :, :], in0=src, scalar1=scale_of(r, c), scalar2=None, op0=ALU.mult)
+                words[r, g] = [t[:].bitcast(F32)[:, P * u : P * u + P] for u in range(2)]
+
+        def widen_x_scalar(r):
+            mine = range(G - vector_share(r))
+            again = mine if r >= REORDER_FROM else []
+            wide = {}
+            for g in mine:
+                t = wide[g] = take("plain", plain) if g in again else take("turnable", turnable)
                 for q in range(4):
-                    nc.vector.tensor_copy(
-                        out=ws[32 * q : 32 * q + 32, :, :],
-                        in_=wsb[32 * q : 32 * q + 32, :].rearrange("p (g q d) -> p g q d", q=4, d=8)[:, :, q, :],
+                    c = 4 * g + q
+                    nc.scalar.activation(out=t[:, 128 * q : 128 * q + 128], in_=x_raw[r][:, 128 * c : 128 * c + 128].bitcast(F8), func=COPY, scale=scale_of(r, c))
+                words[r, g] = [t[:].bitcast(F32)[:, u : 2 * P : 2] for u in range(2)]
+            for g in again:
+                t = take("turnable", turnable)
+                nc.scalar.copy(out=t[:].bitcast(F32).rearrange("p (u s) -> p u s", u=2), in_=wide[g][:].bitcast(F32).rearrange("p (s u) -> p u s", u=2))
+                words[r, g] = [t[:].bitcast(F32)[:, P * u : P * u + P] for u in range(2)]
+
+        for g in range(G):
+            words[MEANS, g] = [mw[:, 512 * g : 512 * g + 512].bitcast(F32)[:, u : 2 * P : 2] for u in range(2)]
+
+        def turn(r):
+            for b in range(2):
+                bank = turned[r, b] = take("turn", turns)
+                for j in range(4):
+                    nc.tensor.transpose(bank[:, P * j : P * j + P], words[r, 2 * b + j // 2][j % 2], ident[:])
+
+        def collect(r, centres=()):
+            for b in (1, 0):
+                for unit, acc in centres if b == 0 else ():
+                    copy_centre(unit, acc)
+                nc.scalar.copy(
+                    out=grouped[r][:, 1024 * b : 1024 * b + 1024].bitcast(F32).rearrange("p (j s u) -> p j s u", j=2, u=2),
+                    in_=turned[r, b][:].rearrange("p (j u s) -> p j s u", j=2, u=2),
+                )
+
+        def quantise_x(r):
+            nc.vector.quantize_mx(out=x_codes[r][:].bitcast(X4), scales=x_exps[r][:], in_=grouped[r][:])
+
+        def widen_w(part, g):
+            t = widened[part, g] = take("wide", w_wide)[:, : 4 * PARTS[part][1]]
+            nc.scalar.copy(out=t, in_=w_raw[part, g][:].bitcast(F8))
+
+        def interleave_w(part, g):
+            c0, n = PARTS[part]
+            t = interleaved[part, g] = take("grouped", w_grouped)[:, : 4 * n]
+            src = widened[part, g].rearrange("p (t c i) -> p c t i", t=4, i=4)
+            dst = t.rearrange("p (c i t) -> p c t i", t=4, i=4)
+            for j in range(n // 128):
+                d = c0 // 128 + j
+                nc.vector.tensor_scalar(out=dst[:, 32 * j : 32 * j + 32, :, :], in0=src[:, 32 * j : 32 * j + 32, :, :], scalar1=ws[:, g, d : d + 1], scalar2=None, op0=ALU.mult)
+
+        def quantise_w(part, g):
+            c0, n = PARTS[part]
+            nc.vector.quantize_mx(out=w_codes[g][:, c0 : c0 + n].bitcast(X4), scales=w_exps[g][:, c0 : c0 + n], in_=interleaved[part, g])
+
+        def multiply(unit):
+            rows, c0, n = unit
+            acc = free_banks.pop(0)
+            for j, r in enumerate(rows):
+                for g in range(G):
+                    nc.tensor.matmul_mx(
+                        out=acc[:, n * j : n * j + n],
+                        lhsT=x_codes[r][:, P * g : P * g + P].bitcast(X4),
+                        lhsT_scale=x_exps[r][:, P * g : P * g + P],
+                        rhs=w_codes[g][:, c0 : c0 + n].bitcast(X4),
+                        rhs_scale=w_exps[g][:, c0 : c0 + n],
+                        start=(g == 0),
+                        stop=(g == G - 1),
                     )
-            else:
+            return acc
+
+        def shaped(ap, unit):
+            rows, c0, n = unit
+            return ap[:, : n * len(rows)].rearrange("p (j n) -> p j n", n=n) if len(rows) > 1 else ap[:, :n]
+
+        def columns(tile, unit):
+            rows, c0, n = unit
+            return tile[:, c0 : c0 + n].unsqueeze(1).to_broadcast([P, len(rows), n]) if len(rows) > 1 else tile[:, c0 : c0 + n]
+
+        spare, later = [], [grouped[0][:].bitcast(F32)[:, BANK * h : BANK * h + BANK] for h in range(2)]
+
+        def subtract(unit, acc):
+            if not spare:
+                count["diff"] += 1
+                spare.append(keep.tile([P, BANK], F32, name="diff%d" % count["diff"])[:])
+            diff = spare.pop(0)
+            nc.vector.tensor_tensor(out=shaped(diff, unit), in0=shaped(acc, unit), in1=columns(cen, unit), op=ALU.subtract)
+            free_banks.append(acc)
+            return diff
+
+        def store(unit, result):
+            rows, c0, n = unit
+            dst = out_rows[:, rows[0] : rows[0] + len(rows), c0 : c0 + n] if len(rows) > 1 else out_rows[:, rows[0], c0 : c0 + n]
+            nc.sync.dma_start(out=dst, in_=shaped(result, unit))
+
+        def gain_vector(unit, diff):
+            nc.vector.tensor_tensor(out=shaped(diff, unit), in0=shaped(diff, unit), in1=columns(gain_p, unit), op=ALU.mult)
+            store(unit, diff)
+
+        def gain_pool(unit, diff, room):
+            nc.gpsimd.tensor_tensor(out=shaped(room, unit), in0=shaped(diff, unit), in1=columns(gain_b, unit), op=ALU.mult)
+
+        def copy_centre(unit, acc):
+            nc.scalar.copy(out=cen[:, unit[1] : unit[1] + unit[2]], in_=acc[:, : unit[2]])
+            free_banks.append(acc)
+
+        narrow = {}
+        for part, first, rate in ((1, THIRD_FROM, RATE3), (2, FOURTH_FROM, RATE4)):
+            for g in range(G):
+                narrow.setdefault(first + g // rate, []).append((part, g))
+        third_ready = THIRD_FROM + (G - 1) // RATE3 + 1
+        fourth_ready = FOURTH_FROM + (G - 1) // RATE4 + 1
+        paired = (third_ready - 2) // 2 * 2
+
+        widen_x_vector(0)
+        for q in range(4):
+            rows = slice(32 * q, 32 * q + 32)
+            nc.vector.tensor_copy(out=ws[rows, :, :], in_=wsb[rows, :].rearrange("p (g q d) -> p g q d", q=4, d=8)[:, :, q, :])
+        turn(0)
+        for g in range(3):
+            widen_w(0, g)
+        interleave_w(0, 0)
+        widen_w(0, 3)
+        collect(0)
+        turn(MEANS)
+        widen_x_scalar(1)
+        collect(MEANS)
+        for g in range(1, G):
+            interleave_w(0, g)
+            quantise_w(0, g - 1)
+        quantise_x(0)
+        quantise_w(0, G - 1)
+        quantise_x(MEANS)
+        for job in narrow.get(2, []):
+            widen_w(*job)
+        widen_x_scalar(2)
+
+        due = [((MEANS,), 0, BANK), ((0,), 0, BANK)]
+        full, waiting, given = [], [], 0
+        for i in range(2, R + 1):
+            tile = order[i]
+            if i == third_ready:
+                due = due + [((MEANS,), 512, 256)] + [((r, r + 1), 512, 256) for r in range(0, paired, 2)]
+            if i == fourth_ready:
+                due = due + [((MEANS,), 768, 256)] + [((r, r + 1), 768, 256) for r in range(0, paired, 2)] + [((r,), BANK, BANK) for r in range(paired, i - 2)]
+            if i > 2:
+                due = due + [((i - 2,), c0, BANK) for c0 in range(0, N if i >= fourth_ready else BANK, BANK)]
+            if i == third_ready:
+                left = len(due) + 1 + paired // 2 + (R - 1 - paired) + (R - i) - HOLD
+            k, rounds = i - third_ready, R + 1 - third_ready
+            cap = i - 1 if k < 0 else -(-left * (k + 1) // rounds) - given
+            turn(tile)
+            new = [unit[1] for unit, acc in full if unit[0][0] == MEANS]
+            held = [(unit, acc) for unit, acc in full if unit[0][0] != MEANS and unit[1] in new]
+            for unit, acc in reversed(full):
+                if unit[0][0] != MEANS and unit[1] not in new:
+                    waiting.append((unit, subtract(unit, acc)))
+            collect(tile, [(unit, acc) for unit, acc in full if unit[0][0] == MEANS])
+            cap = min(cap, len(free_banks), len(due))
+            now, due = due[:cap], due[cap:]
+            given += cap if k >= 0 else 0
+            full = [(unit, multiply(unit)) for unit in now]
+            if i == GAIN_AT:
                 for h in range(2):
                     cols = slice(BANK * h, BANK * h + BANK)
                     nc.tensor.matmul(out=gain_p[:, cols], lhsT=ident_b[:], rhs=gain_b[:, cols], start=True, stop=True)
+            jobs = narrow.get(i, [])
+            for job in jobs:
+                interleave_w(*job)
+            if i < R:
+                widen_x_vector(i)
+            for job in reversed(jobs):
+                quantise_w(*job)
+            quantise_x(tile)
+            for unit, acc in held:
+                waiting.append((unit, subtract(unit, acc)))
+            for job in narrow.get(i + 1, []):
+                widen_w(*job)
+            if i + 1 < R:
+                widen_x_scalar(i + 1)
+            mine = len(full) - 1 if i >= fourth_ready else 0
+            stretch = mine + len(held) + len([unit for unit, acc in full if unit[0][0] != MEANS])
+            theirs = [w for w in waiting if w[0][2] == BANK][: 2 * stretch // 5 if i > third_ready else 0]
+            halves = [grouped[tile][:].bitcast(F32)[:, BANK * h : BANK * h + BANK] for h in range(2)]
+            rooms = [halves[0]] + [diff for unit, diff in theirs[1:]]
+            for (unit, diff), room in zip(theirs, rooms):
+                gain_pool(unit, diff, room)
+            waiting = [w for w in waiting if w not in theirs]
+            pairs_first = sorted(waiting, key=lambda w: w[0][2])[:mine]
+            for unit, diff in pairs_first:
+                gain_vector(unit, diff)
+            waiting = [w for w in waiting if w not in pairs_first]
+            for (unit, diff), room in zip(theirs, rooms):
+                store(unit, room)
+            spare.extend(later)
+            later = halves[1:] if theirs else halves
+            if i == fourth_ready:
+                later = later + [t[:].bitcast(F32)[:, BANK * h : BANK * h + BANK] for t in [mw] + w_wide + w_grouped for h in range(2)]
 
-        at = [0] * len(queues)
-        written = set()
-        while any(at[j] < len(queue) for j, queue in enumerate(queues)):
-            moved = False
-            for j, queue in enumerate(queues):
-                if at[j] < len(queue) and all(need in written for need in needs(queue[at[j]])):
-                    op = queue[at[j]]
-                    emit(op, queue)
-                    written.add(name_of(op))
-                    at[j] += 1
-                    moved = True
-            assert moved, [queue[at[j]] for j, queue in enumerate(queues) if at[j] < len(queue)]
+        free_banks.extend(turns)
+        due = due + [((R - 1,), 0, BANK), ((R - 1,), 512, 256), ((R - 1,), 768, 256)]
+        pool_turn = True
+        while full or due:
+            if due and free_banks:
+                unit = due.pop(0)
+                full.append((unit, multiply(unit)))
+                continue
+            unit, acc = full.pop(0)
+            diff = subtract(unit, acc)
+            if waiting:
+                gain_vector(*waiting.pop(0))
+            if pool_turn and len(full) + len(due) >= TG:
+                gain_pool(unit, diff, diff)
+                store(unit, diff)
+            else:
+                waiting.append((unit, diff))
+            pool_turn = not pool_turn
+        for unit, diff in waiting:
+            gain_vector(unit, diff)

@@ -27,7 +27,7 @@ THIRD_FROM = 2
 FOURTH_FROM = 6
 RATE3 = 1
 RATE4 = 2
-ONE_FROM = 9
+ONE_FROM = 11
 REORDER_FROM = 8
 HOLD = 1
 TG = 2
@@ -65,7 +65,7 @@ def tile_plate_centred_gene_scores_d2_kernel(tc, x_bytes, x_scale, w_bytes, w_sc
         w_exps = tiles(keep, "wq", G, [P, N], U8)
         xs_first = keep.tile([P, 2 * C], F32, name="xs_first")
         xs_rest = keep.tile([P, (R - 2) * C], F32, name="xs_rest")
-        wsb = keep.tile([P, C * 8], F32, name="wsb")
+        ws_col = keep.tile([P, 1], F32, name="ws_col")
         ws = keep.tile([P, G, 8], F32, name="ws")
         gain_b = keep.tile([P, N], BF16, name="gain_b")
         mw = keep.tile([P, K], BF16, name="mw")
@@ -96,7 +96,7 @@ def tile_plate_centred_gene_scores_d2_kernel(tc, x_bytes, x_scale, w_bytes, w_sc
             return xs_first[:, C * r + c : C * r + c + 1] if r < 2 else xs_rest[:, C * (r - 2) + c : C * (r - 2) + c + 1]
 
         nc.scalar.dma_start(out=xs_first[:], in_=x_scales[:, : 2 * C])
-        nc.scalar.dma_start(out=wsb[:], in_=w_scale.rearrange("c d -> (c d)").partition_broadcast(P))
+        nc.scalar.dma_start(out=ws_col[:], in_=w_scale.rearrange("c (d o) -> (c d) o", o=1))
         load_x(0, 1)
         for g in range(G):
             load_w(0, g)
@@ -109,8 +109,10 @@ def tile_plate_centred_gene_scores_d2_kernel(tc, x_bytes, x_scale, w_bytes, w_sc
         load_x(4, 2)
         for g in range(G):
             load_w(2, g)
+        load_x(6, 2)
+        load_x(8, 2)
         nc.sync.dma_start(out=gain_b[:], in_=gain.partition_broadcast(P))
-        for r in range(6, R, 2):
+        for r in range(10, R, 2):
             load_x(r, 2)
 
         order = [0, MEANS] + list(range(1, R))
@@ -122,7 +124,7 @@ def tile_plate_centred_gene_scores_d2_kernel(tc, x_bytes, x_scale, w_bytes, w_sc
             return ring[(count[name] - 1) % len(ring)]
 
         def vector_share(r):
-            return G if r == 0 else 0 if r == 1 else 1 if r >= ONE_FROM and r % 2 else 2
+            return G if r == 0 else 1 if r >= ONE_FROM and r % 2 else 2
 
         def widen_x_vector(r):
             for g in range(G - vector_share(r), G):
@@ -187,11 +189,11 @@ def tile_plate_centred_gene_scores_d2_kernel(tc, x_bytes, x_scale, w_bytes, w_sc
             c0, n = PARTS[part]
             nc.vector.quantize_mx(out=w_codes[g][:, c0 : c0 + n].bitcast(X4), scales=w_exps[g][:, c0 : c0 + n], in_=interleaved[part, g])
 
-        def multiply(unit):
+        def multiply(unit, acc=None, passes=range(G)):
             rows, c0, n = unit
-            acc = free_banks.pop(0)
+            acc = free_banks.pop(0) if acc is None else acc
             for j, r in enumerate(rows):
-                for g in range(G):
+                for g in passes:
                     nc.tensor.matmul_mx(
                         out=acc[:, n * j : n * j + n],
                         lhsT=x_codes[r][:, P * g : P * g + P].bitcast(X4),
@@ -246,44 +248,58 @@ def tile_plate_centred_gene_scores_d2_kernel(tc, x_bytes, x_scale, w_bytes, w_sc
         fourth_ready = FOURTH_FROM + (G - 1) // RATE4 + 1
         paired = (third_ready - 2) // 2 * 2
 
+        spread = take("turn", turns)
+        nc.tensor.transpose(spread[:, :P], ws_col[:].to_broadcast([P, P]), ident[:])
         widen_x_vector(0)
         for q in range(4):
             rows = slice(32 * q, 32 * q + 32)
-            nc.vector.tensor_copy(out=ws[rows, :, :], in_=wsb[rows, :].rearrange("p (g q d) -> p g q d", q=4, d=8)[:, :, q, :])
+            nc.vector.tensor_copy(out=ws[rows, :, :], in_=spread[rows, :P].rearrange("p (g q d) -> p g q d", q=4, d=8)[:, :, q, :])
         turn(0)
-        for g in range(3):
-            widen_w(0, g)
+        first = [(((0,), 0, BANK), free_banks.pop(0)), (((MEANS,), 0, BANK), free_banks.pop(0))]
+        widen_w(0, 0)
+        widen_w(0, 1)
+        collect(0)
+        widen_w(0, 2)
         interleave_w(0, 0)
         widen_w(0, 3)
-        collect(0)
         turn(MEANS)
         widen_x_scalar(1)
         collect(MEANS)
-        for g in range(1, G):
-            interleave_w(0, g)
-            quantise_w(0, g - 1)
+        interleave_w(0, 1)
+        quantise_w(0, 0)
         quantise_x(0)
-        quantise_w(0, G - 1)
+        interleave_w(0, 2)
+        quantise_w(0, 1)
+        multiply(*first[0], range(2))
+        widen_x_vector(1)
+        turn(1)
+        interleave_w(0, 3)
+        quantise_w(0, 2)
+        multiply(*first[0], range(2, 3))
         quantise_x(MEANS)
+        multiply(*first[1], range(3))
+        quantise_w(0, 3)
         for job in narrow.get(2, []):
             widen_w(*job)
         widen_x_scalar(2)
 
-        due = [((MEANS,), 0, BANK), ((0,), 0, BANK)]
+        due = []
         full, waiting, given = [], [], 0
         for i in range(2, R + 1):
             tile = order[i]
-            if i == third_ready:
-                due = due + [((MEANS,), 512, 256)] + [((r, r + 1), 512, 256) for r in range(0, paired, 2)]
-            if i == fourth_ready:
-                due = due + [((MEANS,), 768, 256)] + [((r, r + 1), 768, 256) for r in range(0, paired, 2)] + [((r,), BANK, BANK) for r in range(paired, i - 2)]
-            if i > 2:
-                due = due + [((i - 2,), c0, BANK) for c0 in range(0, N if i >= fourth_ready else BANK, BANK)]
+            fresh = [((i - 2,), c0, BANK) for c0 in range(0, N if i >= fourth_ready else BANK, BANK)] if i > 2 else []
+            if i in (third_ready, fourth_ready):
+                c0 = 512 if i == third_ready else 768
+                pairs = [((r, r + 1), c0, 256) for r in range(0, paired, 2)]
+                wholes = [((r,), BANK, BANK) for r in range(paired, i - 2)] if i == fourth_ready else []
+                fresh = [((MEANS,), c0, 256)] + pairs[:1] + fresh[:1] + wholes + pairs[1:] + fresh[1:]
+            due = due + fresh
             if i == third_ready:
                 left = len(due) + 1 + paired // 2 + (R - 1 - paired) + (R - i) - HOLD
             k, rounds = i - third_ready, R + 1 - third_ready
             cap = i - 1 if k < 0 else -(-left * (k + 1) // rounds) - given
-            turn(tile)
+            if i > 2:
+                turn(tile)
             new = [unit[1] for unit, acc in full if unit[0][0] == MEANS]
             held = [(unit, acc) for unit, acc in full if unit[0][0] != MEANS and unit[1] in new]
             for unit, acc in reversed(full):
@@ -294,6 +310,8 @@ def tile_plate_centred_gene_scores_d2_kernel(tc, x_bytes, x_scale, w_bytes, w_sc
             now, due = due[:cap], due[cap:]
             given += cap if k >= 0 else 0
             full = [(unit, multiply(unit)) for unit in now]
+            if i == 2:
+                full = [(unit, multiply(unit, acc, range(3, G))) for unit, acc in first]
             if i == GAIN_AT:
                 for h in range(2):
                     cols = slice(BANK * h, BANK * h + BANK)

@@ -59,10 +59,15 @@ def tile_plate_centred_gene_scores_d2_kernel(tc, x_bytes, x_scale, w_bytes, w_sc
         grouped = tiles(keep, "xg", R + 1, [P, K], BF16)
         w_wide = tiles(keep, "ww", 3, [P, K], BF16)
         w_grouped = tiles(keep, "wg", 2, [P, K], BF16)
-        x_codes = tiles(keep, "xc", R + 1, [P, G * P], U32)
-        x_exps = tiles(keep, "xq", R + 1, [P, G * P], U8)
-        w_codes = tiles(keep, "wc", G, [P, N], U32)
-        w_exps = tiles(keep, "wq", G, [P, N], U8)
+
+        def placed(name, count, width, dtype, skip):
+            whole = keep.tile([P, skip + count * width], dtype, name=name, align_bytes=256)
+            return [whole[:, skip + j * width : skip + (j + 1) * width] for j in range(count)]
+
+        x_codes = placed("xc", R + 1, G * P, U32, 0)
+        x_exps = placed("xq", R + 1, G * P, U8, 64)
+        w_codes = placed("wc", G, N, U32, 32)
+        w_exps = placed("wq", G, N, U8, 192)
         xs_first = keep.tile([P, 2 * C], F32, name="xs_first")
         xs_rest = keep.tile([P, (R - 2) * C], F32, name="xs_rest")
         ws_col = keep.tile([P, 1], F32, name="ws_col")
@@ -170,7 +175,7 @@ def tile_plate_centred_gene_scores_d2_kernel(tc, x_bytes, x_scale, w_bytes, w_sc
                 )
 
         def quantise_x(r):
-            nc.vector.quantize_mx(out=x_codes[r][:].bitcast(X4), scales=x_exps[r][:], in_=grouped[r][:])
+            nc.vector.quantize_mx(out=x_codes[r].bitcast(X4), scales=x_exps[r], in_=grouped[r][:])
 
         def widen_w(part, g):
             t = widened[part, g] = take("wide", w_wide)[:, : 4 * PARTS[part][1]]

@@ -30,8 +30,8 @@ RATE4 = 2
 ONE_FROM = 11
 REORDER_FROM = 8
 HOLD = 1
+GAIN_AT = 2
 TG = 2
-GAIN_AT = 4
 TURNABLE = 10
 ACCS = 4
 TURNS = 3
@@ -49,9 +49,9 @@ def tile_plate_centred_gene_scores_d2_kernel(tc, x_bytes, x_scale, w_bytes, w_sc
 
         ident = keep.tile([P, P], F32, name="ident")
         make_identity(nc, ident[:])
-        ident_b = keep.tile([P, P], BF16, name="ident_b")
-        make_identity(nc, ident_b[:])
-        gain_p = psum.tile([P, N], BF16, name="gain_p")
+        gain_words = psum.tile([P, BANK], F32, name="gain_words")
+        gain_p = gain_words[:].bitcast(BF16)
+        gain_col = keep.tile([P, 8], BF16, name="gain_col")
         turns = [psum.tile([P, BANK], F32, name="turn%d" % j) for j in range(TURNS)]
         free_banks = [psum.tile([P, BANK], F32, name="acc%d" % j) for j in range(ACCS)]
         turnable = tiles(keep, "xt", TURNABLE, [P, 512], BF16)
@@ -108,16 +108,14 @@ def tile_plate_centred_gene_scores_d2_kernel(tc, x_bytes, x_scale, w_bytes, w_sc
         load_x(1, 1)
         nc.sync.dma_start(out=mw[:], in_=means)
         nc.sync.dma_start(out=xs_rest[:], in_=x_scales[:, 2 * C :])
+        nc.sync.dma_start(out=gain_col[:], in_=gain.rearrange("(p c) -> p c", c=8))
         load_x(2, 2)
         for g in range(G):
             load_w(1, g)
         load_x(4, 2)
         for g in range(G):
             load_w(2, g)
-        load_x(6, 2)
-        load_x(8, 2)
-        nc.sync.dma_start(out=gain_b[:], in_=gain.partition_broadcast(P))
-        for r in range(10, R, 2):
+        for r in range(6, R, 2):
             load_x(r, 2)
 
         order = [0, MEANS] + list(range(1, R))
@@ -278,6 +276,8 @@ def tile_plate_centred_gene_scores_d2_kernel(tc, x_bytes, x_scale, w_bytes, w_sc
         multiply(*first[0], range(2))
         widen_x_vector(1)
         turn(1)
+        for c in range(4):
+            nc.tensor.transpose(gain_words[:, c:BANK:4], gain_col[:].bitcast(F32)[:, c : c + 1].to_broadcast([P, P]), ident[:])
         interleave_w(0, 3)
         quantise_w(0, 2)
         multiply(*first[0], range(2, 3))
@@ -317,10 +317,6 @@ def tile_plate_centred_gene_scores_d2_kernel(tc, x_bytes, x_scale, w_bytes, w_sc
             full = [(unit, multiply(unit)) for unit in now]
             if i == 2:
                 full = [(unit, multiply(unit, acc, range(3, G))) for unit, acc in first]
-            if i == GAIN_AT:
-                for h in range(2):
-                    cols = slice(BANK * h, BANK * h + BANK)
-                    nc.tensor.matmul(out=gain_p[:, cols], lhsT=ident_b[:], rhs=gain_b[:, cols], start=True, stop=True)
             jobs = narrow.get(i, [])
             for job in jobs:
                 interleave_w(*job)
@@ -335,6 +331,8 @@ def tile_plate_centred_gene_scores_d2_kernel(tc, x_bytes, x_scale, w_bytes, w_sc
                 widen_w(*job)
             if i + 1 < R:
                 widen_x_scalar(i + 1)
+            if i == GAIN_AT:
+                nc.scalar.copy(out=gain_b[:].bitcast(F32), in_=gain_words[:])
             mine = len(full) - 1 if i >= fourth_ready else 0
             stretch = mine + len(held) + len([unit for unit, acc in full if unit[0][0] != MEANS])
             theirs = [w for w in waiting if w[0][2] == BANK][: 2 * stretch // 5 if i > third_ready else 0]

@@ -100,8 +100,8 @@ def tile_plate_centred_gene_scores_d2_kernel(tc, x_bytes, x_scale, w_bytes, w_sc
         def scale_of(r, c):
             return xs_first[:, C * r + c : C * r + c + 1] if r < 2 else xs_rest[:, C * (r - 2) + c : C * (r - 2) + c + 1]
 
-        nc.scalar.dma_start(out=xs_first[:], in_=x_scales[:, : 2 * C])
-        nc.scalar.dma_start(out=ws_col[:], in_=w_scale.rearrange("c (d o) -> (c d) o", o=1))
+        nc.sync.dma_start(out=xs_first[:], in_=x_scales[:, : 2 * C])
+        nc.sync.dma_start(out=ws_col[:], in_=w_scale.rearrange("c (d o) -> (c d) o", o=1))
         load_x(0, 1)
         for g in range(G):
             load_w(0, g)

@@ -20,21 +20,16 @@ R = T // PLATES
 G = K // 512
 C = K // 128
 BANK = 512
+QUARTER = 256
 MEANS = R
-PARTS = [(0, 512), (512, 256), (768, 256)]
 
-THIRD_FROM = 2
-FOURTH_FROM = 6
-RATE3 = 1
-RATE4 = 2
+PARTS = [(0, BANK), (BANK, QUARTER), (BANK + QUARTER, QUARTER)]
+THIRD_READY = 2 + G
+FOURTH_READY = THIRD_READY + G // 2
+PAIRED = THIRD_READY - 2
 ONE_FROM = 11
 REORDER_FROM = 8
-HOLD = 1
-GAIN_AT = 2
-TG = 2
-TURNABLE = 10
-ACCS = 4
-TURNS = 3
+HELD = 1
 
 
 def tile_plate_centred_gene_scores_d2_kernel(tc, x_bytes, x_scale, w_bytes, w_scale, means, gain, out):
@@ -44,157 +39,190 @@ def tile_plate_centred_gene_scores_d2_kernel(tc, x_bytes, x_scale, w_bytes, w_sc
         psum = ctx.enter_context(tc.psum_pool(name="psum", bufs=1))
         ctx.enter_context(tc.manual_schedule())
 
-        def tiles(pool, name, count, shape, dtype):
-            return [pool.tile(shape, dtype, name="%s%d" % (name, j), align_bytes=64) for j in range(count)]
-
-        ident = keep.tile([P, P], F32, name="ident")
-        make_identity(nc, ident[:])
-        gain_words = psum.tile([P, BANK], F32, name="gain_words")
-        gain_p = gain_words[:].bitcast(BF16)
-        gain_col = keep.tile([P, 8], BF16, name="gain_col")
-        turns = [psum.tile([P, BANK], F32, name="turn%d" % j) for j in range(TURNS)]
-        free_banks = [psum.tile([P, BANK], F32, name="acc%d" % j) for j in range(ACCS)]
-        turnable = tiles(keep, "xt", TURNABLE, [P, 512], BF16)
-        plain = tiles(keep, "xs", 4, [P, 512], BF16)
-        grouped = tiles(keep, "xg", R + 1, [P, K], BF16)
-        w_wide = tiles(keep, "ww", 3, [P, K], BF16)
-        w_grouped = tiles(keep, "wg", 2, [P, K], BF16)
+        def tiles(name, count, shape, dtype):
+            return [keep.tile(shape, dtype, name="%s%d" % (name, j), align_bytes=64) for j in range(count)]
 
         def placed(name, count, width, dtype, skip):
             whole = keep.tile([P, skip + count * width], dtype, name=name, align_bytes=256)
             return [whole[:, skip + j * width : skip + (j + 1) * width] for j in range(count)]
 
+        def halves(tile):
+            return [tile[:].bitcast(F32)[:, BANK * h : BANK * h + BANK] for h in range(2)]
+
+        ident = keep.tile([P, P], F32, name="ident")
+        make_identity(nc, ident[:])
+
+        gain_words = psum.tile([P, BANK], F32, name="gain_words")
+        gain_psum = gain_words[:].bitcast(BF16)
+        gain_col = keep.tile([P, N // P], BF16, name="gain_col")
+        turn_banks = [psum.tile([P, BANK], F32, name="turn%d" % j) for j in range(3)]
+        free_banks = [psum.tile([P, BANK], F32, name="acc%d" % j) for j in range(4)]
+
+        turnable = tiles("xt", 2 * G + 2, [P, 512], BF16)
+        unordered = tiles("xs", G, [P, 512], BF16)
+        grouped = tiles("xg", R + 1, [P, K], BF16)
+        w_wide = tiles("ww", G, [P, K], BF16)
+
         x_codes = placed("xc", R + 1, G * P, U32, 0)
         x_exps = placed("xq", R + 1, G * P, U8, 64)
         w_codes = placed("wc", G, N, U32, 32)
         w_exps = placed("wq", G, N, U8, 192)
+
         xs_first = keep.tile([P, 2 * C], F32, name="xs_first")
         xs_rest = keep.tile([P, (R - 2) * C], F32, name="xs_rest")
         ws_col = keep.tile([P, 1], F32, name="ws_col")
-        ws = keep.tile([P, G, 8], F32, name="ws")
-        gain_b = keep.tile([P, N], BF16, name="gain_b")
-        mw = keep.tile([P, K], BF16, name="mw")
-        cen = keep.tile([P, N], F32, name="cen")
+        ws = keep.tile([P, G, N // 128], F32, name="ws")
+        quadrant = keep.tile([P, 4], F32, name="quadrant")
+        picked = keep.tile([P, G, N // 128, 4], F32, name="picked")
+        gain_sbuf = keep.tile([P, N], BF16, name="gain_sbuf")
+        means_rows = keep.tile([P, K], BF16, name="means_rows")
+        centre = keep.tile([P, N], F32, name="centre")
 
         x_rows = x_bytes.rearrange("(p r) k -> p r k", r=R)
+        x_scales = x_scale.rearrange("(p r) c -> p (r c)", r=R)
         out_rows = out.rearrange("(p r) n -> p r n", r=R)
         w_raw, x_raw = {}, {}
 
-        def load_w(part, g):
+        def load_w(part):
             c0, n = PARTS[part]
-            t = keep.tile([P, 4 * n], U8, name="wb%d%d" % (part, g))
-            nc.sync.dma_start(
-                out=t[:].rearrange("p (t n) -> p t n", t=4),
-                in_=w_bytes[512 * g : 512 * g + 512, c0 : c0 + n].rearrange("(p t) n -> p t n", t=4),
-            )
-            w_raw[part, g] = t
+            for g in range(G):
+                w_raw[part, g] = keep.tile([P, 4 * n], U8, name="wb%d%d" % (part, g))
+                nc.sync.dma_start(
+                    out=w_raw[part, g][:].rearrange("p (t n) -> p t n", t=4),
+                    in_=w_bytes[512 * g : 512 * g + 512, c0 : c0 + n].rearrange("(p t) n -> p t n", t=4),
+                )
 
         def load_x(r, rows):
-            t = keep.tile([P, rows * K], U8, name="xb%d" % r)
-            nc.sync.dma_start(out=t[:], in_=x_rows[:, r : r + rows, :].rearrange("p r k -> p (r k)"))
+            raw = keep.tile([P, rows * K], U8, name="xb%d" % r)
+            nc.sync.dma_start(out=raw[:], in_=x_rows[:, r : r + rows, :].rearrange("p r k -> p (r k)"))
             for j in range(rows):
-                x_raw[r + j] = t[:, j * K : (j + 1) * K]
-
-        x_scales = x_scale.rearrange("(p r) c -> p (r c)", r=R)
-
-        def scale_of(r, c):
-            return xs_first[:, C * r + c : C * r + c + 1] if r < 2 else xs_rest[:, C * (r - 2) + c : C * (r - 2) + c + 1]
+                x_raw[r + j] = raw[:, j * K : (j + 1) * K]
 
         nc.sync.dma_start(out=xs_first[:], in_=x_scales[:, : 2 * C])
         nc.sync.dma_start(out=ws_col[:], in_=w_scale.rearrange("c (d o) -> (c d) o", o=1))
         load_x(0, 1)
-        for g in range(G):
-            load_w(0, g)
+        load_w(0)
         load_x(1, 1)
-        nc.sync.dma_start(out=mw[:], in_=means)
+        nc.sync.dma_start(out=means_rows[:], in_=means)
         nc.sync.dma_start(out=xs_rest[:], in_=x_scales[:, 2 * C :])
-        nc.sync.dma_start(out=gain_col[:], in_=gain.rearrange("(p c) -> p c", c=8))
+        nc.sync.dma_start(out=gain_col[:], in_=gain.rearrange("(p c) -> p c", p=P))
         load_x(2, 2)
-        for g in range(G):
-            load_w(1, g)
+        load_w(1)
         load_x(4, 2)
-        for g in range(G):
-            load_w(2, g)
+        load_w(2)
         for r in range(6, R, 2):
             load_x(r, 2)
 
-        order = [0, MEANS] + list(range(1, R))
-        count = {"turnable": 0, "plain": 0, "turn": 0, "diff": 0, "wide": 0, "grouped": 0}
-        words, turned, widened, interleaved = {}, {}, {}, {}
+        taken = {}
 
         def take(name, ring):
-            count[name] += 1
-            return ring[(count[name] - 1) % len(ring)]
+            taken[name] = taken.get(name, -1) + 1
+            return ring[taken[name] % len(ring)]
 
-        def vector_share(r):
-            return G if r == 0 else 1 if r >= ONE_FROM and r % 2 else 2
+        def block(r, c):
+            scales, row = (xs_first, r) if r < 2 else (xs_rest, r - 2)
+            return x_raw[r][:, 128 * c : 128 * c + 128].bitcast(F8), scales[:, C * row + c : C * row + c + 1]
 
-        def widen_x_vector(r):
-            for g in range(G - vector_share(r), G):
-                t = take("turnable", turnable)
-                dst = t[:].rearrange("p (u s e) -> p s u e", u=2, e=2)
+        words, turned, widened, interleaved = {}, {}, {}, {}
+
+        def every_second(ap):
+            return [ap.bitcast(F32)[:, u : 2 * P : 2] for u in range(2)]
+
+        def side_by_side(ap):
+            return [ap.bitcast(F32)[:, P * u : P * u + P] for u in range(2)]
+
+        def widen_x_vector(r, passes):
+            for g in passes:
+                wide = take("turnable", turnable)
+                reordered = wide[:].rearrange("p (u s e) -> p s u e", u=2, e=2)
                 for q in range(4):
-                    c = 4 * g + q
-                    src = x_raw[r][:, 128 * c : 128 * c + 128].bitcast(F8).rearrange("p (s u e) -> p s u e", u=2, e=2)
-                    nc.vector.tensor_scalar(out=dst[:, 32 * q : 32 * q + 32, :, :], in0=src, scalar1=scale_of(r, c), scalar2=None, op0=ALU.mult)
-                words[r, g] = [t[:].bitcast(F32)[:, P * u : P * u + P] for u in range(2)]
+                    codes, scale = block(r, 4 * g + q)
+                    nc.vector.tensor_scalar(
+                        out=reordered[:, 32 * q : 32 * q + 32, :, :],
+                        in0=codes.rearrange("p (s u e) -> p s u e", u=2, e=2),
+                        scalar1=scale,
+                        scalar2=None,
+                        op0=ALU.mult,
+                    )
+                words[r, g] = side_by_side(wide[:])
 
-        def widen_x_scalar(r):
-            mine = range(G - vector_share(r))
-            again = mine if r >= REORDER_FROM else []
+        def widen_x_scalar(r, passes):
+            reorder = r >= REORDER_FROM
             wide = {}
-            for g in mine:
-                t = wide[g] = take("plain", plain) if g in again else take("turnable", turnable)
+            for g in passes:
+                wide[g] = take("unordered", unordered) if reorder else take("turnable", turnable)
                 for q in range(4):
-                    c = 4 * g + q
-                    nc.scalar.activation(out=t[:, 128 * q : 128 * q + 128], in_=x_raw[r][:, 128 * c : 128 * c + 128].bitcast(F8), func=COPY, scale=scale_of(r, c))
-                words[r, g] = [t[:].bitcast(F32)[:, u : 2 * P : 2] for u in range(2)]
-            for g in again:
-                t = take("turnable", turnable)
-                nc.scalar.copy(out=t[:].bitcast(F32).rearrange("p (u s) -> p u s", u=2), in_=wide[g][:].bitcast(F32).rearrange("p (s u) -> p u s", u=2))
-                words[r, g] = [t[:].bitcast(F32)[:, P * u : P * u + P] for u in range(2)]
+                    codes, scale = block(r, 4 * g + q)
+                    nc.scalar.activation(out=wide[g][:, 128 * q : 128 * q + 128], in_=codes, func=COPY, scale=scale)
+                words[r, g] = every_second(wide[g][:])
+            if reorder:
+                for g in passes:
+                    reordered = take("turnable", turnable)
+                    nc.scalar.copy(
+                        out=reordered[:].bitcast(F32).rearrange("p (u s) -> p u s", u=2),
+                        in_=wide[g][:].bitcast(F32).rearrange("p (s u) -> p u s", u=2),
+                    )
+                    words[r, g] = side_by_side(reordered[:])
+
+        def vector_passes(r):
+            return range(G - (1 if r >= ONE_FROM and r % 2 else 2), G)
+
+        def scalar_passes(r):
+            return [g for g in range(G) if g not in vector_passes(r)]
 
         for g in range(G):
-            words[MEANS, g] = [mw[:, 512 * g : 512 * g + 512].bitcast(F32)[:, u : 2 * P : 2] for u in range(2)]
+            words[MEANS, g] = every_second(means_rows[:, 512 * g : 512 * g + 512])
 
         def turn(r):
             for b in range(2):
-                bank = turned[r, b] = take("turn", turns)
+                turned[r, b] = take("turn", turn_banks)
                 for j in range(4):
-                    nc.tensor.transpose(bank[:, P * j : P * j + P], words[r, 2 * b + j // 2][j % 2], ident[:])
+                    nc.tensor.transpose(turned[r, b][:, P * j : P * j + P], words[r, 2 * b + j // 2][j % 2], ident[:])
 
         def collect(r, centres=()):
             for b in (1, 0):
                 for unit, acc in centres if b == 0 else ():
-                    copy_centre(unit, acc)
+                    nc.scalar.copy(out=centre[:, unit[1] : unit[1] + unit[2]], in_=acc[:, : unit[2]])
+                    free_banks.append(acc)
                 nc.scalar.copy(
-                    out=grouped[r][:, 1024 * b : 1024 * b + 1024].bitcast(F32).rearrange("p (j s u) -> p j s u", j=2, u=2),
+                    out=halves(grouped[r])[b].rearrange("p (j s u) -> p j s u", j=2, u=2),
                     in_=turned[r, b][:].rearrange("p (j u s) -> p j s u", j=2, u=2),
                 )
 
         def quantise_x(r):
             nc.vector.quantize_mx(out=x_codes[r].bitcast(X4), scales=x_exps[r], in_=grouped[r][:])
 
+        def room(wide_tiles, narrow_tiles, part, g):
+            if part == 0:
+                return wide_tiles[g][:]
+            j = G * (part - 1) + g
+            return narrow_tiles[j // 2][:, K // 2 * (j % 2) : K // 2 * (j % 2 + 1)]
+
         def widen_w(part, g):
-            t = widened[part, g] = take("wide", w_wide)[:, : 4 * PARTS[part][1]]
-            nc.scalar.copy(out=t, in_=w_raw[part, g][:].bitcast(F8))
+            widened[part, g] = room(grouped[G : 2 * G], w_wide, part, g)
+            nc.scalar.copy(out=widened[part, g], in_=w_raw[part, g][:].bitcast(F8))
 
         def interleave_w(part, g):
             c0, n = PARTS[part]
-            t = interleaved[part, g] = take("grouped", w_grouped)[:, : 4 * n]
+            interleaved[part, g] = room(grouped[3 * G :], grouped[2 * G :], part, g)
             src = widened[part, g].rearrange("p (t c i) -> p c t i", t=4, i=4)
-            dst = t.rearrange("p (c i t) -> p c t i", t=4, i=4)
+            dst = interleaved[part, g].rearrange("p (c i t) -> p c t i", t=4, i=4)
             for j in range(n // 128):
                 d = c0 // 128 + j
-                nc.vector.tensor_scalar(out=dst[:, 32 * j : 32 * j + 32, :, :], in0=src[:, 32 * j : 32 * j + 32, :, :], scalar1=ws[:, g, d : d + 1], scalar2=None, op0=ALU.mult)
+                nc.vector.tensor_scalar(
+                    out=dst[:, 32 * j : 32 * j + 32, :, :],
+                    in0=src[:, 32 * j : 32 * j + 32, :, :],
+                    scalar1=ws[:, g, d : d + 1],
+                    scalar2=None,
+                    op0=ALU.mult,
+                )
 
         def quantise_w(part, g):
             c0, n = PARTS[part]
             nc.vector.quantize_mx(out=w_codes[g][:, c0 : c0 + n].bitcast(X4), scales=w_exps[g][:, c0 : c0 + n], in_=interleaved[part, g])
 
-        def multiply(unit, acc=None, passes=range(G)):
+        def multiply(unit, acc, passes):
             rows, c0, n = unit
-            acc = free_banks.pop(0) if acc is None else acc
             for j, r in enumerate(rows):
                 for g in passes:
                     nc.tensor.matmul_mx(
@@ -206,26 +234,26 @@ def tile_plate_centred_gene_scores_d2_kernel(tc, x_bytes, x_scale, w_bytes, w_sc
                         start=(g == 0),
                         stop=(g == G - 1),
                     )
-            return acc
+            return unit, acc
 
         def shaped(ap, unit):
             rows, c0, n = unit
             return ap[:, : n * len(rows)].rearrange("p (j n) -> p j n", n=n) if len(rows) > 1 else ap[:, :n]
 
-        def columns(tile, unit):
+        def columns(ap, unit):
             rows, c0, n = unit
-            return tile[:, c0 : c0 + n].unsqueeze(1).to_broadcast([P, len(rows), n]) if len(rows) > 1 else tile[:, c0 : c0 + n]
+            return ap[:, c0 : c0 + n].unsqueeze(1).to_broadcast([P, len(rows), n]) if len(rows) > 1 else ap[:, c0 : c0 + n]
 
-        spare, later = [], [grouped[0][:].bitcast(F32)[:, BANK * h : BANK * h + BANK] for h in range(2)]
+        spare = []
 
         def subtract(unit, acc):
             if not spare:
-                count["diff"] += 1
-                spare.append(keep.tile([P, BANK], F32, name="diff%d" % count["diff"])[:])
+                taken["diff"] = taken.get("diff", -1) + 1
+                spare.append(keep.tile([P, BANK], F32, name="diff%d" % taken["diff"])[:])
             diff = spare.pop(0)
-            nc.vector.tensor_tensor(out=shaped(diff, unit), in0=shaped(acc, unit), in1=columns(cen, unit), op=ALU.subtract)
+            nc.vector.tensor_tensor(out=shaped(diff, unit), in0=shaped(acc, unit), in1=columns(centre, unit), op=ALU.subtract)
             free_banks.append(acc)
-            return diff
+            return unit, diff
 
         def store(unit, result):
             rows, c0, n = unit
@@ -233,30 +261,29 @@ def tile_plate_centred_gene_scores_d2_kernel(tc, x_bytes, x_scale, w_bytes, w_sc
             nc.sync.dma_start(out=dst, in_=shaped(result, unit))
 
         def gain_vector(unit, diff):
-            nc.vector.tensor_tensor(out=shaped(diff, unit), in0=shaped(diff, unit), in1=columns(gain_p, unit), op=ALU.mult)
+            nc.vector.tensor_tensor(out=shaped(diff, unit), in0=shaped(diff, unit), in1=columns(gain_psum, unit), op=ALU.mult)
             store(unit, diff)
 
-        def gain_pool(unit, diff, room):
-            nc.gpsimd.tensor_tensor(out=shaped(room, unit), in0=shaped(diff, unit), in1=columns(gain_b, unit), op=ALU.mult)
+        def gain_gpsimd(unit, diff, result):
+            nc.gpsimd.tensor_tensor(out=result, in0=diff, in1=columns(gain_sbuf, unit), op=ALU.mult)
 
-        def copy_centre(unit, acc):
-            nc.scalar.copy(out=cen[:, unit[1] : unit[1] + unit[2]], in_=acc[:, : unit[2]])
-            free_banks.append(acc)
+        def jobs_of(i):
+            if i < THIRD_READY:
+                return [(1, i - 2)]
+            return [(2, 2 * (i - THIRD_READY) + j) for j in range(2)] if i < FOURTH_READY else []
 
-        narrow = {}
-        for part, first, rate in ((1, THIRD_FROM, RATE3), (2, FOURTH_FROM, RATE4)):
-            for g in range(G):
-                narrow.setdefault(first + g // rate, []).append((part, g))
-        third_ready = THIRD_FROM + (G - 1) // RATE3 + 1
-        fourth_ready = FOURTH_FROM + (G - 1) // RATE4 + 1
-        paired = (third_ready - 2) // 2 * 2
-
-        spread = take("turn", turns)
+        spread = take("turn", turn_banks)
         nc.tensor.transpose(spread[:, :P], ws_col[:].to_broadcast([P, P]), ident[:])
-        widen_x_vector(0)
-        for q in range(4):
-            rows = slice(32 * q, 32 * q + 32)
-            nc.vector.tensor_copy(out=ws[rows, :, :], in_=spread[rows, :P].rearrange("p (g q d) -> p g q d", q=4, d=8)[:, :, q, :])
+        nc.vector.tensor_reduce(out=quadrant[:], in_=ident[:].rearrange("p (q j) -> p q j", q=4), op=ALU.add, axis=mybir.AxisListType.X)
+        widen_x_vector(0, range(G - 1))
+        nc.vector.tensor_tensor(
+            out=picked[:],
+            in0=spread[:, :P].rearrange("p (g q d) -> p g d q", g=G, q=4),
+            in1=quadrant[:].unsqueeze(1).unsqueeze(1).to_broadcast([P, G, N // 128, 4]),
+            op=ALU.mult,
+        )
+        widen_x_vector(0, range(G - 1, G))
+        nc.vector.tensor_reduce(out=ws[:], in_=picked[:], op=ALU.add, axis=mybir.AxisListType.X)
         turn(0)
         first = [(((0,), 0, BANK), free_banks.pop(0)), (((MEANS,), 0, BANK), free_banks.pop(0))]
         widen_w(0, 0)
@@ -266,7 +293,7 @@ def tile_plate_centred_gene_scores_d2_kernel(tc, x_bytes, x_scale, w_bytes, w_sc
         interleave_w(0, 0)
         widen_w(0, 3)
         turn(MEANS)
-        widen_x_scalar(1)
+        widen_x_scalar(1, scalar_passes(1))
         collect(MEANS)
         interleave_w(0, 1)
         quantise_w(0, 0)
@@ -274,7 +301,7 @@ def tile_plate_centred_gene_scores_d2_kernel(tc, x_bytes, x_scale, w_bytes, w_sc
         interleave_w(0, 2)
         quantise_w(0, 1)
         multiply(*first[0], range(2))
-        widen_x_vector(1)
+        widen_x_vector(1, vector_passes(1))
         turn(1)
         for c in range(4):
             nc.tensor.transpose(gain_words[:, c:BANK:4], gain_col[:].bitcast(F32)[:, c : c + 1].to_broadcast([P, P]), ident[:])
@@ -284,91 +311,92 @@ def tile_plate_centred_gene_scores_d2_kernel(tc, x_bytes, x_scale, w_bytes, w_sc
         quantise_x(MEANS)
         multiply(*first[1], range(3))
         quantise_w(0, 3)
-        for job in narrow.get(2, []):
+        for job in jobs_of(2):
             widen_w(*job)
-        widen_x_scalar(2)
+        widen_x_scalar(2, scalar_passes(2))
 
-        due = []
-        full, waiting, given = [], [], 0
+        paced = 2 + PAIRED + (R - 1 - PAIRED) + (R + 1 - THIRD_READY) - HELD
+        due, full, waiting, given = [], [], [], 0
+        later = halves(grouped[0])
         for i in range(2, R + 1):
-            tile = order[i]
-            fresh = [((i - 2,), c0, BANK) for c0 in range(0, N if i >= fourth_ready else BANK, BANK)] if i > 2 else []
-            if i in (third_ready, fourth_ready):
-                c0 = 512 if i == third_ready else 768
-                pairs = [((r, r + 1), c0, 256) for r in range(0, paired, 2)]
-                wholes = [((r,), BANK, BANK) for r in range(paired, i - 2)] if i == fourth_ready else []
-                fresh = [((MEANS,), c0, 256)] + pairs[:1] + fresh[:1] + wholes + pairs[1:] + fresh[1:]
+            tile = i - 1
+            fresh = [((i - 2,), c0, BANK) for c0 in range(0, N if i >= FOURTH_READY else BANK, BANK)] if i > 2 else []
+            if i in (THIRD_READY, FOURTH_READY):
+                c0 = PARTS[1 if i == THIRD_READY else 2][0]
+                pairs = [((r, r + 1), c0, QUARTER) for r in range(0, PAIRED, 2)]
+                wholes = [((r,), BANK, BANK) for r in range(PAIRED, i - 2)]
+                fresh = [((MEANS,), c0, QUARTER)] + pairs[:1] + fresh[:1] + wholes + pairs[1:] + fresh[1:]
             due = due + fresh
-            if i == third_ready:
-                left = len(due) + 1 + paired // 2 + (R - 1 - paired) + (R - i) - HOLD
-            k, rounds = i - third_ready, R + 1 - third_ready
-            cap = i - 1 if k < 0 else -(-left * (k + 1) // rounds) - given
             if i > 2:
                 turn(tile)
-            new = [unit[1] for unit, acc in full if unit[0][0] == MEANS]
-            held = [(unit, acc) for unit, acc in full if unit[0][0] != MEANS and unit[1] in new]
+
+            centres = [(unit, acc) for unit, acc in full if unit[0][0] == MEANS]
+            held = [(unit, acc) for unit, acc in full if unit[0][0] != MEANS and unit[1] in [c[0][1] for c in centres]]
             for unit, acc in reversed(full):
-                if unit[0][0] != MEANS and unit[1] not in new:
-                    waiting.append((unit, subtract(unit, acc)))
-            collect(tile, [(unit, acc) for unit, acc in full if unit[0][0] == MEANS])
-            cap = min(cap, len(free_banks), len(due))
-            now, due = due[:cap], due[cap:]
-            given += cap if k >= 0 else 0
-            full = [(unit, multiply(unit)) for unit in now]
+                if (unit, acc) not in centres + held:
+                    waiting.append(subtract(unit, acc))
+            collect(tile, centres)
+
             if i == 2:
-                full = [(unit, multiply(unit, acc, range(3, G))) for unit, acc in first]
-            jobs = narrow.get(i, [])
-            for job in jobs:
+                full = [multiply(unit, acc, range(G - 1, G)) for unit, acc in first]
+            else:
+                count = min(len(due), len(free_banks), 3)
+                if i >= THIRD_READY:
+                    count = min(count, -(-paced * (i + 1 - THIRD_READY) // (R + 1 - THIRD_READY)) - given)
+                    given += count
+                full = [multiply(unit, free_banks.pop(0), range(G)) for unit in due[:count]]
+                due = due[count:]
+
+            for job in jobs_of(i):
                 interleave_w(*job)
             if i < R:
-                widen_x_vector(i)
-            for job in reversed(jobs):
+                widen_x_vector(i, vector_passes(i))
+            for job in reversed(jobs_of(i)):
                 quantise_w(*job)
             quantise_x(tile)
             for unit, acc in held:
-                waiting.append((unit, subtract(unit, acc)))
-            for job in narrow.get(i + 1, []):
+                waiting.append(subtract(unit, acc))
+            for job in jobs_of(i + 1):
                 widen_w(*job)
             if i + 1 < R:
-                widen_x_scalar(i + 1)
-            if i == GAIN_AT:
-                nc.scalar.copy(out=gain_b[:].bitcast(F32), in_=gain_words[:])
-            mine = len(full) - 1 if i >= fourth_ready else 0
-            stretch = mine + len(held) + len([unit for unit, acc in full if unit[0][0] != MEANS])
-            theirs = [w for w in waiting if w[0][2] == BANK][: 2 * stretch // 5 if i > third_ready else 0]
-            halves = [grouped[tile][:].bitcast(F32)[:, BANK * h : BANK * h + BANK] for h in range(2)]
-            rooms = [halves[0]] + [diff for unit, diff in theirs[1:]]
-            for (unit, diff), room in zip(theirs, rooms):
-                gain_pool(unit, diff, room)
-            waiting = [w for w in waiting if w not in theirs]
-            pairs_first = sorted(waiting, key=lambda w: w[0][2])[:mine]
-            for unit, diff in pairs_first:
-                gain_vector(unit, diff)
-            waiting = [w for w in waiting if w not in pairs_first]
-            for (unit, diff), room in zip(theirs, rooms):
-                store(unit, room)
-            spare.extend(later)
-            later = halves[1:] if theirs else halves
-            if i == fourth_ready:
-                later = later + [t[:].bitcast(F32)[:, BANK * h : BANK * h + BANK] for t in [mw] + w_wide + w_grouped for h in range(2)]
+                widen_x_scalar(i + 1, scalar_passes(i + 1))
+            if i == 2:
+                nc.scalar.copy(out=gain_sbuf[:].bitcast(F32), in_=gain_words[:])
 
-        free_banks.extend(turns)
-        due = due + [((R - 1,), 0, BANK), ((R - 1,), 512, 256), ((R - 1,), 768, 256)]
-        pool_turn = True
+            mine = len(full) - 1 if i >= FOURTH_READY else 0
+            stretch = mine + len(held) + len([unit for unit, acc in full if unit[0][0] != MEANS])
+            theirs = [w for w in waiting if w[0][2] == BANK][: 2 * stretch // 5 if i > THIRD_READY else 0]
+            results = halves(grouped[tile])[:1] + [diff for unit, diff in theirs[1:]]
+            for (unit, diff), result in zip(theirs, results):
+                gain_gpsimd(unit, diff, result)
+            waiting = [w for w in waiting if w not in theirs]
+            chosen = sorted(waiting, key=lambda w: w[0][2])[:mine]
+            for unit, diff in chosen:
+                gain_vector(unit, diff)
+            waiting = [w for w in waiting if w not in chosen]
+            for (unit, diff), result in zip(theirs, results):
+                store(unit, result)
+
+            spare.extend(later)
+            later = halves(grouped[tile])[1 if theirs else 0 :]
+            if i == FOURTH_READY:
+                later = later + [half for done in [means_rows] + w_wide for half in halves(done)]
+
+        free_banks.extend(turn_banks)
+        due = due + [((R - 1,), c0, n) for c0, n in PARTS]
+        gpsimd_turn = True
         while full or due:
             if due and free_banks:
-                unit = due.pop(0)
-                full.append((unit, multiply(unit)))
+                full.append(multiply(due.pop(0), free_banks.pop(0), range(G)))
                 continue
-            unit, acc = full.pop(0)
-            diff = subtract(unit, acc)
+            unit, diff = subtract(*full.pop(0))
             if waiting:
                 gain_vector(*waiting.pop(0))
-            if pool_turn and len(full) + len(due) >= TG:
-                gain_pool(unit, diff, diff)
+            if gpsimd_turn and len(full) + len(due) >= 2:
+                gain_gpsimd(unit, diff, diff)
                 store(unit, diff)
             else:
                 waiting.append((unit, diff))
-            pool_turn = not pool_turn
+            gpsimd_turn = not gpsimd_turn
         for unit, diff in waiting:
             gain_vector(unit, diff)

@@ -27,8 +27,8 @@ PARTS = [(0, BANK), (BANK, QUARTER), (BANK + QUARTER, QUARTER)]
 THIRD_READY = 2 + G
 FOURTH_READY = THIRD_READY + G // 2
 PAIRED = THIRD_READY - 2
-ONE_FROM = 11
-REORDER_FROM = 8
+ONE_FROM = 13
+REORDER_FROM = 9
 HELD = 1
 
 
@@ -59,7 +59,7 @@ def tile_plate_centred_gene_scores_d2_kernel(tc, x_bytes, x_scale, w_bytes, w_sc
         free_banks = [psum.tile([P, BANK], F32, name="acc%d" % j) for j in range(4)]
 
         turnable = tiles("xt", 2 * G + 2, [P, 512], BF16)
-        unordered = tiles("xs", G, [P, 512], BF16)
+        unordered = tiles("xs", G + 1, [P, 512], BF16)
         grouped = tiles("xg", R + 1, [P, K], BF16)
         w_wide = tiles("ww", G, [P, K], BF16)
 
@@ -98,8 +98,8 @@ def tile_plate_centred_gene_scores_d2_kernel(tc, x_bytes, x_scale, w_bytes, w_sc
             for j in range(rows):
                 x_raw[r + j] = raw[:, j * K : (j + 1) * K]
 
-        nc.sync.dma_start(out=xs_first[:], in_=x_scales[:, : 2 * C])
         nc.sync.dma_start(out=ws_col[:], in_=w_scale.rearrange("c (d o) -> (c d) o", o=1))
+        nc.sync.dma_start(out=xs_first[:], in_=x_scales[:, : 2 * C])
         load_x(0, 1)
         load_w(0)
         load_x(1, 1)
@@ -275,15 +275,16 @@ def tile_plate_centred_gene_scores_d2_kernel(tc, x_bytes, x_scale, w_bytes, w_sc
         spread = take("turn", turn_banks)
         nc.tensor.transpose(spread[:, :P], ws_col[:].to_broadcast([P, P]), ident[:])
         nc.vector.tensor_reduce(out=quadrant[:], in_=ident[:].rearrange("p (q j) -> p q j", q=4), op=ALU.add, axis=mybir.AxisListType.X)
-        widen_x_vector(0, range(G - 1))
+        widen_x_vector(0, range(2))
         nc.vector.tensor_tensor(
             out=picked[:],
             in0=spread[:, :P].rearrange("p (g q d) -> p g d q", g=G, q=4),
             in1=quadrant[:].unsqueeze(1).unsqueeze(1).to_broadcast([P, G, N // 128, 4]),
             op=ALU.mult,
         )
-        widen_x_vector(0, range(G - 1, G))
+        widen_x_vector(0, range(2, 3))
         nc.vector.tensor_reduce(out=ws[:], in_=picked[:], op=ALU.add, axis=mybir.AxisListType.X)
+        widen_x_vector(0, range(3, G))
         turn(0)
         first = [(((0,), 0, BANK), free_banks.pop(0)), (((MEANS,), 0, BANK), free_banks.pop(0))]
         widen_w(0, 0)
@@ -308,12 +309,16 @@ def tile_plate_centred_gene_scores_d2_kernel(tc, x_bytes, x_scale, w_bytes, w_sc
         interleave_w(0, 3)
         quantise_w(0, 2)
         multiply(*first[0], range(2, 3))
-        quantise_x(MEANS)
-        multiply(*first[1], range(3))
-        quantise_w(0, 3)
         for job in jobs_of(2):
             widen_w(*job)
         widen_x_scalar(2, scalar_passes(2))
+        collect(1)
+        quantise_x(MEANS)
+        multiply(*first[1], range(2))
+        widen_x_vector(2, vector_passes(2))
+        turn(2)
+        multiply(*first[1], range(2, 3))
+        quantise_w(0, 3)
 
         paced = 2 + PAIRED + (R - 1 - PAIRED) + (R + 1 - THIRD_READY) - HELD
         due, full, waiting, given = [], [], [], 0
@@ -327,7 +332,7 @@ def tile_plate_centred_gene_scores_d2_kernel(tc, x_bytes, x_scale, w_bytes, w_sc
                 wholes = [((r,), BANK, BANK) for r in range(PAIRED, i - 2)]
                 fresh = [((MEANS,), c0, QUARTER)] + pairs[:1] + fresh[:1] + wholes + pairs[1:] + fresh[1:]
             due = due + fresh
-            if i > 2:
+            if i > 3:
                 turn(tile)
 
             centres = [(unit, acc) for unit, acc in full if unit[0][0] == MEANS]
@@ -335,7 +340,8 @@ def tile_plate_centred_gene_scores_d2_kernel(tc, x_bytes, x_scale, w_bytes, w_sc
             for unit, acc in reversed(full):
                 if (unit, acc) not in centres + held:
                     waiting.append(subtract(unit, acc))
-            collect(tile, centres)
+            if i > 2:
+                collect(tile, centres)
 
             if i == 2:
                 full = [multiply(unit, acc, range(G - 1, G)) for unit, acc in first]
@@ -349,18 +355,21 @@ def tile_plate_centred_gene_scores_d2_kernel(tc, x_bytes, x_scale, w_bytes, w_sc
 
             for job in jobs_of(i):
                 interleave_w(*job)
-            if i < R:
+            if i == 2:
+                quantise_x(tile)
+            elif i < R:
                 widen_x_vector(i, vector_passes(i))
             for job in reversed(jobs_of(i)):
                 quantise_w(*job)
-            quantise_x(tile)
+            if i > 2:
+                quantise_x(tile)
             for unit, acc in held:
                 waiting.append(subtract(unit, acc))
             for job in jobs_of(i + 1):
                 widen_w(*job)
             if i + 1 < R:
                 widen_x_scalar(i + 1, scalar_passes(i + 1))
-            if i == 2:
+            if i == THIRD_READY - 1:
                 nc.scalar.copy(out=gain_sbuf[:].bitcast(F32), in_=gain_words[:])
 
             mine = len(full) - 1 if i >= FOURTH_READY else 0
@@ -370,7 +379,7 @@ def tile_plate_centred_gene_scores_d2_kernel(tc, x_bytes, x_scale, w_bytes, w_sc
             for (unit, diff), result in zip(theirs, results):
                 gain_gpsimd(unit, diff, result)
             waiting = [w for w in waiting if w not in theirs]
-            chosen = sorted(waiting, key=lambda w: w[0][2])[:mine]
+            chosen = sorted(waiting, key=lambda w: (w[0] in [unit for unit, acc in held], w[0][2]))[:mine]
             for unit, diff in chosen:
                 gain_vector(unit, diff)
             waiting = [w for w in waiting if w not in chosen]

@@ -27,7 +27,7 @@ PARTS = [(0, BANK), (BANK, QUARTER), (BANK + QUARTER, QUARTER)]
 THIRD_READY = 2 + G
 FOURTH_READY = THIRD_READY + G // 2
 PAIRED = THIRD_READY - 2
-ONE_FROM = 13
+ONE_FROM = 11
 REORDER_FROM = 9
 HELD = 1
 

@@ -23,13 +23,12 @@ BANK = 512
 QUARTER = 256
 MEANS = R
 
+
 PARTS = [(0, BANK), (BANK, QUARTER), (BANK + QUARTER, QUARTER)]
-THIRD_READY = 2 + G
-FOURTH_READY = THIRD_READY + G // 2
-PAIRED = THIRD_READY - 2
-ONE_FROM = 11
-REORDER_FROM = 9
-HELD = 1
+PAIRED = 4
+NEGATED = 2
+V_PASSES = [4,2,2,2,2,2,1,2,2,2,2,2,2,2,2,1]
+RUNS_FROM = 7
 
 
 def tile_plate_centred_gene_scores_d2_kernel(tc, x_bytes, x_scale, w_bytes, w_scale, means, gain, out):
@@ -55,13 +54,30 @@ def tile_plate_centred_gene_scores_d2_kernel(tc, x_bytes, x_scale, w_bytes, w_sc
         gain_words = psum.tile([P, BANK], F32, name="gain_words")
         gain_psum = gain_words[:].bitcast(BF16)
         gain_col = keep.tile([P, N // P], BF16, name="gain_col")
-        turn_banks = [psum.tile([P, BANK], F32, name="turn%d" % j) for j in range(3)]
-        free_banks = [psum.tile([P, BANK], F32, name="acc%d" % j) for j in range(4)]
+        banks = [psum.tile([P, BANK], F32, name="bank%d" % j) for j in range(7)]
 
-        turnable = tiles("xt", 2 * G + 2, [P, 512], BF16)
-        unordered = tiles("xs", G + 1, [P, 512], BF16)
+        turnable = tiles("xt", 4 * G, [P, 512], BF16)
+        unordered = tiles("xs", G, [P, 512], BF16)
         grouped = tiles("xg", R + 1, [P, K], BF16)
-        w_wide = tiles("ww", G, [P, K], BF16)
+        extra = tiles("ww", G, [P, K], BF16)
+
+        narrow_wide = list(extra)
+
+        def room(wide_tiles, narrow_tiles, part, g):
+            if part == 0:
+                return wide_tiles[g][:]
+            c0, n = PARTS[part]
+            first = 4 * (G * (c0 - BANK) + g * n)
+            return narrow_tiles[first // K][:, first % K : first % K + 4 * n]
+
+        def staged_in(r):
+            if G <= r < 2 * G:
+                return [("iw", 0, r - G)]
+            if 3 * G <= r < R:
+                return [("qw", 0, r - 3 * G)]
+            if 2 * G <= r < 3 * G:
+                return [("qw", part, g) for part in range(1, len(PARTS)) for g in range(G) if 4 * (G * (PARTS[part][0] - BANK) + g * PARTS[part][1]) // K == r - 2 * G]
+            return []
 
         x_codes = placed("xc", R + 1, G * P, U32, 0)
         x_exps = placed("xq", R + 1, G * P, U8, 64)
@@ -69,6 +85,7 @@ def tile_plate_centred_gene_scores_d2_kernel(tc, x_bytes, x_scale, w_bytes, w_sc
         w_exps = placed("wq", G, N, U8, 192)
 
         xs_first = keep.tile([P, 2 * C], F32, name="xs_first")
+        xs_minus = keep.tile([P, 2 * C], F32, name="xs_minus")
         xs_rest = keep.tile([P, (R - 2) * C], F32, name="xs_rest")
         ws_col = keep.tile([P, 1], F32, name="ws_col")
         ws = keep.tile([P, G, N // 128], F32, name="ws")
@@ -106,24 +123,18 @@ def tile_plate_centred_gene_scores_d2_kernel(tc, x_bytes, x_scale, w_bytes, w_sc
         nc.sync.dma_start(out=means_rows[:], in_=means)
         nc.sync.dma_start(out=xs_rest[:], in_=x_scales[:, 2 * C :])
         nc.sync.dma_start(out=gain_col[:], in_=gain.rearrange("(p c) -> p c", p=P))
-        load_x(2, 2)
         load_w(1)
-        load_x(4, 2)
+        load_x(2, 2)
         load_w(2)
-        for r in range(6, R, 2):
+        for r in range(4, R, 2):
             load_x(r, 2)
 
-        taken = {}
-
-        def take(name, ring):
-            taken[name] = taken.get(name, -1) + 1
-            return ring[taken[name] % len(ring)]
 
         def block(r, c):
-            scales, row = (xs_first, r) if r < 2 else (xs_rest, r - 2)
+            scales, row = (xs_minus if NEGATED else xs_first, r) if r < 2 else (xs_rest, r - 2)
             return x_raw[r][:, 128 * c : 128 * c + 128].bitcast(F8), scales[:, C * row + c : C * row + c + 1]
 
-        words, turned, widened, interleaved = {}, {}, {}, {}
+        words = {}
 
         def every_second(ap):
             return [ap.bitcast(F32)[:, u : 2 * P : 2] for u in range(2)]
@@ -131,82 +142,58 @@ def tile_plate_centred_gene_scores_d2_kernel(tc, x_bytes, x_scale, w_bytes, w_sc
         def side_by_side(ap):
             return [ap.bitcast(F32)[:, P * u : P * u + P] for u in range(2)]
 
-        def widen_x_vector(r, passes):
-            for g in passes:
-                wide = take("turnable", turnable)
-                reordered = wide[:].rearrange("p (u s e) -> p s u e", u=2, e=2)
-                for q in range(4):
-                    codes, scale = block(r, 4 * g + q)
-                    nc.vector.tensor_scalar(
-                        out=reordered[:, 32 * q : 32 * q + 32, :, :],
-                        in0=codes.rearrange("p (s u e) -> p s u e", u=2, e=2),
-                        scalar1=scale,
-                        scalar2=None,
-                        op0=ALU.mult,
-                    )
-                words[r, g] = side_by_side(wide[:])
+        def slot(r, g):
+            return turnable[(G * r + g) % len(turnable)]
 
-        def widen_x_scalar(r, passes):
-            reorder = r >= REORDER_FROM
-            wide = {}
-            for g in passes:
-                wide[g] = take("unordered", unordered) if reorder else take("turnable", turnable)
-                for q in range(4):
-                    codes, scale = block(r, 4 * g + q)
-                    nc.scalar.activation(out=wide[g][:, 128 * q : 128 * q + 128], in_=codes, func=COPY, scale=scale)
-                words[r, g] = every_second(wide[g][:])
-            if reorder:
-                for g in passes:
-                    reordered = take("turnable", turnable)
-                    nc.scalar.copy(
-                        out=reordered[:].bitcast(F32).rearrange("p (u s) -> p u s", u=2),
-                        in_=wide[g][:].bitcast(F32).rearrange("p (s u) -> p u s", u=2),
-                    )
-                    words[r, g] = side_by_side(reordered[:])
+        def widen_vector(r, g):
+            reordered = slot(r, g)[:].rearrange("p (u s e) -> p s u e", u=2, e=2)
+            for q in range(4):
+                codes, scale = block(r, 4 * g + q)
+                nc.vector.tensor_scalar(
+                    out=reordered[:, 32 * q : 32 * q + 32, :, :],
+                    in0=codes.rearrange("p (s u e) -> p s u e", u=2, e=2),
+                    scalar1=scale,
+                    scalar2=None,
+                    op0=ALU.mult,
+                )
+            words[r, g] = side_by_side(slot(r, g)[:])
 
-        def vector_passes(r):
-            return range(G - (1 if r >= ONE_FROM and r % 2 else 2), G)
+        def widen_scalar(r, g, wide):
+            for q in range(4):
+                codes, scale = block(r, 4 * g + q)
+                nc.scalar.activation(out=wide[:, 128 * q : 128 * q + 128], in_=codes, func=COPY, scale=scale)
+            words[r, g] = every_second(wide[:])
 
-        def scalar_passes(r):
-            return [g for g in range(G) if g not in vector_passes(r)]
+        def reorder(r, g):
+            nc.scalar.copy(
+                out=slot(r, g)[:].bitcast(F32).rearrange("p (u s) -> p u s", u=2),
+                in_=unordered[g][:].bitcast(F32).rearrange("p (s u) -> p u s", u=2),
+            )
+            words[r, g] = side_by_side(slot(r, g)[:])
 
         for g in range(G):
             words[MEANS, g] = every_second(means_rows[:, 512 * g : 512 * g + 512])
 
-        def turn(r):
-            for b in range(2):
-                turned[r, b] = take("turn", turn_banks)
-                for j in range(4):
-                    nc.tensor.transpose(turned[r, b][:, P * j : P * j + P], words[r, 2 * b + j // 2][j % 2], ident[:])
+        def turn(r, b, bank):
+            for j in range(4):
+                nc.tensor.transpose(bank[:, P * j : P * j + P], words[r, 2 * b + j // 2][j % 2], ident[:])
 
-        def collect(r, centres=()):
-            for b in (1, 0):
-                for unit, acc in centres if b == 0 else ():
-                    nc.scalar.copy(out=centre[:, unit[1] : unit[1] + unit[2]], in_=acc[:, : unit[2]])
-                    free_banks.append(acc)
-                nc.scalar.copy(
-                    out=halves(grouped[r])[b].rearrange("p (j s u) -> p j s u", j=2, u=2),
-                    in_=turned[r, b][:].rearrange("p (j u s) -> p j s u", j=2, u=2),
-                )
+        def collect(r, b, bank):
+            nc.scalar.copy(
+                out=halves(grouped[r])[b].rearrange("p (j s u) -> p j s u", j=2, u=2),
+                in_=bank[:].rearrange("p (j u s) -> p j s u", j=2, u=2),
+            )
 
         def quantise_x(r):
             nc.vector.quantize_mx(out=x_codes[r].bitcast(X4), scales=x_exps[r], in_=grouped[r][:])
 
-        def room(wide_tiles, narrow_tiles, part, g):
-            if part == 0:
-                return wide_tiles[g][:]
-            j = G * (part - 1) + g
-            return narrow_tiles[j // 2][:, K // 2 * (j % 2) : K // 2 * (j % 2 + 1)]
-
         def widen_w(part, g):
-            widened[part, g] = room(grouped[G : 2 * G], w_wide, part, g)
-            nc.scalar.copy(out=widened[part, g], in_=w_raw[part, g][:].bitcast(F8))
+            nc.scalar.copy(out=room(grouped[G : 2 * G], narrow_wide, part, g), in_=w_raw[part, g][:].bitcast(F8))
 
-        def interleave_w(part, g):
+        def weave_w(part, g):
             c0, n = PARTS[part]
-            interleaved[part, g] = room(grouped[3 * G :], grouped[2 * G :], part, g)
-            src = widened[part, g].rearrange("p (t c i) -> p c t i", t=4, i=4)
-            dst = interleaved[part, g].rearrange("p (c i t) -> p c t i", t=4, i=4)
+            src = room(grouped[G : 2 * G], narrow_wide, part, g).rearrange("p (t c i) -> p c t i", t=4, i=4)
+            dst = room(grouped[3 * G :], grouped[2 * G :], part, g).rearrange("p (c i t) -> p c t i", t=4, i=4)
             for j in range(n // 128):
                 d = c0 // 128 + j
                 nc.vector.tensor_scalar(
@@ -219,193 +206,446 @@ def tile_plate_centred_gene_scores_d2_kernel(tc, x_bytes, x_scale, w_bytes, w_sc
 
         def quantise_w(part, g):
             c0, n = PARTS[part]
-            nc.vector.quantize_mx(out=w_codes[g][:, c0 : c0 + n].bitcast(X4), scales=w_exps[g][:, c0 : c0 + n], in_=interleaved[part, g])
+            woven = room(grouped[3 * G :], grouped[2 * G :], part, g)
+            nc.vector.quantize_mx(out=w_codes[g][:, c0 : c0 + n].bitcast(X4), scales=w_exps[g][:, c0 : c0 + n], in_=woven)
 
-        def multiply(unit, acc, passes):
-            rows, c0, n = unit
-            for j, r in enumerate(rows):
-                for g in passes:
-                    nc.tensor.matmul_mx(
-                        out=acc[:, n * j : n * j + n],
-                        lhsT=x_codes[r][:, P * g : P * g + P].bitcast(X4),
-                        lhsT_scale=x_exps[r][:, P * g : P * g + P],
-                        rhs=w_codes[g][:, c0 : c0 + n].bitcast(X4),
-                        rhs_scale=w_exps[g][:, c0 : c0 + n],
-                        start=(g == 0),
-                        stop=(g == G - 1),
-                    )
-            return unit, acc
+        def multiply(r, c0, n, g, acc, start, stop):
+            nc.tensor.matmul_mx(
+                out=acc,
+                lhsT=x_codes[r][:, P * g : P * g + P].bitcast(X4),
+                lhsT_scale=x_exps[r][:, P * g : P * g + P],
+                rhs=w_codes[g][:, c0 : c0 + n].bitcast(X4),
+                rhs_scale=w_exps[g][:, c0 : c0 + n],
+                start=start,
+                stop=stop,
+            )
 
         def shaped(ap, unit):
             rows, c0, n = unit
             return ap[:, : n * len(rows)].rearrange("p (j n) -> p j n", n=n) if len(rows) > 1 else ap[:, :n]
 
+        def pair_home(unit):
+            rows, c0, n = unit
+            return grouped[rows[0]][:].bitcast(F32).rearrange("p (j n) -> p j n", j=2)[:, :, c0 - BANK : c0 - BANK + n]
+
         def columns(ap, unit):
             rows, c0, n = unit
             return ap[:, c0 : c0 + n].unsqueeze(1).to_broadcast([P, len(rows), n]) if len(rows) > 1 else ap[:, c0 : c0 + n]
 
-        spare = []
+        def copy_centre(unit, acc):
+            nc.scalar.copy(out=centre[:, unit[1] : unit[1] + unit[2]], in_=acc[:, : unit[2]])
+
+        diff, result = {}, {}
 
         def subtract(unit, acc):
-            if not spare:
-                taken["diff"] = taken.get("diff", -1) + 1
-                spare.append(keep.tile([P, BANK], F32, name="diff%d" % taken["diff"])[:])
-            diff = spare.pop(0)
-            nc.vector.tensor_tensor(out=shaped(diff, unit), in0=shaped(acc, unit), in1=columns(centre, unit), op=ALU.subtract)
-            free_banks.append(acc)
-            return unit, diff
+            dst = pair_home(unit) if len(unit[0]) > 1 else shaped(diff[unit], unit)
+            if unit[0][0] < NEGATED:
+                nc.vector.scalar_tensor_tensor(out=dst, in0=shaped(acc, unit), scalar=-1.0, in1=columns(centre, unit), op0=ALU.mult, op1=ALU.subtract)
+            else:
+                nc.vector.tensor_tensor(out=dst, in0=shaped(acc, unit), in1=columns(centre, unit), op=ALU.subtract)
 
-        def store(unit, result):
+        def gain_fused(unit, acc):
+            nc.vector.scalar_tensor_tensor(out=shaped(result[unit], unit), in0=shaped(acc, unit), scalar=-1.0, in1=columns(gain_sbuf, unit), op0=ALU.mult, op1=ALU.mult)
+
+        def gain_vector(unit):
+            nc.vector.tensor_tensor(out=shaped(result[unit], unit), in0=shaped(diff[unit], unit), in1=columns(gain_psum, unit), op=ALU.mult)
+
+        def gain_gpsimd(unit):
+            nc.gpsimd.tensor_tensor(out=shaped(result[unit], unit), in0=shaped(diff[unit], unit), in1=columns(gain_sbuf, unit), op=ALU.mult)
+
+        def store(unit):
             rows, c0, n = unit
             dst = out_rows[:, rows[0] : rows[0] + len(rows), c0 : c0 + n] if len(rows) > 1 else out_rows[:, rows[0], c0 : c0 + n]
-            nc.sync.dma_start(out=dst, in_=shaped(result, unit))
+            nc.sync.dma_start(out=dst, in_=shaped(result[unit], unit))
 
-        def gain_vector(unit, diff):
-            nc.vector.tensor_tensor(out=shaped(diff, unit), in0=shaped(diff, unit), in1=columns(gain_psum, unit), op=ALU.mult)
-            store(unit, diff)
+        def spread_scales():
+            nc.tensor.transpose(banks[2][:, :P], ws_col[:].to_broadcast([P, P]), ident[:])
 
-        def gain_gpsimd(unit, diff, result):
-            nc.gpsimd.tensor_tensor(out=result, in0=diff, in1=columns(gain_sbuf, unit), op=ALU.mult)
+        def spread_gain():
+            for c in range(4):
+                nc.tensor.transpose(gain_words[:, c:BANK:4], gain_col[:].bitcast(F32)[:, c : c + 1].to_broadcast([P, P]), ident[:])
 
-        def jobs_of(i):
-            if i < THIRD_READY:
-                return [(1, i - 2)]
-            return [(2, 2 * (i - THIRD_READY) + j) for j in range(2)] if i < FOURTH_READY else []
+        def copy_gain():
+            nc.scalar.copy(out=gain_sbuf[:].bitcast(F32), in_=gain_words[:])
 
-        spread = take("turn", turn_banks)
-        nc.tensor.transpose(spread[:, :P], ws_col[:].to_broadcast([P, P]), ident[:])
-        nc.vector.tensor_reduce(out=quadrant[:], in_=ident[:].rearrange("p (q j) -> p q j", q=4), op=ALU.add, axis=mybir.AxisListType.X)
-        widen_x_vector(0, range(2))
-        nc.vector.tensor_tensor(
-            out=picked[:],
-            in0=spread[:, :P].rearrange("p (g q d) -> p g d q", g=G, q=4),
-            in1=quadrant[:].unsqueeze(1).unsqueeze(1).to_broadcast([P, G, N // 128, 4]),
-            op=ALU.mult,
-        )
-        widen_x_vector(0, range(2, 3))
-        nc.vector.tensor_reduce(out=ws[:], in_=picked[:], op=ALU.add, axis=mybir.AxisListType.X)
-        widen_x_vector(0, range(3, G))
-        turn(0)
-        first = [(((0,), 0, BANK), free_banks.pop(0)), (((MEANS,), 0, BANK), free_banks.pop(0))]
-        widen_w(0, 0)
-        widen_w(0, 1)
-        collect(0)
-        widen_w(0, 2)
-        interleave_w(0, 0)
-        widen_w(0, 3)
-        turn(MEANS)
-        widen_x_scalar(1, scalar_passes(1))
-        collect(MEANS)
-        interleave_w(0, 1)
-        quantise_w(0, 0)
-        quantise_x(0)
-        interleave_w(0, 2)
-        quantise_w(0, 1)
-        multiply(*first[0], range(2))
-        widen_x_vector(1, vector_passes(1))
-        turn(1)
-        for c in range(4):
-            nc.tensor.transpose(gain_words[:, c:BANK:4], gain_col[:].bitcast(F32)[:, c : c + 1].to_broadcast([P, P]), ident[:])
-        interleave_w(0, 3)
-        quantise_w(0, 2)
-        multiply(*first[0], range(2, 3))
-        for job in jobs_of(2):
-            widen_w(*job)
-        widen_x_scalar(2, scalar_passes(2))
-        collect(1)
-        quantise_x(MEANS)
-        multiply(*first[1], range(2))
-        widen_x_vector(2, vector_passes(2))
-        turn(2)
-        multiply(*first[1], range(2, 3))
-        quantise_w(0, 3)
+        def mark_quadrants():
+            nc.vector.tensor_reduce(out=quadrant[:], in_=ident[:].rearrange("p (q j) -> p q j", q=4), op=ALU.add, axis=mybir.AxisListType.X)
 
-        paced = 2 + PAIRED + (R - 1 - PAIRED) + (R + 1 - THIRD_READY) - HELD
-        due, full, waiting, given = [], [], [], 0
-        later = halves(grouped[0])
-        for i in range(2, R + 1):
-            tile = i - 1
-            fresh = [((i - 2,), c0, BANK) for c0 in range(0, N if i >= FOURTH_READY else BANK, BANK)] if i > 2 else []
-            if i in (THIRD_READY, FOURTH_READY):
-                c0 = PARTS[1 if i == THIRD_READY else 2][0]
-                pairs = [((r, r + 1), c0, QUARTER) for r in range(0, PAIRED, 2)]
-                wholes = [((r,), BANK, BANK) for r in range(PAIRED, i - 2)]
-                fresh = [((MEANS,), c0, QUARTER)] + pairs[:1] + fresh[:1] + wholes + pairs[1:] + fresh[1:]
-            due = due + fresh
-            if i > 3:
-                turn(tile)
+        def negate_scales():
+            nc.vector.tensor_scalar(out=xs_minus[:], in0=xs_first[:], scalar1=-1.0, scalar2=None, op0=ALU.mult)
 
-            centres = [(unit, acc) for unit, acc in full if unit[0][0] == MEANS]
-            held = [(unit, acc) for unit, acc in full if unit[0][0] != MEANS and unit[1] in [c[0][1] for c in centres]]
-            for unit, acc in reversed(full):
-                if (unit, acc) not in centres + held:
-                    waiting.append(subtract(unit, acc))
-            if i > 2:
-                collect(tile, centres)
+        def pick_scales():
+            nc.vector.tensor_tensor(
+                out=picked[:],
+                in0=banks[2][:, :P].rearrange("p (g q d) -> p g d q", g=G, q=4),
+                in1=quadrant[:].unsqueeze(1).unsqueeze(1).to_broadcast([P, G, N // 128, 4]),
+                op=ALU.mult,
+            )
 
-            if i == 2:
-                full = [multiply(unit, acc, range(G - 1, G)) for unit, acc in first]
+        def sum_scales():
+            nc.vector.tensor_reduce(out=ws[:], in_=picked[:], op=ALU.add, axis=mybir.AxisListType.X)
+
+        queues = {"tensor": [], "vector": [], "scalar": [], "gpsimd": [], "sync": []}
+
+        def put(engine, name, needs, call, *args):
+            queues[engine].append((name, needs, call, args))
+
+        last_user = {}
+
+        def claim(bank, name):
+            before = [last_user[bank]] if bank in last_user else []
+            last_user[bank] = name
+            return before
+
+        def v_passes(r):
+            return range(G - V_PASSES[r], G)
+
+        def s_passes(r):
+            return [g for g in range(G) if g not in v_passes(r)]
+
+        def freed(r, g):
+            return [("turn", r - 4, g // 2)] if r >= 4 else []
+
+        def put_widen_vector(r):
+            for g in v_passes(r):
+                put("vector", ("x", r, g), freed(r, g), widen_vector, r, g)
+
+        def put_widen_scalar(r, reorders):
+            again = s_passes(r)[:reorders]
+            for g in s_passes(r):
+                if g in again:
+                    put("scalar", ("xs", r, g), [], widen_scalar, r, g, unordered[g])
+                else:
+                    put("scalar", ("x", r, g), freed(r, g), widen_scalar, r, g, slot(r, g))
+            for g in again:
+                put("scalar", ("x", r, g), freed(r, g), reorder, r, g)
+
+        pair_of, bank_of = {}, {}
+
+        def put_turn(r, b, bank):
+            pair_of[r, b] = banks[bank]
+            needs = claim(bank, ("collect", r, b)) + ([("x", r, g) for g in (2 * b, 2 * b + 1)] if r != MEANS else [])
+            put("tensor", ("turn", r, b), needs, turn, r, b, pair_of[r, b])
+
+        def put_collect(r, b):
+            put("scalar", ("collect", r, b), [("turn", r, b)] + staged_in(r), collect, r, b, pair_of[r, b])
+
+        def put_quantise(r):
+            put("vector", ("qx", r), [("collect", r, 0), ("collect", r, 1)], quantise_x, r)
+
+        def parts_of(unit):
+            return [j for j, (c0, n) in enumerate(PARTS) if c0 < unit[1] + unit[2] and unit[1] < c0 + n]
+
+        def centres_of(unit):
+            return [("out", ((MEANS,),) + PARTS[j]) for j in parts_of(unit)]
+
+        fused = set()
+
+        def put_multiply(unit, passes, bank=None):
+            rows, c0, n = unit
+            if bank is not None:
+                bank_of[unit] = banks[bank]
+            for j, r in enumerate(rows):
+                for g in passes:
+                    who = MEANS if g >= G else r
+                    needs = [("qx", who)] + [("qw", part, g % G) for part in parts_of(unit)]
+                    if j == 0 and bank is not None and g == passes[0]:
+                        needs = needs + claim(bank, ("out", unit))
+                    last = 2 * G - 1 if unit in fused else G - 1
+                    put("tensor", ("mm", unit, r, g), needs, multiply, who, c0, n, g % G, bank_of[unit][:, n * j : n * j + n], g == 0, g == last)
+
+        def put_centre(unit):
+            put("scalar", ("out", unit), [("mm", unit, MEANS, G - 1)], copy_centre, unit, bank_of[unit])
+
+        spare = [half for done in [] for half in halves(done)]
+        spare_whole = {}
+        extra.append(means_rows)
+        whole_home = {r: grouped[r] for r in range(R)}
+        lent = set()
+        made_by, second = {}, {}
+
+        def home(unit):
+            rows, c0, n = unit
+            place = (rows[0], c0 // BANK)
+            if rows[0] < PAIRED:
+                return halves(grouped[rows[0] // 2 * 2 + 1])[rows[0] % 2]
+            if n < BANK:
+                if place not in second:
+                    second[place] = home((rows, place[1] * BANK, BANK))
+                return second[place][:, c0 % BANK : c0 % BANK + n]
+            if (place[0], "whole") in lent:
+                if place[0] not in spare_whole:
+                    spare_whole[place[0]] = extra.pop()
+                    whole_home[place[0]] = spare_whole[place[0]]
+                return halves(spare_whole[place[0]])[place[1]]
+            return spare.pop(0) if place in lent else halves(grouped[place[0]])[place[1]]
+
+        def put_subtract(unit):
+            if unit in fused:
+                result[unit] = home(unit)
+                put("vector", ("out", unit), [("mm", unit, unit[0][-1], 2 * G - 1), "gain copy"], gain_fused, unit, bank_of[unit])
+                put("sync", ("store", unit), [("out", unit)], store, unit)
+                return
+            if len(unit[0]) > 1:
+                for j, r in enumerate(unit[0]):
+                    diff[(r,), BANK, BANK] = halves(grouped[unit[0][0]])[j]
+                    made_by[(r,), BANK, BANK] = ("out", unit)
             else:
-                count = min(len(due), len(free_banks), 3)
-                if i >= THIRD_READY:
-                    count = min(count, -(-paced * (i + 1 - THIRD_READY) // (R + 1 - THIRD_READY)) - given)
-                    given += count
-                full = [multiply(unit, free_banks.pop(0), range(G)) for unit in due[:count]]
-                due = due[count:]
+                diff[unit] = home(unit)
+            put("vector", ("out", unit), [("mm", unit, unit[0][-1], G - 1)] + centres_of(unit), subtract, unit, bank_of[unit])
 
-            for job in jobs_of(i):
-                interleave_w(*job)
-            if i == 2:
-                quantise_x(tile)
-            elif i < R:
-                widen_x_vector(i, vector_passes(i))
-            for job in reversed(jobs_of(i)):
-                quantise_w(*job)
-            if i > 2:
-                quantise_x(tile)
-            for unit, acc in held:
-                waiting.append(subtract(unit, acc))
-            for job in jobs_of(i + 1):
-                widen_w(*job)
-            if i + 1 < R:
-                widen_x_scalar(i + 1, scalar_passes(i + 1))
-            if i == THIRD_READY - 1:
-                nc.scalar.copy(out=gain_sbuf[:].bitcast(F32), in_=gain_words[:])
+        def put_gain_vector(unit):
+            result[unit] = diff[unit]
+            put("vector", ("gain", unit), [made_by.get(unit, ("out", unit)), "gain"], gain_vector, unit)
+            put_store(unit)
 
-            mine = len(full) - 1 if i >= FOURTH_READY else 0
-            stretch = mine + len(held) + len([unit for unit, acc in full if unit[0][0] != MEANS])
-            theirs = [w for w in waiting if w[0][2] == BANK][: 2 * stretch // 5 if i > THIRD_READY else 0]
-            results = halves(grouped[tile])[:1] + [diff for unit, diff in theirs[1:]]
-            for (unit, diff), result in zip(theirs, results):
-                gain_gpsimd(unit, diff, result)
-            waiting = [w for w in waiting if w not in theirs]
-            chosen = sorted(waiting, key=lambda w: (w[0] in [unit for unit, acc in held], w[0][2]))[:mine]
-            for unit, diff in chosen:
-                gain_vector(unit, diff)
-            waiting = [w for w in waiting if w not in chosen]
-            for (unit, diff), result in zip(theirs, results):
-                store(unit, result)
+        def put_gain_gpsimd(unit, behind=None):
+            result[unit] = diff[unit]
+            needs = [made_by.get(unit, ("out", unit)), "gain copy"]
+            if behind is not None:
+                lent.add((behind, 1))
+                result[unit] = halves(grouped[behind])[1]
+                needs = needs + [("qx", behind)]
+            put("gpsimd", ("gain", unit), needs, gain_gpsimd, unit)
 
-            spare.extend(later)
-            later = halves(grouped[tile])[1 if theirs else 0 :]
-            if i == FOURTH_READY:
-                later = later + [half for done in [means_rows] + w_wide for half in halves(done)]
+        def put_gain_wide(r, behind=None):
+            unit = ((r,), 0, N)
+            diff[unit] = result[unit] = whole_home[r][:].bitcast(F32)
+            needs = [("out", ((r,), 0, BANK)), ("out", ((r,), BANK, BANK)), "gain copy"]
+            if behind is not None:
+                result[unit] = grouped[behind][:].bitcast(F32)
+                needs = needs + [("qx", behind)]
+            put("gpsimd", ("gain", unit), needs, gain_gpsimd, unit)
 
-        free_banks.extend(turn_banks)
-        due = due + [((R - 1,), c0, n) for c0, n in PARTS]
-        gpsimd_turn = True
-        while full or due:
-            if due and free_banks:
-                full.append(multiply(due.pop(0), free_banks.pop(0), range(G)))
-                continue
-            unit, diff = subtract(*full.pop(0))
-            if waiting:
-                gain_vector(*waiting.pop(0))
-            if gpsimd_turn and len(full) + len(due) >= 2:
-                gain_gpsimd(unit, diff, diff)
-                store(unit, diff)
+        def put_store(unit):
+            put("sync", ("store", unit), [("gain", unit)], store, unit)
+
+        def put_w(engine, h, g):
+            if engine == "scalar":
+                put("scalar", ("ww", h, g), [], widen_w, h, g)
+            elif engine == "weave":
+                put("vector", ("iw", h, g), [("ww", h, g), "ws"], weave_w, h, g)
             else:
-                waiting.append((unit, diff))
-            gpsimd_turn = not gpsimd_turn
-        for unit, diff in waiting:
-            gain_vector(unit, diff)
+                put("vector", ("qw", h, g), [("iw", h, g)], quantise_w, h, g)
+
+
+        def half(r, h):
+            return (r,), BANK * h, BANK
+
+        def pair(r, part):
+            return ((r, r + 1),) + PARTS[part]
+
+        def middle(part):
+            return ((MEANS,),) + PARTS[part]
+
+        turn_ring, acc_ring = [0, 1, 2], [3, 4, 5, 6]
+
+        def rotate(ring):
+            ring.append(ring.pop(0))
+            return ring[-1]
+
+        def put_turns(*row_halves):
+            for r, b in row_halves:
+                put_turn(r, b, rotate(turn_ring))
+
+        def put_units(*units):
+            for unit in units:
+                put_multiply(unit, range(2 * G if unit in fused else G), rotate(acc_ring))
+
+        def both(r):
+            return [(r, 0), (r, 1)]
+
+        fused.update(half(r, 0) for r in range(NEGATED))
+        late_halves = [(r, b) for r in range(RUNS_FROM, R) for b in range(2)]
+        runs = [late_halves[j : j + 3] for j in range(0, len(late_halves), 3)]
+        late_units = [half(r, h) for r in range(RUNS_FROM - 2, R - 1) for h in range(2)]
+        last_units = [((R - 1,), c0, QUARTER) for c0 in range(0, N, QUARTER)]
+
+        put("tensor", "spread", claim(2, "picked"), spread_scales)
+        put_turns(*both(0), *both(MEANS))
+        put_multiply(half(0, 0), [0, 1], rotate(acc_ring))
+        put_turns(*both(1))
+        put("tensor", "gain", [], spread_gain)
+        put_multiply(half(0, 0), [2, G, G + 1])
+        put_turns(*both(2))
+        put_multiply(half(0, 0), [G + 2, 3, G + 3])
+        put_units(half(1, 0), middle(0))
+        put_turns(*both(3))
+        put_units(half(2, 0), middle(1), pair(0, 1))
+        put_turns(*both(4))
+        put_units(half(3, 0), pair(2, 1), half(4, 0))
+        put_turns(*both(5))
+        put_units(middle(2), pair(0, 2))
+        put_turns(*both(6))
+        put_units(pair(2, 2), half(4, 1))
+        for j, run in enumerate(runs):
+            put_turns(*run)
+            put_units(*late_units[3 * j : 3 * j + 3])
+        put_units(late_units[3 * len(runs)])
+        acc_ring = turn_ring[:2][::-1] + acc_ring
+        put_units(*late_units[3 * len(runs) + 1 :], *last_units)
+
+        def put_collects(*row_halves):
+            for r, b in row_halves:
+                put_collect(r, b)
+
+        def later_first(r):
+            return both(r)[::-1]
+
+        def put_w_jobs(kind, part, passes):
+            for g in passes:
+                put_w(kind, part, g)
+
+        put_w_jobs("scalar", 0, [0, 1])
+        put_collects(*later_first(0))
+        put_w_jobs("scalar", 0, [2, 3])
+        put_widen_scalar(1, 0)
+        put_collects(*later_first(MEANS))
+        put_w_jobs("scalar", 1, [0, 1])
+        put_widen_scalar(2, 0)
+        put_collects(*later_first(1))
+        put_w_jobs("scalar", 1, [2, 3])
+        put_widen_scalar(3, 0)
+        put("scalar", "gain copy", ["gain"], copy_gain)
+        put_collects(*later_first(2))
+        put_w_jobs("scalar", 2, [0, 1])
+        put_centre(middle(0))
+        put_widen_scalar(4, 0)
+        put_collects(*later_first(3))
+        put_w_jobs("scalar", 2, [2, 3])
+        put_centre(middle(1))
+        put_collects(*later_first(4))
+        put_widen_scalar(5, 0)
+        put_widen_scalar(6, 0)
+        put_collects(*later_first(5))
+        put_centre(middle(2))
+        put_widen_scalar(7, 0)
+        put_collects(*later_first(6))
+        to_widen = list(range(RUNS_FROM + 1, R))
+        put_widen_scalar(to_widen.pop(0), G)
+        for j, run in enumerate(runs):
+            put_collects(*run)
+            for r in to_widen[: 2 - j % 2]:
+                put_widen_scalar(r, G)
+            to_widen = to_widen[2 - j % 2 :]
+
+        for r in (5, 6, 9, 12, 15):
+            lent.add((r, "whole"))
+        put("vector", "minus", [], negate_scales)
+        put("vector", "quadrant", [], mark_quadrants)
+        put("vector", ("x", 0, 0), [], widen_vector, 0, 0)
+        put("vector", ("x", 0, 1), [], widen_vector, 0, 1)
+        put("vector", "picked", ["spread"], pick_scales)
+        put("vector", ("x", 0, 2), [], widen_vector, 0, 2)
+        put("vector", "ws", [], sum_scales)
+        put("vector", ("x", 0, 3), [], widen_vector, 0, 3)
+        put_w_jobs("weave", 0, [0, 1])
+        put_w("q", 0, 0)
+        put_quantise(0)
+        put_w("weave", 0, 2)
+        put_w("q", 0, 1)
+        put_widen_vector(1)
+        put_w("weave", 0, 3)
+        put_w("q", 0, 2)
+        put_quantise(MEANS)
+        put_widen_vector(2)
+        put_w("q", 0, 3)
+        put_w_jobs("weave", 1, [0, 1])
+        put_quantise(1)
+        put_w_jobs("q", 1, [1, 0])
+        put_w_jobs("weave", 1, [2, 3])
+        put_widen_vector(3)
+        put_w_jobs("q", 1, [3, 2])
+        put_quantise(2)
+        put_subtract(half(1, 0))
+        put_subtract(half(0, 0))
+        put_w_jobs("weave", 2, [0, 1])
+        put_widen_vector(4)
+        put_w_jobs("q", 2, [1, 0])
+        put_quantise(3)
+        put_subtract(half(2, 0))
+        put_w_jobs("weave", 2, [2, 3])
+        put_quantise(4)
+        put_w_jobs("q", 2, [3, 2])
+        put_widen_vector(5)
+        put_subtract(pair(0, 1))
+        put_subtract(half(3, 0))
+        put_widen_vector(6)
+        put_widen_vector(7)
+        put_subtract(pair(2, 1))
+        put_quantise(5)
+        put_gain_gpsimd(half(2, 0), behind=5)
+        put_gain_gpsimd(half(3, 0))
+        put_subtract(half(4, 0))
+        put_subtract(pair(0, 2))
+        put_gain_vector(half(4, 0))
+        put_subtract(pair(2, 2))
+        put_gain_vector(half(0, 1))
+        put_store(half(2, 0))
+        put_store(half(3, 0))
+        put_widen_vector(8)
+        put_widen_vector(9)
+        put_quantise(6)
+        put_gain_gpsimd(half(1, 1), behind=6)
+        put_gain_gpsimd(half(2, 1))
+        put_subtract(half(4, 1))
+        put_gain_vector(half(3, 1))
+        put_subtract(half(5, 0))
+        put_gain_vector(half(4, 1))
+        put_subtract(half(5, 1))
+        put_store(half(1, 1))
+        put_store(half(2, 1))
+        full = late_units[2:]
+        for a in (7, 10):
+            put_quantise(a)
+            for r in range(a + 3, a + 6):
+                put_widen_vector(r)
+            put_quantise(a + 1)
+            put_quantise(a + 2)
+            put_gain_wide(a - 2, behind=a + 2)
+            put_subtract(full.pop(0))
+            put_subtract(full.pop(0))
+            put_gain_wide(a - 1)
+            put_subtract(full.pop(0))
+            put_subtract(full.pop(0))
+            mine = [half(r, h) for r in range(a, a + (1 if a == 7 else 2)) for h in range(2)]
+            for j, unit in enumerate(mine):
+                put_gain_vector(unit)
+                if j < 3:
+                    put_subtract(full.pop(0))
+            put_store(((a - 2,), 0, N))
+            put_store(((a - 1,), 0, N))
+        put_quantise(13)
+        put_quantise(14)
+        put_subtract(full.pop(0))
+        put_quantise(15)
+        put_gain_wide(12, behind=15)
+        put_subtract(half(13, 0))
+        put_subtract(half(13, 1))
+        put_gain_vector(half(13, 0))
+        put_store(((12,), 0, N))
+        put_subtract(half(14, 0))
+        put_gain_gpsimd(half(14, 0))
+        put_gain_vector(half(13, 1))
+        put_subtract(half(14, 1))
+        put_gain_gpsimd(half(14, 1))
+        put_subtract(last_units[0])
+        put_store(half(14, 0))
+        for j in range(1, len(last_units)):
+            put_subtract(last_units[j])
+            if j == len(last_units) - 1:
+                put_store(half(14, 1))
+            put_gain_vector(last_units[j - 1])
+        put_gain_vector(last_units[-1])
+
+
+        done = set()
+        while any(queues.values()):
+            moved = False
+            for steps in queues.values():
+                while steps and all(need in done for need in steps[0][1]):
+                    name, needs, call, args = steps.pop(0)
+                    call(*args)
+                    done.add(name)
+                    moved = True
+            assert moved, [steps[0][:2] for steps in queues.values() if steps]

@@ -27,8 +27,10 @@ MEANS = R
 PARTS = [(0, BANK), (BANK, QUARTER), (BANK + QUARTER, QUARTER)]
 PAIRED = 4
 NEGATED = 2
-V_PASSES = [4,2,2,2,2,2,1,2,2,2,2,2,2,2,2,1]
-RUNS_FROM = 7
+RUNS_FROM = 6
+RELEASES = (5, 8, 11, 14, 15)
+V_PASSES = [4,2,2,1,2,2,2,2,1,2,2,0,2,2,0,2]
+REORDERED = [0,0,0,0,0,0,1,2,2,2,0,1,2,0,1,2]
 
 
 def tile_plate_centred_gene_scores_d2_kernel(tc, x_bytes, x_scale, w_bytes, w_scale, means, gain, out):
@@ -59,9 +61,7 @@ def tile_plate_centred_gene_scores_d2_kernel(tc, x_bytes, x_scale, w_bytes, w_sc
         turnable = tiles("xt", 4 * G, [P, 512], BF16)
         unordered = tiles("xs", G, [P, 512], BF16)
         grouped = tiles("xg", R + 1, [P, K], BF16)
-        extra = tiles("ww", G, [P, K], BF16)
-
-        narrow_wide = list(extra)
+        narrow_wide = tiles("ww", G, [P, K], BF16)
 
         def room(wide_tiles, narrow_tiles, part, g):
             if part == 0:
@@ -311,8 +311,8 @@ def tile_plate_centred_gene_scores_d2_kernel(tc, x_bytes, x_scale, w_bytes, w_sc
                 put("vector", ("x", r, g), freed(r, g), widen_vector, r, g)
 
         def put_widen_scalar(r, reorders):
-            again = s_passes(r)[:reorders]
-            for g in s_passes(r):
+            again = s_passes(r)[::-1][:reorders][::-1]
+            for g in again + [g for g in s_passes(r) if g not in again]:
                 if g in again:
                     put("scalar", ("xs", r, g), [], widen_scalar, r, g, unordered[g])
                 else:
@@ -339,7 +339,7 @@ def tile_plate_centred_gene_scores_d2_kernel(tc, x_bytes, x_scale, w_bytes, w_sc
         def centres_of(unit):
             return [("out", ((MEANS,),) + PARTS[j]) for j in parts_of(unit)]
 
-        fused = set()
+        fused, issued = set(), {}
 
         def put_multiply(unit, passes, bank=None):
             rows, c0, n = unit
@@ -351,34 +351,24 @@ def tile_plate_centred_gene_scores_d2_kernel(tc, x_bytes, x_scale, w_bytes, w_sc
                     needs = [("qx", who)] + [("qw", part, g % G) for part in parts_of(unit)]
                     if j == 0 and bank is not None and g == passes[0]:
                         needs = needs + claim(bank, ("out", unit))
-                    last = 2 * G - 1 if unit in fused else G - 1
-                    put("tensor", ("mm", unit, r, g), needs, multiply, who, c0, n, g % G, bank_of[unit][:, n * j : n * j + n], g == 0, g == last)
+                    issued[unit, r] = issued.get((unit, r), 0) + 1
+                    total = 2 * G if unit in fused else G
+                    put("tensor", ("mm", unit, r, issued[unit, r] - 1), needs, multiply, who, c0, n, g % G, bank_of[unit][:, n * j : n * j + n], issued[unit, r] == 1, issued[unit, r] == total)
 
         def put_centre(unit):
             put("scalar", ("out", unit), [("mm", unit, MEANS, G - 1)], copy_centre, unit, bank_of[unit])
 
-        spare = [half for done in [] for half in halves(done)]
-        spare_whole = {}
-        extra.append(means_rows)
-        whole_home = {r: grouped[r] for r in range(R)}
-        lent = set()
-        made_by, second = {}, {}
+        spare = [half for done in narrow_wide for half in halves(done)]
+        lent, made_by, homes = set(), {}, {}
 
         def home(unit):
             rows, c0, n = unit
-            place = (rows[0], c0 // BANK)
-            if rows[0] < PAIRED:
-                return halves(grouped[rows[0] // 2 * 2 + 1])[rows[0] % 2]
-            if n < BANK:
-                if place not in second:
-                    second[place] = home((rows, place[1] * BANK, BANK))
-                return second[place][:, c0 % BANK : c0 % BANK + n]
-            if (place[0], "whole") in lent:
-                if place[0] not in spare_whole:
-                    spare_whole[place[0]] = extra.pop()
-                    whole_home[place[0]] = spare_whole[place[0]]
-                return halves(spare_whole[place[0]])[place[1]]
-            return spare.pop(0) if place in lent else halves(grouped[place[0]])[place[1]]
+            r, h = rows[0], c0 // BANK
+            if r < PAIRED:
+                return halves(grouped[r // 2 * 2 + 1])[r % 2]
+            if (r, h) not in homes:
+                homes[r, h] = spare.pop(0) if h == 1 and r in lent else halves(grouped[r])[h]
+            return homes[r, h][:, c0 % BANK : c0 % BANK + n]
 
         def put_subtract(unit):
             if unit in fused:
@@ -403,17 +393,7 @@ def tile_plate_centred_gene_scores_d2_kernel(tc, x_bytes, x_scale, w_bytes, w_sc
             result[unit] = diff[unit]
             needs = [made_by.get(unit, ("out", unit)), "gain copy"]
             if behind is not None:
-                lent.add((behind, 1))
                 result[unit] = halves(grouped[behind])[1]
-                needs = needs + [("qx", behind)]
-            put("gpsimd", ("gain", unit), needs, gain_gpsimd, unit)
-
-        def put_gain_wide(r, behind=None):
-            unit = ((r,), 0, N)
-            diff[unit] = result[unit] = whole_home[r][:].bitcast(F32)
-            needs = [("out", ((r,), 0, BANK)), ("out", ((r,), BANK, BANK)), "gain copy"]
-            if behind is not None:
-                result[unit] = grouped[behind][:].bitcast(F32)
                 needs = needs + [("qx", behind)]
             put("gpsimd", ("gain", unit), needs, gain_gpsimd, unit)
 
@@ -450,40 +430,47 @@ def tile_plate_centred_gene_scores_d2_kernel(tc, x_bytes, x_scale, w_bytes, w_sc
 
         def put_units(*units):
             for unit in units:
-                put_multiply(unit, range(2 * G if unit in fused else G), rotate(acc_ring))
+                put_multiply(unit, range(G), rotate(acc_ring))
 
         def both(r):
             return [(r, 0), (r, 1)]
 
         fused.update(half(r, 0) for r in range(NEGATED))
+        lent.update(RELEASES)
         late_halves = [(r, b) for r in range(RUNS_FROM, R) for b in range(2)]
         runs = [late_halves[j : j + 3] for j in range(0, len(late_halves), 3)]
-        late_units = [half(r, h) for r in range(RUNS_FROM - 2, R - 1) for h in range(2)]
+        late_units = [half(r, h) for r in range(RUNS_FROM - 2, R - 1) for h in range(2)][1:]
         last_units = [((R - 1,), c0, QUARTER) for c0 in range(0, N, QUARTER)]
 
         put("tensor", "spread", claim(2, "picked"), spread_scales)
         put_turns(*both(0), *both(MEANS))
-        put_multiply(half(0, 0), [0, 1], rotate(acc_ring))
-        put_turns(*both(1))
         put("tensor", "gain", [], spread_gain)
-        put_multiply(half(0, 0), [2, G, G + 1])
+        put_multiply(half(0, 0), [0, 1, G, G + 1], rotate(acc_ring))
+        put_multiply(middle(0), [0, 1], rotate(acc_ring))
+        put_turns(*both(1))
+        put_multiply(half(1, 0), [G, G + 1], rotate(acc_ring))
+        put_multiply(half(0, 0), [2, G + 2])
+        put_multiply(middle(0), [2])
         put_turns(*both(2))
-        put_multiply(half(0, 0), [G + 2, 3, G + 3])
-        put_units(half(1, 0), middle(0))
+        acc_ring.insert(0, turn_ring.pop(0))
+        put_multiply(half(1, 0), [G + 2])
+        put_multiply(half(0, 0), [3, G + 3])
+        put_multiply(middle(0), [3])
+        put_multiply(half(1, 0), [G + 3, 0, 1, 2, 3])
         put_turns(*both(3))
-        put_units(half(2, 0), middle(1), pair(0, 1))
+        put_units(middle(1), half(2, 0), pair(0, 1))
         put_turns(*both(4))
         put_units(half(3, 0), pair(2, 1), half(4, 0))
         put_turns(*both(5))
-        put_units(middle(2), pair(0, 2))
-        put_turns(*both(6))
-        put_units(pair(2, 2), half(4, 1))
-        for j, run in enumerate(runs):
+        put_units(middle(2), pair(0, 2), pair(2, 2))
+        turn_ring.append(acc_ring.pop(0))
+        for j, run in enumerate(runs[:-1]):
             put_turns(*run)
             put_units(*late_units[3 * j : 3 * j + 3])
-        put_units(late_units[3 * len(runs)])
+        put_turns(*runs[-1])
+        put_units(*late_units[-3:-1])
         acc_ring = turn_ring[:2][::-1] + acc_ring
-        put_units(*late_units[3 * len(runs) + 1 :], *last_units)
+        put_units(late_units[-1], *last_units)
 
         def put_collects(*row_halves):
             for r, b in row_halves:
@@ -496,41 +483,44 @@ def tile_plate_centred_gene_scores_d2_kernel(tc, x_bytes, x_scale, w_bytes, w_sc
             for g in passes:
                 put_w(kind, part, g)
 
+        def put_x_scalar(*rows):
+            for r in rows:
+                put_widen_scalar(r, REORDERED[r])
+
         put_w_jobs("scalar", 0, [0, 1])
         put_collects(*later_first(0))
         put_w_jobs("scalar", 0, [2, 3])
-        put_widen_scalar(1, 0)
         put_collects(*later_first(MEANS))
+        put_x_scalar(1)
         put_w_jobs("scalar", 1, [0, 1])
-        put_widen_scalar(2, 0)
+        put_x_scalar(2)
         put_collects(*later_first(1))
         put_w_jobs("scalar", 1, [2, 3])
-        put_widen_scalar(3, 0)
-        put("scalar", "gain copy", ["gain"], copy_gain)
         put_collects(*later_first(2))
+        put_x_scalar(3)
+        put("scalar", "gain copy", ["gain"], copy_gain)
         put_w_jobs("scalar", 2, [0, 1])
         put_centre(middle(0))
-        put_widen_scalar(4, 0)
-        put_collects(*later_first(3))
+        put_collects(*both(3))
+        put_x_scalar(4)
         put_w_jobs("scalar", 2, [2, 3])
-        put_centre(middle(1))
         put_collects(*later_first(4))
-        put_widen_scalar(5, 0)
-        put_widen_scalar(6, 0)
-        put_collects(*later_first(5))
+        put_centre(middle(1))
+        put_x_scalar(5, 6)
+        put_collects(*both(5))
         put_centre(middle(2))
-        put_widen_scalar(7, 0)
-        put_collects(*later_first(6))
-        to_widen = list(range(RUNS_FROM + 1, R))
-        put_widen_scalar(to_widen.pop(0), G)
+        put_x_scalar(7)
+        widened = 7
         for j, run in enumerate(runs):
             put_collects(*run)
-            for r in to_widen[: 2 - j % 2]:
-                put_widen_scalar(r, G)
-            to_widen = to_widen[2 - j % 2 :]
+            needed = runs[j + 1][-1][0] if j + 1 < len(runs) else widened
+            put_x_scalar(*range(widened + 1, needed + 1))
+            widened = needed
 
-        for r in (5, 6, 9, 12, 15):
-            lent.add((r, "whole"))
+        def put_x_vector(*rows):
+            for r in rows:
+                put_widen_vector(r)
+
         put("vector", "minus", [], negate_scales)
         put("vector", "quadrant", [], mark_quadrants)
         put("vector", ("x", 0, 0), [], widen_vector, 0, 0)
@@ -544,97 +534,94 @@ def tile_plate_centred_gene_scores_d2_kernel(tc, x_bytes, x_scale, w_bytes, w_sc
         put_quantise(0)
         put_w("weave", 0, 2)
         put_w("q", 0, 1)
-        put_widen_vector(1)
+        put_quantise(MEANS)
+        put_x_vector(1)
         put_w("weave", 0, 3)
         put_w("q", 0, 2)
-        put_quantise(MEANS)
-        put_widen_vector(2)
+        put_x_vector(2)
         put_w("q", 0, 3)
         put_w_jobs("weave", 1, [0, 1])
         put_quantise(1)
         put_w_jobs("q", 1, [1, 0])
         put_w_jobs("weave", 1, [2, 3])
-        put_widen_vector(3)
+        put_x_vector(3)
         put_w_jobs("q", 1, [3, 2])
         put_quantise(2)
-        put_subtract(half(1, 0))
+        put_w("weave", 2, 0)
         put_subtract(half(0, 0))
-        put_w_jobs("weave", 2, [0, 1])
-        put_widen_vector(4)
-        put_w_jobs("q", 2, [1, 0])
+        put_w("weave", 2, 1)
+        put_x_vector(4)
         put_quantise(3)
-        put_subtract(half(2, 0))
+        put_w_jobs("q", 2, [1, 0])
+        put_subtract(half(1, 0))
         put_w_jobs("weave", 2, [2, 3])
         put_quantise(4)
+        put_x_vector(5)
+        put_subtract(half(2, 0))
         put_w_jobs("q", 2, [3, 2])
-        put_widen_vector(5)
         put_subtract(pair(0, 1))
         put_subtract(half(3, 0))
-        put_widen_vector(6)
-        put_widen_vector(7)
+        put_x_vector(6)
         put_subtract(pair(2, 1))
-        put_quantise(5)
-        put_gain_gpsimd(half(2, 0), behind=5)
-        put_gain_gpsimd(half(3, 0))
+        put_x_vector(7)
         put_subtract(half(4, 0))
-        put_subtract(pair(0, 2))
-        put_gain_vector(half(4, 0))
-        put_subtract(pair(2, 2))
-        put_gain_vector(half(0, 1))
-        put_store(half(2, 0))
-        put_store(half(3, 0))
-        put_widen_vector(8)
-        put_widen_vector(9)
-        put_quantise(6)
-        put_gain_gpsimd(half(1, 1), behind=6)
-        put_gain_gpsimd(half(2, 1))
-        put_subtract(half(4, 1))
-        put_gain_vector(half(3, 1))
-        put_subtract(half(5, 0))
-        put_gain_vector(half(4, 1))
-        put_subtract(half(5, 1))
-        put_store(half(1, 1))
-        put_store(half(2, 1))
-        full = late_units[2:]
-        for a in (7, 10):
+        put_x_vector(8)
+
+        full = [pair(0, 2), pair(2, 2)] + late_units + last_units
+        waiting = [half(2, 0), half(3, 0), half(4, 0)]
+
+        def stretch(release, subtractions, theirs, mine):
+            given = []
+            while subtractions or mine or theirs:
+                ready = [unit for unit in waiting if unit[2] == BANK]
+                while theirs and ready:
+                    given.append(ready.pop(0))
+                    waiting.remove(given[-1])
+                    put_gain_gpsimd(given[-1], behind=release if len(given) == 1 else None)
+                    theirs -= 1
+                if subtractions:
+                    unit = full.pop(0)
+                    put_subtract(unit)
+                    subtractions -= 1
+                    fresh = [half(r, 1) for r in unit[0]] if len(unit[0]) > 1 else [unit]
+                else:
+                    fresh = []
+                if mine and waiting and not theirs:
+                    put_gain_vector(waiting.pop(0))
+                    mine -= 1
+                waiting.extend(fresh)
+            for unit in given:
+                put_store(unit)
+
+        put_quantise(5)
+        stretch(5, 4, 2, 2)
+        for a in (6, 9):
             put_quantise(a)
-            for r in range(a + 3, a + 6):
-                put_widen_vector(r)
+            put_x_vector(a + 3, a + 4, a + 5)
             put_quantise(a + 1)
             put_quantise(a + 2)
-            put_gain_wide(a - 2, behind=a + 2)
-            put_subtract(full.pop(0))
-            put_subtract(full.pop(0))
-            put_gain_wide(a - 1)
-            put_subtract(full.pop(0))
-            put_subtract(full.pop(0))
-            mine = [half(r, h) for r in range(a, a + (1 if a == 7 else 2)) for h in range(2)]
-            for j, unit in enumerate(mine):
-                put_gain_vector(unit)
-                if j < 3:
-                    put_subtract(full.pop(0))
-            put_store(((a - 2,), 0, N))
-            put_store(((a - 1,), 0, N))
+            stretch(a + 2, 6, 3 if a == 6 else 4, 4)
+        put_quantise(12)
+        put_x_vector(15)
+        put_gain_vector(waiting.pop(0))
         put_quantise(13)
         put_quantise(14)
-        put_subtract(full.pop(0))
+        stretch(14, 4, 2, 2)
         put_quantise(15)
-        put_gain_wide(12, behind=15)
-        put_subtract(half(13, 0))
-        put_subtract(half(13, 1))
-        put_gain_vector(half(13, 0))
-        put_store(((12,), 0, N))
-        put_subtract(half(14, 0))
-        put_gain_gpsimd(half(14, 0))
-        put_gain_vector(half(13, 1))
-        put_subtract(half(14, 1))
-        put_gain_gpsimd(half(14, 1))
+        put_gain_gpsimd(half(R - 3, 0), behind=R - 1)
+        put_subtract(half(R - 3, 1))
+        put_gain_gpsimd(half(R - 3, 1))
+        put_subtract(half(R - 2, 0))
+        put_store(half(R - 3, 0))
+        put_gain_vector(half(R - 2, 0))
+        put_subtract(half(R - 2, 1))
+        put_gain_gpsimd(half(R - 2, 1))
+        put_store(half(R - 3, 1))
         put_subtract(last_units[0])
-        put_store(half(14, 0))
         for j in range(1, len(last_units)):
             put_subtract(last_units[j])
             if j == len(last_units) - 1:
-                put_store(half(14, 1))
+                put_store(half(R - 2, 1))
             put_gain_vector(last_units[j - 1])
         put_gain_vector(last_units[-1])
 

@@ -29,8 +29,8 @@ PAIRED = 4
 NEGATED = 2
 RUNS_FROM = 6
 RELEASES = (5, 8, 11, 14, 15)
-V_PASSES = [4,2,2,1,2,2,2,2,1,2,2,0,2,2,0,2]
-REORDERED = [0,0,0,0,0,0,1,2,2,2,0,1,2,0,1,2]
+V_PASSES = [4,2,2,2,2,2,2,3,1,2,3,1,2,3,1,2]
+REORDERED = [0,0,0,0,0,0,2,0,2,2,0,2,2,0,2,2]
 
 
 def tile_plate_centred_gene_scores_d2_kernel(tc, x_bytes, x_scale, w_bytes, w_scale, means, gain, out):
@@ -534,8 +534,8 @@ def tile_plate_centred_gene_scores_d2_kernel(tc, x_bytes, x_scale, w_bytes, w_sc
         put_quantise(0)
         put_w("weave", 0, 2)
         put_w("q", 0, 1)
-        put_quantise(MEANS)
         put_x_vector(1)
+        put_quantise(MEANS)
         put_w("weave", 0, 3)
         put_w("q", 0, 2)
         put_x_vector(2)

@@ -29,7 +29,7 @@ PAIRED = 4
 NEGATED = 2
 RUNS_FROM = 6
 RELEASES = (5, 8, 11, 14, 15)
-V_PASSES = [4,2,2,2,2,2,2,3,1,2,3,1,2,3,1,2]
+V_PASSES = [4,2,2,2,2,2,2,2,1,2,3,1,2,3,1,2]
 REORDERED = [0,0,0,0,0,0,2,0,2,2,0,2,2,0,2,2]
 
 
@@ -126,7 +126,9 @@ def tile_plate_centred_gene_scores_d2_kernel(tc, x_bytes, x_scale, w_bytes, w_sc
         load_w(1)
         load_x(2, 2)
         load_w(2)
-        for r in range(4, R, 2):
+        load_x(4, 2)
+        nc.sync.dma_start(out=gain_sbuf[:], in_=gain.partition_broadcast(P))
+        for r in range(6, R, 2):
             load_x(r, 2)
 
 
@@ -265,9 +267,6 @@ def tile_plate_centred_gene_scores_d2_kernel(tc, x_bytes, x_scale, w_bytes, w_sc
             for c in range(4):
                 nc.tensor.transpose(gain_words[:, c:BANK:4], gain_col[:].bitcast(F32)[:, c : c + 1].to_broadcast([P, P]), ident[:])
 
-        def copy_gain():
-            nc.scalar.copy(out=gain_sbuf[:].bitcast(F32), in_=gain_words[:])
-
         def mark_quadrants():
             nc.vector.tensor_reduce(out=quadrant[:], in_=ident[:].rearrange("p (q j) -> p q j", q=4), op=ALU.add, axis=mybir.AxisListType.X)
 
@@ -373,7 +372,7 @@ def tile_plate_centred_gene_scores_d2_kernel(tc, x_bytes, x_scale, w_bytes, w_sc
         def put_subtract(unit):
             if unit in fused:
                 result[unit] = home(unit)
-                put("vector", ("out", unit), [("mm", unit, unit[0][-1], 2 * G - 1), "gain copy"], gain_fused, unit, bank_of[unit])
+                put("vector", ("out", unit), [("mm", unit, unit[0][-1], 2 * G - 1)], gain_fused, unit, bank_of[unit])
                 put("sync", ("store", unit), [("out", unit)], store, unit)
                 return
             if len(unit[0]) > 1:
@@ -391,7 +390,7 @@ def tile_plate_centred_gene_scores_d2_kernel(tc, x_bytes, x_scale, w_bytes, w_sc
 
         def put_gain_gpsimd(unit, behind=None):
             result[unit] = diff[unit]
-            needs = [made_by.get(unit, ("out", unit)), "gain copy"]
+            needs = [made_by.get(unit, ("out", unit))]
             if behind is not None:
                 result[unit] = halves(grouped[behind])[1]
                 needs = needs + [("qx", behind)]
@@ -498,7 +497,6 @@ def tile_plate_centred_gene_scores_d2_kernel(tc, x_bytes, x_scale, w_bytes, w_sc
         put_w_jobs("scalar", 1, [2, 3])
         put_collects(*later_first(2))
         put_x_scalar(3)
-        put("scalar", "gain copy", ["gain"], copy_gain)
         put_w_jobs("scalar", 2, [0, 1])
         put_centre(middle(0))
         put_collects(*both(3))
@@ -600,7 +598,7 @@ def tile_plate_centred_gene_scores_d2_kernel(tc, x_bytes, x_scale, w_bytes, w_sc
             put_x_vector(a + 3, a + 4, a + 5)
             put_quantise(a + 1)
             put_quantise(a + 2)
-            stretch(a + 2, 6, 3 if a == 6 else 4, 4)
+            stretch(a + 2, 6, 4 if a == 6 else 4, 3 if a == 6 else 4)
         put_quantise(12)
         put_x_vector(15)
         put_gain_vector(waiting.pop(0))

from contextlib import ExitStack

import concourse.mybir as mybir
from concourse.masks import make_identity

T, K, N, PLATES = 2048, 2048, 1024, 128
FLOPS = 2 * T * K * N + 2 * PLATES * K * N

F32 = mybir.dt.float32
BF16 = mybir.dt.bfloat16
U32 = mybir.dt.uint32
U8 = mybir.dt.uint8
F8 = mybir.dt.float8_e4m3fn
X4 = mybir.dt.float8_e4m3fn_x4
ALU = mybir.AluOpType
COPY = mybir.ActivationFunctionType.Copy

P = 128
R = T // PLATES
G = K // 512
C = K // 128
BANK = 512
QUARTER = 256
MEANS = R


PARTS = [(0, BANK), (BANK, QUARTER), (BANK + QUARTER, QUARTER)]
PAIRED = 4
NEGATED = 2
RUNS_FROM = 6
RELEASES = (5, 8, 11, 14, 15)
V_PASSES = [4,2,2,2,2,2,2,2,1,2,3,1,2,3,1,2]
REORDERED = [0,0,0,0,0,0,2,0,2,2,0,2,2,0,2,2]


def tile_plate_centred_gene_scores_d2_kernel(tc, x_bytes, x_scale, w_bytes, w_scale, means, gain, out):
    nc = tc.nc
    with ExitStack() as ctx:
        keep = ctx.enter_context(tc.tile_pool(name="keep", bufs=1))
        psum = ctx.enter_context(tc.psum_pool(name="psum", bufs=1))
        ctx.enter_context(tc.manual_schedule())

        def tiles(name, count, shape, dtype):
            return [keep.tile(shape, dtype, name="%s%d" % (name, j), align_bytes=64) for j in range(count)]

        def placed(name, count, width, dtype, skip):
            whole = keep.tile([P, skip + count * width], dtype, name=name, align_bytes=256)
            return [whole[:, skip + j * width : skip + (j + 1) * width] for j in range(count)]

        def halves(tile):
            return [tile[:].bitcast(F32)[:, BANK * h : BANK * h + BANK] for h in range(2)]

        ident = keep.tile([P, P], F32, name="ident")
        make_identity(nc, ident[:])

        gain_words = psum.tile([P, BANK], F32, name="gain_words")
        gain_psum = gain_words[:].bitcast(BF16)
        gain_col = keep.tile([P, N // P], BF16, name="gain_col")
        banks = [psum.tile([P, BANK], F32, name="bank%d" % j) for j in range(7)]

        turnable = tiles("xt", 4 * G, [P, 512], BF16)
        unordered = tiles("xs", G, [P, 512], BF16)
        grouped = tiles("xg", R + 1, [P, K], BF16)
        narrow_wide = tiles("ww", G, [P, K], BF16)

        def room(wide_tiles, narrow_tiles, part, g):
            if part == 0:
                return wide_tiles[g][:]
            c0, n = PARTS[part]
            first = 4 * (G * (c0 - BANK) + g * n)
            return narrow_tiles[first // K][:, first % K : first % K + 4 * n]

        def staged_in(r):
            if G <= r < 2 * G:
                return [("iw", 0, r - G)]
            if 3 * G <= r < R:
                return [("qw", 0, r - 3 * G)]
            if 2 * G <= r < 3 * G:
                return [("qw", part, g) for part in range(1, len(PARTS)) for g in range(G) if 4 * (G * (PARTS[part][0] - BANK) + g * PARTS[part][1]) // K == r - 2 * G]
            return []

        x_codes = placed("xc", R + 1, G * P, U32, 0)
        x_exps = placed("xq", R + 1, G * P, U8, 64)
        w_codes = placed("wc", G, N, U32, 32)
        w_exps = placed("wq", G, N, U8, 192)

        xs_first = keep.tile([P, 2 * C], F32, name="xs_first")
        xs_minus = keep.tile([P, 2 * C], F32, name="xs_minus")
        xs_rest = keep.tile([P, (R - 2) * C], F32, name="xs_rest")
        ws_col = keep.tile([P, 1], F32, name="ws_col")
        ws = keep.tile([P, G, N // 128], F32, name="ws")
        quadrant = keep.tile([P, 4], F32, name="quadrant")
        picked = keep.tile([P, G, N // 128, 4], F32, name="picked")
        gain_sbuf = keep.tile([P, N], BF16, name="gain_sbuf")
        means_rows = keep.tile([P, K], BF16, name="means_rows")
        centre = keep.tile([P, N], F32, name="centre")

        x_rows = x_bytes.rearrange("(p r) k -> p r k", r=R)
        x_scales = x_scale.rearrange("(p r) c -> p (r c)", r=R)
        out_rows = out.rearrange("(p r) n -> p r n", r=R)
        w_raw, x_raw = {}, {}

        def load_w(part):
            c0, n = PARTS[part]
            for g in range(G):
                w_raw[part, g] = keep.tile([P, 4 * n], U8, name="wb%d%d" % (part, g))
                nc.sync.dma_start(
                    out=w_raw[part, g][:].rearrange("p (t n) -> p t n", t=4),
                    in_=w_bytes[512 * g : 512 * g + 512, c0 : c0 + n].rearrange("(p t) n -> p t n", t=4),
                )

        def load_x(r, rows):
            raw = keep.tile([P, rows * K], U8, name="xb%d" % r)
            nc.sync.dma_start(out=raw[:], in_=x_rows[:, r : r + rows, :].rearrange("p r k -> p (r k)"))
            for j in range(rows):
                x_raw[r + j] = raw[:, j * K : (j + 1) * K]

        nc.sync.dma_start(out=ws_col[:], in_=w_scale.rearrange("c (d o) -> (c d) o", o=1))
        nc.sync.dma_start(out=xs_first[:], in_=x_scales[:, : 2 * C])
        load_x(0, 1)
        load_w(0)
        load_x(1, 1)
        nc.sync.dma_start(out=means_rows[:], in_=means)
        nc.sync.dma_start(out=xs_rest[:], in_=x_scales[:, 2 * C :])
        nc.sync.dma_start(out=gain_col[:], in_=gain.rearrange("(p c) -> p c", p=P))
        load_w(1)
        load_x(2, 2)
        load_w(2)
        load_x(4, 2)
        nc.sync.dma_start(out=gain_sbuf[:], in_=gain.partition_broadcast(P))
        for r in range(6, R, 2):
            load_x(r, 2)


        def block(r, c):
            scales, row = (xs_minus if NEGATED else xs_first, r) if r < 2 else (xs_rest, r - 2)
            return x_raw[r][:, 128 * c : 128 * c + 128].bitcast(F8), scales[:, C * row + c : C * row + c + 1]

        words = {}

        def every_second(ap):
            return [ap.bitcast(F32)[:, u : 2 * P : 2] for u in range(2)]

        def side_by_side(ap):
            return [ap.bitcast(F32)[:, P * u : P * u + P] for u in range(2)]

        def slot(r, g):
            return turnable[(G * r + g) % len(turnable)]

        def widen_vector(r, g):
            reordered = slot(r, g)[:].rearrange("p (u s e) -> p s u e", u=2, e=2)
            for q in range(4):
                codes, scale = block(r, 4 * g + q)
                nc.vector.tensor_scalar(
                    out=reordered[:, 32 * q : 32 * q + 32, :, :],
                    in0=codes.rearrange("p (s u e) -> p s u e", u=2, e=2),
                    scalar1=scale,
                    scalar2=None,
                    op0=ALU.mult,
                )
            words[r, g] = side_by_side(slot(r, g)[:])

        def widen_scalar(r, g, wide):
            for q in range(4):
                codes, scale = block(r, 4 * g + q)
                nc.scalar.activation(out=wide[:, 128 * q : 128 * q + 128], in_=codes, func=COPY, scale=scale)
            words[r, g] = every_second(wide[:])

        def reorder(r, g):
            nc.scalar.copy(
                out=slot(r, g)[:].bitcast(F32).rearrange("p (u s) -> p u s", u=2),
                in_=unordered[g][:].bitcast(F32).rearrange("p (s u) -> p u s", u=2),
            )
            words[r, g] = side_by_side(slot(r, g)[:])

        for g in range(G):
            words[MEANS, g] = every_second(means_rows[:, 512 * g : 512 * g + 512])

        def turn(r, b, bank):
            for j in range(4):
                nc.tensor.transpose(bank[:, P * j : P * j + P], words[r, 2 * b + j // 2][j % 2], ident[:])

        def collect(r, b, bank):
            nc.scalar.copy(
                out=halves(grouped[r])[b].rearrange("p (j s u) -> p j s u", j=2, u=2),
                in_=bank[:].rearrange("p (j u s) -> p j s u", j=2, u=2),
            )

        def quantise_x(r):
            nc.vector.quantize_mx(out=x_codes[r].bitcast(X4), scales=x_exps[r], in_=grouped[r][:])

        def widen_w(part, g):
            nc.scalar.copy(out=room(grouped[G : 2 * G], narrow_wide, part, g), in_=w_raw[part, g][:].bitcast(F8))

        def weave_w(part, g):
            c0, n = PARTS[part]
            src = room(grouped[G : 2 * G], narrow_wide, part, g).rearrange("p (t c i) -> p c t i", t=4, i=4)
            dst = room(grouped[3 * G :], grouped[2 * G :], part, g).rearrange("p (c i t) -> p c t i", t=4, i=4)
            for j in range(n // 128):
                d = c0 // 128 + j
                nc.vector.tensor_scalar(
                    out=dst[:, 32 * j : 32 * j + 32, :, :],
                    in0=src[:, 32 * j : 32 * j + 32, :, :],
                    scalar1=ws[:, g, d : d + 1],
                    scalar2=None,
                    op0=ALU.mult,
                )

        def quantise_w(part, g):
            c0, n = PARTS[part]
            woven = room(grouped[3 * G :], grouped[2 * G :], part, g)
            nc.vector.quantize_mx(out=w_codes[g][:, c0 : c0 + n].bitcast(X4), scales=w_exps[g][:, c0 : c0 + n], in_=woven)

        def multiply(r, c0, n, g, acc, start, stop):
            nc.tensor.matmul_mx(
                out=acc,
                lhsT=x_codes[r][:, P * g : P * g + P].bitcast(X4),
                lhsT_scale=x_exps[r][:, P * g : P * g + P],
                rhs=w_codes[g][:, c0 : c0 + n].bitcast(X4),
                rhs_scale=w_exps[g][:, c0 : c0 + n],
                start=start,
                stop=stop,
            )

        def shaped(ap, unit):
            rows, c0, n = unit
            return ap[:, : n * len(rows)].rearrange("p (j n) -> p j n", n=n) if len(rows) > 1 else ap[:, :n]

        def pair_home(unit):
            rows, c0, n = unit
            return grouped[rows[0]][:].bitcast(F32).rearrange("p (j n) -> p j n", j=2)[:, :, c0 - BANK : c0 - BANK + n]

        def columns(ap, unit):
            rows, c0, n = unit
            return ap[:, c0 : c0 + n].unsqueeze(1).to_broadcast([P, len(rows), n]) if len(rows) > 1 else ap[:, c0 : c0 + n]

        def copy_centre(unit, acc):
            nc.scalar.copy(out=centre[:, unit[1] : unit[1] + unit[2]], in_=acc[:, : unit[2]])

        diff, result = {}, {}

        def subtract(unit, acc):
            dst = pair_home(unit) if len(unit[0]) > 1 else shaped(diff[unit], unit)
            if unit[0][0] < NEGATED:
                nc.vector.scalar_tensor_tensor(out=dst, in0=shaped(acc, unit), scalar=-1.0, in1=columns(centre, unit), op0=ALU.mult, op1=ALU.subtract)
            else:
                nc.vector.tensor_tensor(out=dst, in0=shaped(acc, unit), in1=columns(centre, unit), op=ALU.subtract)

        def gain_fused(unit, acc):
            nc.vector.scalar_tensor_tensor(out=shaped(result[unit], unit), in0=shaped(acc, unit), scalar=-1.0, in1=columns(gain_sbuf, unit), op0=ALU.mult, op1=ALU.mult)

        def gain_vector(unit):
            nc.vector.tensor_tensor(out=shaped(result[unit], unit), in0=shaped(diff[unit], unit), in1=columns(gain_psum, unit), op=ALU.mult)

        def gain_gpsimd(unit):
            nc.gpsimd.tensor_tensor(out=shaped(result[unit], unit), in0=shaped(diff[unit], unit), in1=columns(gain_sbuf, unit), op=ALU.mult)

        def store(unit):
            rows, c0, n = unit
            dst = out_rows[:, rows[0] : rows[0] + len(rows), c0 : c0 + n] if len(rows) > 1 else out_rows[:, rows[0], c0 : c0 + n]
            nc.sync.dma_start(out=dst, in_=shaped(result[unit], unit))

        def spread_scales():
            nc.tensor.transpose(banks[2][:, :P], ws_col[:].to_broadcast([P, P]), ident[:])

        def spread_gain():
            for c in range(4):
                nc.tensor.transpose(gain_words[:, c:BANK:4], gain_col[:].bitcast(F32)[:, c : c + 1].to_broadcast([P, P]), ident[:])

        def mark_quadrants():
            nc.vector.tensor_reduce(out=quadrant[:], in_=ident[:].rearrange("p (q j) -> p q j", q=4), op=ALU.add, axis=mybir.AxisListType.X)

        def negate_scales():
            nc.vector.tensor_scalar(out=xs_minus[:], in0=xs_first[:], scalar1=-1.0, scalar2=None, op0=ALU.mult)

        def pick_scales():
            nc.vector.tensor_tensor(
                out=picked[:],
                in0=banks[2][:, :P].rearrange("p (g q d) -> p g d q", g=G, q=4),
                in1=quadrant[:].unsqueeze(1).unsqueeze(1).to_broadcast([P, G, N // 128, 4]),
                op=ALU.mult,
            )

        def sum_scales():
            nc.vector.tensor_reduce(out=ws[:], in_=picked[:], op=ALU.add, axis=mybir.AxisListType.X)

        queues = {"tensor": [], "vector": [], "scalar": [], "gpsimd": [], "sync": []}

        def put(engine, name, needs, call, *args):
            queues[engine].append((name, needs, call, args))

        last_user = {}

        def claim(bank, name):
            before = [last_user[bank]] if bank in last_user else []
            last_user[bank] = name
            return before

        def v_passes(r):
            return range(G - V_PASSES[r], G)

        def s_passes(r):
            return [g for g in range(G) if g not in v_passes(r)]

        def freed(r, g):
            return [("turn", r - 4, g // 2)] if r >= 4 else []

        def put_widen_vector(r):
            for g in v_passes(r):
                put("vector", ("x", r, g), freed(r, g), widen_vector, r, g)

        def put_widen_scalar(r, reorders):
            again = s_passes(r)[::-1][:reorders][::-1]
            for g in again + [g for g in s_passes(r) if g not in again]:
                if g in again:
                    put("scalar", ("xs", r, g), [], widen_scalar, r, g, unordered[g])
                else:
                    put("scalar", ("x", r, g), freed(r, g), widen_scalar, r, g, slot(r, g))
            for g in again:
                put("scalar", ("x", r, g), freed(r, g), reorder, r, g)

        pair_of, bank_of = {}, {}

        def put_turn(r, b, bank):
            pair_of[r, b] = banks[bank]
            needs = claim(bank, ("collect", r, b)) + ([("x", r, g) for g in (2 * b, 2 * b + 1)] if r != MEANS else [])
            put("tensor", ("turn", r, b), needs, turn, r, b, pair_of[r, b])

        def put_collect(r, b):
            put("scalar", ("collect", r, b), [("turn", r, b)] + staged_in(r), collect, r, b, pair_of[r, b])

        def put_quantise(r):
            put("vector", ("qx", r), [("collect", r, 0), ("collect", r, 1)], quantise_x, r)

        def parts_of(unit):
            return [j for j, (c0, n) in enumerate(PARTS) if c0 < unit[1] + unit[2] and unit[1] < c0 + n]

        def centres_of(unit):
            return [("out", ((MEANS,),) + PARTS[j]) for j in parts_of(unit)]

        fused, issued = set(), {}

        def put_multiply(unit, passes, bank=None):
            rows, c0, n = unit
            if bank is not None:
                bank_of[unit] = banks[bank]
            for j, r in enumerate(rows):
                for g in passes:
                    who = MEANS if g >= G else r
                    needs = [("qx", who)] + [("qw", part, g % G) for part in parts_of(unit)]
                    if j == 0 and bank is not None and g == passes[0]:
                        needs = needs + claim(bank, ("out", unit))
                    issued[unit, r] = issued.get((unit, r), 0) + 1
                    total = 2 * G if unit in fused else G
                    put("tensor", ("mm", unit, r, issued[unit, r] - 1), needs, multiply, who, c0, n, g % G, bank_of[unit][:, n * j : n * j + n], issued[unit, r] == 1, issued[unit, r] == total)

        def put_centre(unit):
            put("scalar", ("out", unit), [("mm", unit, MEANS, G - 1)], copy_centre, unit, bank_of[unit])

        spare = [half for done in narrow_wide for half in halves(done)]
        lent, made_by, homes = set(), {}, {}

        def home(unit):
            rows, c0, n = unit
            r, h = rows[0], c0 // BANK
            if r < PAIRED:
                return halves(grouped[r // 2 * 2 + 1])[r % 2]
            if (r, h) not in homes:
                homes[r, h] = spare.pop(0) if h == 1 and r in lent else halves(grouped[r])[h]
            return homes[r, h][:, c0 % BANK : c0 % BANK + n]

        def put_subtract(unit):
            if unit in fused:
                result[unit] = home(unit)
                put("vector", ("out", unit), [("mm", unit, unit[0][-1], 2 * G - 1)], gain_fused, unit, bank_of[unit])
                put("sync", ("store", unit), [("out", unit)], store, unit)
                return
            if len(unit[0]) > 1:
                for j, r in enumerate(unit[0]):
                    diff[(r,), BANK, BANK] = halves(grouped[unit[0][0]])[j]
                    made_by[(r,), BANK, BANK] = ("out", unit)
            else:
                diff[unit] = home(unit)
            put("vector", ("out", unit), [("mm", unit, unit[0][-1], G - 1)] + centres_of(unit), subtract, unit, bank_of[unit])

        def put_gain_vector(unit):
            result[unit] = diff[unit]
            put("vector", ("gain", unit), [made_by.get(unit, ("out", unit)), "gain"], gain_vector, unit)
            put_store(unit)

        def put_gain_gpsimd(unit, behind=None):
            result[unit] = diff[unit]
            needs = [made_by.get(unit, ("out", unit))]
            if behind is not None:
                result[unit] = halves(grouped[behind])[1]
                needs = needs + [("qx", behind)]
            put("gpsimd", ("gain", unit), needs, gain_gpsimd, unit)

        def put_store(unit):
            put("sync", ("store", unit), [("gain", unit)], store, unit)

        def put_w(engine, h, g):
            if engine == "scalar":
                put("scalar", ("ww", h, g), [], widen_w, h, g)
            elif engine == "weave":
                put("vector", ("iw", h, g), [("ww", h, g), "ws"], weave_w, h, g)
            else:
                put("vector", ("qw", h, g), [("iw", h, g)], quantise_w, h, g)


        def half(r, h):
            return (r,), BANK * h, BANK

        def pair(r, part):
            return ((r, r + 1),) + PARTS[part]

        def middle(part):
            return ((MEANS,),) + PARTS[part]

        turn_ring, acc_ring = [0, 1, 2], [3, 4, 5, 6]

        def rotate(ring):
            ring.append(ring.pop(0))
            return ring[-1]

        def put_turns(*row_halves):
            for r, b in row_halves:
                put_turn(r, b, rotate(turn_ring))

        def put_units(*units):
            for unit in units:
                put_multiply(unit, range(G), rotate(acc_ring))

        def both(r):
            return [(r, 0), (r, 1)]

        fused.update(half(r, 0) for r in range(NEGATED))
        lent.update(RELEASES)
        late_halves = [(r, b) for r in range(RUNS_FROM, R) for b in range(2)]
        runs = [late_halves[j : j + 3] for j in range(0, len(late_halves), 3)]
        late_units = [half(r, h) for r in range(RUNS_FROM - 2, R - 1) for h in range(2)][1:]
        last_units = [((R - 1,), c0, QUARTER) for c0 in range(0, N, QUARTER)]

        put("tensor", "spread", claim(2, "picked"), spread_scales)
        put_turns(*both(0), *both(MEANS))
        put("tensor", "gain", [], spread_gain)
        put_multiply(half(0, 0), [0, 1, G, G + 1], rotate(acc_ring))
        put_multiply(middle(0), [0, 1], rotate(acc_ring))
        put_turns(*both(1))
        put_multiply(half(1, 0), [G, G + 1], rotate(acc_ring))
        put_multiply(half(0, 0), [2, G + 2])
        put_multiply(middle(0), [2])
        put_turns(*both(2))
        acc_ring.insert(0, turn_ring.pop(0))
        put_multiply(half(1, 0), [G + 2])
        put_multiply(half(0, 0), [3, G + 3])
        put_multiply(middle(0), [3])
        put_multiply(half(1, 0), [G + 3, 0, 1, 2, 3])
        put_turns(*both(3))
        put_units(middle(1), half(2, 0), pair(0, 1))
        put_turns(*both(4))
        put_units(half(3, 0), pair(2, 1), half(4, 0))
        put_turns(*both(5))
        put_units(middle(2), pair(0, 2), pair(2, 2))
        turn_ring.append(acc_ring.pop(0))
        for j, run in enumerate(runs[:-1]):
            put_turns(*run)
            put_units(*late_units[3 * j : 3 * j + 3])
        put_turns(*runs[-1])
        put_units(*late_units[-3:-1])
        acc_ring = turn_ring[:2][::-1] + acc_ring
        put_units(late_units[-1], *last_units)

        def put_collects(*row_halves):
            for r, b in row_halves:
                put_collect(r, b)

        def later_first(r):
            return both(r)[::-1]

        def put_w_jobs(kind, part, passes):
            for g in passes:
                put_w(kind, part, g)

        def put_x_scalar(*rows):
            for r in rows:
                put_widen_scalar(r, REORDERED[r])

        put_w_jobs("scalar", 0, [0, 1])
        put_collects(*later_first(0))
        put_w_jobs("scalar", 0, [2, 3])
        put_collects(*later_first(MEANS))
        put_x_scalar(1)
        put_w_jobs("scalar", 1, [0, 1])
        put_x_scalar(2)
        put_collects(*later_first(1))
        put_w_jobs("scalar", 1, [2, 3])
        put_collects(*later_first(2))
        put_x_scalar(3)
        put_w_jobs("scalar", 2, [0, 1])
        put_centre(middle(0))
        put_collects(*both(3))
        put_x_scalar(4)
        put_w_jobs("scalar", 2, [2, 3])
        put_collects(*later_first(4))
        put_centre(middle(1))
        put_x_scalar(5, 6)
        put_collects(*both(5))
        put_centre(middle(2))
        put_x_scalar(7)
        widened = 7
        for j, run in enumerate(runs):
            put_collects(*run)
            needed = runs[j + 1][-1][0] if j + 1 < len(runs) else widened
            put_x_scalar(*range(widened + 1, needed + 1))
            widened = needed

        def put_x_vector(*rows):
            for r in rows:
                put_widen_vector(r)

        put("vector", "minus", [], negate_scales)
        put("vector", "quadrant", [], mark_quadrants)
        put("vector", ("x", 0, 0), [], widen_vector, 0, 0)
        put("vector", ("x", 0, 1), [], widen_vector, 0, 1)
        put("vector", "picked", ["spread"], pick_scales)
        put("vector", ("x", 0, 2), [], widen_vector, 0, 2)
        put("vector", "ws", [], sum_scales)
        put("vector", ("x", 0, 3), [], widen_vector, 0, 3)
        put_w_jobs("weave", 0, [0, 1])
        put_w("q", 0, 0)
        put_quantise(0)
        put_w("weave", 0, 2)
        put_w("q", 0, 1)
        put_x_vector(1)
        put_quantise(MEANS)
        put_w("weave", 0, 3)
        put_w("q", 0, 2)
        put_x_vector(2)
        put_w("q", 0, 3)
        put_w_jobs("weave", 1, [0, 1])
        put_quantise(1)
        put_w_jobs("q", 1, [1, 0])
        put_w_jobs("weave", 1, [2, 3])
        put_x_vector(3)
        put_w_jobs("q", 1, [3, 2])
        put_quantise(2)
        put_w("weave", 2, 0)
        put_subtract(half(0, 0))
        put_w("weave", 2, 1)
        put_x_vector(4)
        put_quantise(3)
        put_w_jobs("q", 2, [1, 0])
        put_subtract(half(1, 0))
        put_w_jobs("weave", 2, [2, 3])
        put_quantise(4)
        put_x_vector(5)
        put_subtract(half(2, 0))
        put_w_jobs("q", 2, [3, 2])
        put_subtract(pair(0, 1))
        put_subtract(half(3, 0))
        put_x_vector(6)
        put_subtract(pair(2, 1))
        put_x_vector(7)
        put_subtract(half(4, 0))
        put_x_vector(8)

        full = [pair(0, 2), pair(2, 2)] + late_units + last_units
        waiting = [half(2, 0), half(3, 0), half(4, 0)]

        def stretch(release, subtractions, theirs, mine):
            given = []
            while subtractions or mine or theirs:
                ready = [unit for unit in waiting if unit[2] == BANK]
                while theirs and ready:
                    given.append(ready.pop(0))
                    waiting.remove(given[-1])
                    put_gain_gpsimd(given[-1], behind=release if len(given) == 1 else None)
                    theirs -= 1
                if subtractions:
                    unit = full.pop(0)
                    put_subtract(unit)
                    subtractions -= 1
                    fresh = [half(r, 1) for r in unit[0]] if len(unit[0]) > 1 else [unit]
                else:
                    fresh = []
                if mine and waiting and not theirs:
                    put_gain_vector(waiting.pop(0))
                    mine -= 1
                waiting.extend(fresh)
            for unit in given:
                put_store(unit)

        put_quantise(5)
        stretch(5, 4, 2, 2)
        for a in (6, 9):
            put_quantise(a)
            put_x_vector(a + 3, a + 4, a + 5)
            put_quantise(a + 1)
            put_quantise(a + 2)
            stretch(a + 2, 6, 4 if a == 6 else 4, 3 if a == 6 else 4)
        put_quantise(12)
        put_x_vector(15)
        put_gain_vector(waiting.pop(0))
        put_quantise(13)
        put_quantise(14)
        stretch(14, 4, 2, 2)
        put_quantise(15)
        put_gain_gpsimd(half(R - 3, 0), behind=R - 1)
        put_subtract(half(R - 3, 1))
        put_gain_gpsimd(half(R - 3, 1))
        put_subtract(half(R - 2, 0))
        put_store(half(R - 3, 0))
        put_gain_vector(half(R - 2, 0))
        put_subtract(half(R - 2, 1))
        put_gain_gpsimd(half(R - 2, 1))
        put_store(half(R - 3, 1))
        put_subtract(last_units[0])
        for j in range(1, len(last_units)):
            put_subtract(last_units[j])
            if j == len(last_units) - 1:
                put_store(half(R - 2, 1))
            put_gain_vector(last_units[j - 1])
        put_gain_vector(last_units[-1])


        done = set()
        while any(queues.values()):
            moved = False
            for steps in queues.values():
                while steps and all(need in done for need in steps[0][1]):
                    name, needs, call, args = steps.pop(0)
                    call(*args)
                    done.add(name)
                    moved = True
            assert moved, [steps[0][:2] for steps in queues.values() if steps]
